import numpy as np, ml_dtypes
CORES = [66,74,82,90,194,202,210,218]
N = 8
BF = ml_dtypes.bfloat16
def gentries(a):
    return np.ascontiguousarray(a.reshape(8, 16, -1).transpose(0, 2, 1)).reshape(8, -1)
def gtable(e):
    e = np.asarray(e); return np.ascontiguousarray(e.reshape(8, -1, 16).transpose(0, 2, 1)).reshape(128, -1).astype(np.int32)
XI, M, E, L, S, RO, D = 2048, 1024, 1024, 1024, 128, 3, 6
LB = 10
def forest(rng):
    o = np.argsort(rng.random((N, 8, M)), axis=-1); k = np.arange(M)
    inner = (2 * k + 2 < M) & (rng.random((N, 8, M)) >= 0.12); sw = rng.integers(0, 2, (N, 8, M))
    k0 = np.zeros_like(o); k1 = np.zeros_like(o)
    np.put_along_axis(k0, o, np.take_along_axis(o, np.where(inner, 2 * k + 1 + sw, k), 2), 2)
    np.put_along_axis(k1, o, np.take_along_axis(o, np.where(inner, 2 * k + 2 - sw, k), 2), 2)
    return o, k0, k1
def begin(rng, o, lo, hi):
    lv = rng.integers(lo, hi, (N, 8, L))
    return np.take_along_axis(o, 2 ** lv - 1 + (rng.random((N, 8, L)) * 2 ** lv).astype(np.int64), 2)
def vals(rng, n):
    return rng.integers(0, 256, (N, 8, 16, n))
def parts(rng):
    o, k0, k1 = forest(rng)
    return dict(o=o, x=vals(rng, XI), prev=rng.integers(0, XI, (N, 8, XI)), z=vals(rng, M), rs=vals(rng, M), kid0=k0, kid1=k1, env=vals(rng, E),
                start=begin(rng, o, LB - 3 - D, LB - 1), cur=rng.integers(0, XI, (N, 8, L)), w=rng.integers(1, 128, (N, 8, 16)), th=rng.integers(1000, 1500, (N, 8, 1)))
def pack(d):
    r = {}
    for k in ("x", "prev", "z", "rs", "kid0", "kid1", "env", "start", "cur", "w", "th"):
        if k in ("x", "z", "rs", "env"): r[k] = np.ascontiguousarray(d[k].reshape(N, 128, -1)).astype(np.float32).astype(BF)
        elif k in ("start", "cur"): r[k] = np.stack([gtable(a) for a in d[k]])
        elif k == "w": r[k] = d[k].reshape(N, 128, 1).astype(np.int32)
        else: r[k] = np.ascontiguousarray(d[k]).astype(np.int32)
    return r
def setup_inputs(rng):
    return pack(parts(rng))
def setup_inputs_full(rng):
    d = parts(rng)
    d["start"][:, ::2, :S] = d["o"][:, ::2, M // 2:M // 2 + S]; d["th"][:, ::2] = 0
    d["start"][::2, :, :S] = d["o"][::2, :, M // 2:M // 2 + S]; d["th"][::2] = 0
    return pack(d)
def setup_inputs_ties(rng):
    d = parts(rng)
    for k in ("x", "z", "rs", "env"): d[k] = d[k] // 64 * 64
    d["th"] = 64 * rng.integers(18, 22, (N, 8, 1))
    return pack(d)
def setup_inputs_alike(rng):
    d = parts(rng); m = np.arange(M)
    d["start"][:, 0] = d["o"][:, 0, M - 1:M]; d["th"][:, 0] = 0
    d["start"][:, 1] = rng.choice(np.array([0, M - 1]), (N, L)); d["cur"][:, 1] = rng.choice(np.array([0, XI - 1]), (N, L))
    d["prev"][:, 1] = np.where(rng.random((N, XI)) < 0.5, np.arange(XI), rng.choice(np.array([0, XI - 1]), (N, XI)))
    d["kid0"][:, 2] = (m + 1) & (M - 1); d["kid1"][:, 2] = (m + 1 + rng.integers(0, M - 1, (N, M))) & (M - 1)
    d["kid0"][:, 3] = m; d["kid1"][:, 3] = m
    d["start"][:, 3] = np.take_along_axis(rng.integers(0, M, (N, 40)), rng.integers(0, 40, (N, L)), 1)
    d["w"][:, 4] = 0; d["th"][:, 4] = 4096
    d["z"][:, 5] = 0; d["rs"][:, 5] = rng.choice(np.array([0, 255]), (N, 16, M))
    d["kid1"][:, 6] = d["kid0"][:, 6]; d["prev"][:, 6] = np.arange(XI)
    d["x"][:, 7] = 255; d["env"][:, 7] = 255; d["w"][:, 7] = 127; d["th"][:, 7] = 0
    return pack(d)
def setup_inputs_edges(rng):
    d = parts(rng); r = np.arange(N)[:, None]
    d["start"][:, :2, :S] = d["o"][:, :2, M // 2:M // 2 + S]; d["env"][:, :2] = 0
    c = rng.integers(0, 256, (16, 1)); d["x"][:, 0] = c
    d["rs"][:, 0] = np.where(rng.random((N, 1, M)) < 0.5, c, d["rs"][:, 0]); d["th"][:, 0] = r & 1
    c = 255 * rng.integers(0, 2, (16, 1)); d["x"][:, 1] = c
    d["rs"][:, 1] = 255 - c; d["rs"][:, 1, 0] = np.abs(255 - c[0] - rng.integers(0, 3, (N, M)))
    d["th"][:, 1] = np.array([4080, 4081, 4096, 4079])[r & 3]
    d["x"][:, 2:4] = rng.integers(250, 256, (N, 2, 16, XI)); d["w"][:, 2:4] = 127; d["env"][:, 3] = 0
    d["th"][:, 3] = rng.integers(2040, 2060, (N, 1))
    d["kid1"][:, 4] = np.where(rng.random((N, M)) < 0.5, d["kid0"][:, 4], d["kid1"][:, 4])
    return pack(d)
def setup_inputs_spread(rng):
    d = parts(rng); m = np.arange(M); lf = rng.random((N, 4, M)) < 0.5
    for k in ("kid0", "kid1"): d[k][:, 1::2] = np.where(lf, m, (m + rng.integers(1, M, (N, 4, M))) & (M - 1))
    for k, n in (("x", XI), ("z", M), ("rs", M), ("env", E)):
        d[k] = np.minimum((np.exp2(8 * rng.random((N, 8, 1, n))) * rng.random((N, 8, 16, n))).astype(np.int64), 255)
    d["w"] = np.minimum(np.exp2(7 * rng.random((N, 8, 16))).astype(np.int64), 127)
    d["th"] = np.minimum(np.exp2(12 * rng.random((N, 8, 1))).astype(np.int64), 4096); d["th"][:, 0] = 1; d["th"][:, 1] = 0
    d["start"] = begin(rng, d["o"], 0, LB)
    d["cur"] = np.minimum((XI * rng.random((N, 8, L)) ** 3).astype(np.int64), XI - 1)
    d["prev"] = np.where(rng.random((N, 8, XI)) < 0.5, np.maximum(np.arange(XI) - rng.integers(0, 40, (N, 8, XI)), 0), d["prev"])
    return pack(d)
def check_inputs(d):
    bad = []
    for k, lo, hi in (("x", 0, 255), ("prev", 0, XI - 1), ("z", 0, 255), ("rs", 0, 255), ("kid0", 0, M - 1), ("kid1", 0, M - 1), ("env", 0, 255), ("start", 0, M - 1), ("cur", 0, XI - 1), ("w", 0, 127), ("th", 0, 4096)):
        a = np.asarray(d[k]).astype(np.float32)
        if not np.all((a >= lo) & (a <= hi) & (a == np.floor(a))): bad.append("range of " + k)
    m = np.arange(M)
    if np.any((np.asarray(d["kid0"]) == m) != (np.asarray(d["kid1"]) == m)): bad.append("one kid of a node is the node itself, the other isn't")
    return bad
def pick(a, ix):
    return np.take_along_axis(a, ix[:, :, None, :], 3)
def reference(x, prev, z, rs, kid0, kid1, env, start, cur, w, th):
    def cols(a, more):
        b = a.astype(np.float32).astype(np.int32).reshape(N, 8, 16, -1)
        return np.concatenate([b, np.zeros((N, 8, 16, more), np.int32)], axis=3)
    X = cols(x, RO * L); Z = cols(z, 2 * S * RO); R = cols(rs, 2 * S * RO); EN = cols(env, 0)
    P = np.concatenate([prev.astype(np.int64), np.zeros((N, 8, RO * L), np.int64)], axis=2)
    own = np.zeros((N, 8, 1), np.int64) + np.arange(M, M + 2 * S * RO)
    K0 = np.concatenate([kid0.astype(np.int64), own], axis=2); K1 = np.concatenate([kid1.astype(np.int64), own], axis=2)
    F0 = np.stack([gentries(a) for a in start]).astype(np.int64); C = np.stack([gentries(a) for a in cur]).astype(np.int64)
    W = w.reshape(N, 8, 16, 1).astype(np.int32); TH = th.reshape(N, 8, 1).astype(np.int64)
    lower = np.arange(S)[None, :] < np.arange(S)[:, None]
    for t in range(RO):
        f = F0; s = C
        for step in range(D):
            k0 = np.take_along_axis(K0, f, 2); k1 = np.take_along_axis(K1, f, 2); go = k0 != f
            b = np.sum(pick(X, s) >= pick(Z, f), axis=2) >= 9
            f = np.where(go, np.where(b, k1, k0), f); s = np.where(go, np.take_along_axis(P, s, 2), s)
        xc = pick(X, C); rf = pick(R, f); a = np.sum(rf > xc, axis=2)
        y = pick(EN, (np.sum(W * xc, axis=2) + 97 * a) & (E - 1)); v = (xc + y) & 255
        fs = f[:, :, :S]; leaf = np.take_along_axis(K0, fs, 2) == fs
        first = ~np.any((fs[:, :, :, None] == fs[:, :, None, :]) & lower, axis=3)
        far = np.sum(np.abs(rf[..., :S] - v[..., :S]), axis=2) >= TH
        q, g, i = np.nonzero(leaf & first & far); at = fs[q, g, i]; n0 = M + 2 * S * t + 2 * i; xs = pick(X, s[:, :, :S])
        Z[q, g, :, at] = xs[q, g, :, i]; K0[q, g, at] = n0; K1[q, g, at] = n0 + 1
        R[q, g, :, n0] = rf[q, g, :, i]; R[q, g, :, n0 + 1] = (rf[q, g, :, i] + v[q, g, :, i]) >> 1
        came = np.roll(v, 1, axis=0)
        h = np.sum(W * came, axis=2) & (L - 1); lo = XI + L * t
        X[..., lo:lo + L] = came; P[..., lo:lo + L] = np.take_along_axis(C, h, 2)
        C = np.zeros((N, 8, 1), np.int64) + np.arange(lo, lo + L)
    return {"yk0": K0.astype(np.float32), "yk1": K1.astype(np.float32), "yr": np.ascontiguousarray(R[..., M:].reshape(N, 128, 2 * S * RO)).astype(np.float32).astype(BF), "yp": np.ascontiguousarray(P[..., XI:]).astype(np.float32)}

@@ -1,0 +1,545 @@
+from concourse.mybir import AluOpType, AxisListType, ActivationFunctionType
+import comms_topo
+
+A = AluOpType
+F = ActivationFunctionType
+TB = 1920
+XAW = 6272
+XV = 736
+KS = 832
+
+BUFS = {
+    "bfloat16": dict(XW=2048, PW=2048, ZW=TB, KW=TB, RW=2048, CT=1792, EM=1024, EP=1024, CP=3072, XA0=XAW, XA1=XAW, BT0=1024,
+                     BT1=1024, KG0=1024, KG1=1024, PG0=1024, PG1=1024, SP=1024, TT=1024, PB0=128, PB1=128, KBL=128, KBH=128,
+                     KBF=64, KG6=128, CG=128, BE=128, BO=128, EE=64, RN=256, DD=128, DA=128, XV6=128, V4=144, V97=144, VP=144,
+                     VKK=144, VK1=144, VW=144, EY=128, G0=240, SCE=128, SCO=128, KN=384, ZB=512, CBB=224),
+    "int32": dict(CURI=64, STI=64, PC=128, PCL=128, KC=128, KCL=128, OWN=64, OWN2=64, TM=64, TN=64, FI=64, SWI=64, HI=64, QI=64,
+                  QI2=64, OA=256, YI=64, YI2=64, S1=128, V1=128, H1=128, H2=128, IP=1, IQ=3, I14=14, CBI=154,
+                  WI=1, THB=8, KI=64, K0=64, K1=64, LF=48, L24=40),
+    "uint16": dict(IXP=192, IX=192, SL0=64, SL1=64, ST=64, FL0=64, FL1=64, XL=8, HL=64, OL=64, SCL=8, SCR=16),
+    "float32": dict(CURF=64, CURW=1024, YPC=1024, U=64, YF1=64, YF2=64, YK0=112, YK1=112, RJ=1024,
+                    FM=8, w8=96, col=64, IC=144, IG=240, ID=128, JN=128, J2=256, I8=8, T0=8, TL=8, T2=8, LN=8, DM=8, THM=8),
+}
+PSUM = ("pA", "pK", "pP", "pS", "pD0", "pD1", "pM", "pN")
+SCRATCH = {n: ("sbuf", [128, w], d) for d, b in BUFS.items() for n, w in b.items()}
+SCRATCH["THR"] = ("sbuf", [1, 8], "int32")
+SCRATCH["CD"] = ("dram", [16, 1792], "bfloat16")
+for _n in PSUM:
+    SCRATCH[_n] = ("psum", [128, 512], "float32")
+LOADS = ["l_cur", "l_start", "l_prev", "l_kid0", "l_kid1", "l_x", "l_z", "l_env", "l_w", "l_th", "l_rs"]
+TAGS = ("e", "c0", "c1", "c2", "i0a", "i0b", "i1a", "i1b", "i2a", "i2b")
+SEMAPHORES = ["c_v", "c_s", "c_t", "c_g", "d_p", "d_k", "d_cw", "d_c1", "d_c2", "o_yp0", "o_yp1", "o_yp2", "o_yr0", "o_yr1",
+              "o_yk0", "o_yk1"] + LOADS + [a + b for a in ("r_", "q_") for b in TAGS]
+
+
+def rank_program(g, core, T, topo):
+    rank = T.rank_of(core)
+    if rank is None:
+        return
+    nxt = T.cores[(rank + 1) % len(T.cores)]
+    prv = T.cores[(rank - 1) % len(T.cores)]
+    queues = {"v": g.vector, "s": g.scalar, "t": g.tensor, "y": g.sync, "g": g}
+    clock = {q: {} for q in queues}
+    total = {}
+    hist = {}
+
+    def wait(q, ev):
+        sem, val, snap = ev
+        c = clock[q]
+        if c.get(sem, 0) >= val:
+            return
+        queues[q].wait_ge(T.sem[sem], val)
+        for k, v in snap.items():
+            if c.get(k, 0) < v:
+                c[k] = v
+        c[sem] = val
+
+    def meets(r, s):
+        if r[1] >= s[2] or s[1] >= r[2]:
+            return False
+        return r[3] is None or s[3] is None or r[3] == s[3]
+
+    def spec(r):
+        if not isinstance(r, tuple):
+            r = (r,)
+        r = tuple(r) + (0, 1 << 20, None)[len(r) - 1:]
+        return (r[0], 0, 1 << 20, None) if r[0] in PSUM else r
+
+    def need(q, reads, writes):
+        own = "c_" + q
+        evs = []
+        for wr, regs in ((False, reads), (True, writes)):
+            for r in regs:
+                for s, kind, ev in hist.get(r[0], ()):
+                    if meets(r, s) and (ev[0] != own if kind == "p" else (wr or kind == "w")):
+                        evs.append(ev)
+        evs.sort(key=lambda e: -sum(e[2].values()))
+        for ev in evs:
+            wait(q, ev)
+
+    def note(ev, reads, writes):
+        for wr, regs in ((False, reads), (True, writes)):
+            for r in regs:
+                h = hist.setdefault(r[0], [])
+                p = r[0] in PSUM
+                if wr and not p:
+                    h[:] = [e for e in h if not (r[3] is None and r[1] <= e[0][1] and e[0][2] <= r[2])]
+                else:
+                    kd = "p" if p else "r"
+                    h[:] = [e for e in h if not (e[1] == kd and e[0] == r and e[2][0] == ev[0] and e[2][1] <= ev[1])]
+                h.append((r, "p" if p else ("w" if wr else "r"), ev))
+
+    def op(q, fn, reads, writes, sem=None, inc=1, group=None):
+        reads = [spec(r) for r in reads]
+        writes = [spec(r) for r in writes]
+        need(q, reads, writes)
+        ins = fn()
+        sem = sem or "c_" + q
+        ins.then_inc(T.sem[sem], inc)
+        total[sem] = total.get(sem, 0) + inc
+        note((sem, group or total[sem], dict(clock[q])), reads, writes)
+
+    def dma(q, sem, out, in_, reads, writes, n=1):
+        op(q, lambda: queues[q].dma_start(out, in_), reads, writes, sem=sem, inc=16, group=16 * n)
+
+    def ts(out, w, in0, r, s1, s2, op0, op1=None):
+        def fn():
+            if op1 is None:
+                return g.vector.tensor_scalar(out, in0, s1, None, op0)
+            return g.vector.tensor_scalar(out, in0, s1, s2, op0, op1)
+        op("v", fn, r, w)
+
+    def tt(out, w, in0, in1, r, o):
+        op("v", lambda: g.vector.tensor_tensor(out, in0, in1, o), r, w)
+
+    def cp(out, w, in_, r):
+        op("v", lambda: g.vector.tensor_copy(out, in_), r, w)
+
+    def fill(name, lo, hi, c):
+        op("v", lambda: g.vector.memset(T[name][:, lo:hi], c), [], [(name, lo, hi)])
+
+    def act(out, w, in_, r, func=F.Copy, **kw):
+        op("s", lambda: g.scalar.activation(out, in_, func, **kw), r, w)
+
+    def iota(name, pattern, base, cm, small):
+        if small:
+            op("g", lambda: g.iota(T[name][:], pattern, base, cm, allow_small_or_imprecise_dtypes=True), [], [name])
+        else:
+            op("g", lambda: g.iota(T[name][:], pattern, base, cm), [], [name])
+
+    def wrap(ps, lt, src, base, n, start=True, stop=True, contiguous=False):
+        m = n // 16
+
+        def fn():
+            r = None
+            for k in range(16):
+                if contiguous:
+                    rhs = T[src][:, base + k * m:base + (k + 1) * m]
+                else:
+                    rhs = T[src][:, base + k:base + n:16]
+                r = g.tensor.matmul(T[ps][:, 0:m], T[lt][:, 15 - k:143 - k], rhs, start and k == 0, stop and k == 15)
+            return r
+        op("t", fn, [lt, (src, base, base + n)], [ps])
+
+    def send(tag, dst, dlo, src, lo, hi):
+        need("g", [spec((src, lo, hi))], [])
+        rid, pid = topo.addr(nxt, core)
+        g.remote_dma(T[dst][:, dlo:dlo + hi - lo], T[src][:, lo:hi], T.sem["r_" + tag], T.sem["q_" + tag], pid, rid,
+                     topo.mask(core, nxt))
+        n = len(topo.engines(core, nxt))
+        total["q_" + tag] = n
+        note(("q_" + tag, n, dict(clock["g"])), [spec((src, lo, hi))], [])
+        m = len(topo.engines(prv, core))
+        total["r_" + tag] = m
+        note(("r_" + tag, m, {}), [], [spec((dst, dlo, dlo + hi - lo))])
+
+    def gx(q, dst, d0, src, s0, s1, lst, lo, hi):
+        if lo >= hi:
+            return
+        out, w = T[dst][:, d0 + lo:d0 + hi], [(dst, d0 + lo, d0 + hi)]
+        in_, r = T[src][:, s0:s1].indirect(T[lst][:, lo // 16:hi // 16]), [(src, s0, s1), (lst, lo // 16, hi // 16)]
+        if q == "v":
+            cp(out, w, in_, r)
+        else:
+            act(out, w, in_, r)
+
+    ncol = [0]
+
+    def col():
+        ncol[0] += 1
+        return T.col[:, ncol[0] - 1:ncol[0]], ("col", ncol[0] - 1, ncol[0])
+
+    def colop(a, s1, s2, op0, op1=None):
+        c, w = col()
+        ts(c, [w], a[0], [a[1]], s1, s2, op0, op1)
+        return c, w
+
+    def colsum(a, b, o=A.add):
+        c, w = col()
+        tt(c, [w], a[0], b[0], [a[1], b[1]], o)
+        return c, w
+
+    dma("y", "l_cur", T.CURI[:], T.cur[:, :], [], ["CURI"])
+    dma("s", "l_kid0", T.KC[:, 0:64], T.kid0[:, :], [], [("KC", 0, 64)])
+    dma("y", "l_prev", T.PC[:], T.prev[:, :], [], ["PC"])
+    dma("s", "l_kid1", T.KC[:, 64:128], T.kid1[:, :], [], [("KC", 64, 128)])
+    dma("s", "l_start", T.STI[:], T.start[:, :], [], ["STI"])
+    dma("y", "l_x", T.XW[:], T.x[:, :], [], ["XW"])
+
+    iota("IP", [[0, 1]], 0, 1, False)
+    iota("IC", [[1, 144]], -15, 0, True)
+    iota("OWN", [[1, 64]], 0, 64, False)
+    iota("I14", [[1, 14]], 0, 14, False)
+    iota("I8", [[1, 8]], 0, 0, True)
+    iota("T0", [[16, 8]], 1792, 0, True)
+    iota("J2", [[1, 256]], 0, 0, True)
+    iota("JN", [[-1, 128]], -1, 0, True)
+    iota("ID", [[1, 128]], 0, -1, True)
+    iota("IG", [[1, 240]], -112, 0, True)
+    iota("CURW", [[1, 1024]], 0, 0, True)
+
+    fill("ZB", 0, 512, 0.0)
+    for b, lo, hi in (("KW", 0, 512), ("KW", 512, 1024), ("KW", 1024, 1536), ("KW", 1536, TB), ("ZW", 1024, 1536),
+                      ("ZW", 1536, TB), ("RW", 1024, 1536), ("RW", 1536, 2048)):
+        act(T[b][:, lo:hi], [(b, lo, hi)], T.ZB[:, 0:hi - lo], ["ZB"])
+    fill("PW", 0, 2048, 0.0)
+    ip = (T.IP[:], ("IP", 0, 1))
+    for i, (n, o) in enumerate(((4, A.arith_shift_right), (15, A.bitwise_and), (31, A.bitwise_and))):
+        ts(T.IQ[:, i:i + 1], [("IQ", i, i + 1)], T.IP[:], ["IP"], n, None, o)
+    ts(T.OWN2[:], ["OWN2"], T.OWN[:], ["OWN"], 1023, None, A.bitwise_and)
+    iq = [(T.IQ[:, i:i + 1], ("IQ", i, i + 1)) for i in range(3)]
+    p4, p16 = colop(iq[0], 1.0, None, A.mult), colop(iq[0], 16.0, None, A.mult)
+    p15, p31 = colop(iq[1], 1.0, None, A.mult), colop(iq[2], 1.0, None, A.mult)
+
+    cp(T.SL0[:], ["SL0"], T.CURI[:], ["CURI"])
+    ts(T.PCL[:], ["PCL"], T.PC[:], ["PC"], 255, None, A.bitwise_and)
+    cp(T.PB0[:], ["PB0"], T.PCL[:], ["PCL"])
+    tt(T.PB1[:], ["PB1"], T.PC[:], T.PCL[:], ["PC", "PCL"], A.subtract)
+    dma("y", "d_p", T.PW[0:128:16, :], T.PB0[:], ["PB0"], [("PW", 0, 2048, 0)], 2)
+    dma("y", "d_p", T.PW[1:128:16, :], T.PB1[:], ["PB1"], [("PW", 0, 2048, 1)], 2)
+    ts(T.KCL[:], ["KCL"], T.KC[:], ["KC"], 255, None, A.bitwise_and)
+    tt(T.KBF[:], ["KBF"], T.KC[:, 0:64], T.OWN2[:], [("KC", 0, 64), "OWN2"], A.is_equal)
+    cp(T.KBL[:], ["KBL"], T.KCL[:], ["KCL"])
+    tt(T.KBH[:], ["KBH"], T.KC[:], T.KCL[:], ["KC", "KCL"], A.subtract)
+    for q, b, lo in ((15, "KBF", 0), (0, "KBL", 0), (2, "KBL", 64), (1, "KBH", 0), (3, "KBH", 64)):
+        dma("y", "d_k", T.KW[q:128:16, 0:1024], T[b][:, lo:lo + 64], [(b, lo, lo + 64)], [("KW", 0, 1024, q)], 5)
+    dma("y", "l_z", T.ZW[:, 0:1024], T.z[:, :], [], [("ZW", 0, 1024)])
+    dma("y", "l_w", T.WI[:], T.w[:, :], [], ["WI"])
+    dma("y", "l_th", T.THR[:], T.th[:, :], [], ["THR"])
+    dma("y", "l_env", T.EM[:], T.env[:, :], [], ["EM"])
+    dma("y", "l_rs", T.RW[:, 0:1024], T.rs[:, :], [], [("RW", 0, 1024)])
+
+    def vmat(name, s2, more=()):
+        ts(T[name][:], [name], T.IC[:], ["IC", p16[1]] + list(more), p16[0], s2, A.is_equal, A.mult)
+
+    wp, lt4 = colop(p15, 2.0, None, A.is_lt), colop(p15, 4.0, None, A.is_lt)
+    eq15 = colop(p15, 15.0, None, A.is_equal)
+    m15 = colop(eq15, 4194304.0, None, A.mult)
+    wk1 = colsum(lt4, wp, A.subtract)
+    ws = colsum(wp, m15)
+    wk2 = colop(wk1, 2048.0, None, A.mult)
+    cp(T.ST[:], ["ST"], T.STI[:], ["STI"])
+    vmat("VP", wp[0], [wp[1]])
+    vmat("V4", 4096.0)
+    wkk = colsum(ws, wk2)
+    vmat("VK1", wk1[0], [wk1[1]])
+    vmat("VKK", wkk[0], [wkk[1]])
+
+    def more_columns():
+        re, ro = colop(p31, 15.0, None, A.is_equal), colop(p31, 31.0, None, A.is_equal)
+        ce, c27 = colop(p31, 11.0, 64.0, A.is_lt, A.mult), colop(p31, 27.0, 64.0, A.is_lt, A.mult)
+        c16 = colop(p31, 16.0, 64.0, A.is_lt, A.mult)
+        rb = colop(ip, -703.0, None, A.add)
+        e0, e1 = colop(p15, 0.0, None, A.is_equal), colop(p15, 1.0, None, A.is_equal)
+        e2, e3 = colop(p15, 2.0, None, A.is_equal), colop(p15, 3.0, None, A.is_equal)
+        co, c13, c02 = colsum(c27, c16, A.subtract), colsum(e1, e3), colsum(e0, e2)
+        c02d = colop(c02, 2.0, None, A.mult)
+        his = [colop(c13, 1024.0 + 256 * t, None, A.mult) for t in range(3)]
+        return re, ro, ce, co, rb, c02, c02d, [colsum(h, e2) for h in his], [colsum(h, eq15) for h in his]
+
+    def scaled(out, w, in_, r, s, b):
+        act(out, [w], in_, [r, s[1], b[1]], F.Identity, scale=s[0], bias=b[0])
+
+    def tables():
+        scaled(T.SCE[:], "SCE", T.JN[:], "JN", re, ce)
+        scaled(T.SCO[:], "SCO", T.JN[:], "JN", ro, co)
+        for t in range(3):
+            lo, hi = 128 * t, 1024 + 256 * t
+            scaled(T.KN[:, lo:lo + 128], ("KN", lo, lo + 128), T.J2[:, 0:128], "J2", c02d, kbs[t])
+            scaled(T.KW[:, hi:hi + 256], ("KW", hi, hi + 256), T.J2[:], "J2", c02, kcs[t])
+
+    def hand_ahead():
+        wf = colop((T.WI[:], "WI"), 1.0, None, A.mult)
+        vmat("VW", wf[0], [wf[1]])
+        ts(T.EM[:], ["EM"], T.EM[:], ["EM"], -256.0, None, A.add)
+        send("c0", "CP", 0, "XA0", 0, 1024)
+        send("e", "EP", 0, "EM", 0, 1024)
+
+    def codes():
+        for b in range(11):
+            ts(T.CBI[:, 14 * b:14 * b + 14], [("CBI", 14 * b, 14 * b + 14)], T.I14[:], ["I14"], b, 1, A.arith_shift_right,
+               A.bitwise_and)
+        fill("CBB", 154, 210, 0.0)
+        fill("CBB", 210, 224, 1.0)
+        ts(T.CBB[:, 0:154], [("CBB", 0, 154)], T.CBI[:], ["CBI"], 2.0, -1.0, A.mult, A.add)
+        for q in range(16):
+            dma("y", "d_c1", T.CD[q, :], T.CBB[:, 14 * q:14 * q + 14], [("CBB", 14 * q, 14 * q + 14)], [("CD", 0, 1792, q)], 16)
+        for q in range(8):
+            dma("y", "d_c2", T.CT[16 * q:16 * q + 16, :], T.CD[:, :], ["CD"], [("CT", 0, 1792, q)], 8)
+        cp(T.CURF[:], ["CURF"], T.CURI[:], ["CURI"])
+        dma("y", "d_cw", T.CURW[0:128:16, :], T.CURF[:], ["CURF"], ["CURW"])
+
+    def thresholds():
+        vmat("V97", 97.0)
+        ts(T.DM[:], ["DM"], T.I8[:], ["I8", p4[1]], p4[0], None, A.is_equal)
+        op("g", lambda: g.partition_broadcast(T.THB[:], T.THR[:], 128), ["THR"], ["THB"])
+        ts(T.TL[:], ["TL"], T.T0[:], ["T0", p15[1]], p15[0], None, A.add)
+        ts(T.EY[:], ["EY"], T.ID[:], ["ID"], 0.0, None, A.is_equal)
+        ts(T.G0[:], ["G0"], T.IG[:], ["IG", p15[1]], p15[0], None, A.is_equal)
+        tt(T.THM[:], ["THM"], T.THB[:], T.DM[:], ["THB", "DM"], A.mult)
+        ts(T.T2[:], ["T2"], T.TL[:], ["TL"], 2.0, -1792.0, A.mult, A.add)
+        ts(T.LN[:], ["LN"], T.TL[:], ["TL"], 4352.0, None, A.add)
+        c, w = col()
+        op("v", lambda: g.vector.tensor_reduce(c, T.THM[:], AxisListType.X, A.add), ["THM"], [w])
+        return colop((c, w), 4096.0, None, A.mult)
+
+    def zcmp(t, k):
+        xa, lst, b = "XA%d" % (t % 2), "FL%d" % (k % 2) if k else "ST", "BT%d" % (k % 2)
+        lo, hi = 1024 * k, 1024 * k + 1024
+        tt(T[b][:], [b], T.ZW[:].indirect(T[lst][:]), T[xa][:, lo:hi], ["ZW", lst, (xa, lo, hi)], A.is_le)
+
+    def kgather(k, ks=1024):
+        for q, lo, hi in (("s", 0, ks), ("v", ks, 1024)):
+            gx(q, "KG%d" % (k % 2), 0, "KW", 0, TB, "FL%d" % (k % 2) if k else "ST", lo, hi)
+
+    def wraps(k):
+        wrap("pK", "VKK", "KG%d" % (k % 2), 0, 1024)
+        wrap("pA", "V4", "BT%d" % (k % 2), 0, 1024)
+
+    def select(k):
+        fl = "FL%d" % ((k + 1) % 2)
+        cp(T.KI[:], ["KI"], T.pK[:, 0:64], ["pK"])
+        ts(T.K0[:], ["K0"], T.KI[:], ["KI"], 2047, None, A.bitwise_and)
+        ts(T.K1[:], ["K1"], T.KI[:], ["KI"], 11, 2047, A.arith_shift_right, A.bitwise_and)
+        ts(T.U[:], ["U"], T.K0[:], ["K0"], 34816.0, None, A.add)
+        ts(T.LF[:, 8 * k:8 * k + 8], [("LF", 8 * k, 8 * k + 8)], T.KI[:, 0:8], ["KI"], 12, 1024, A.arith_shift_right, A.bitwise_and)
+        tt(T.TN[:], ["TN"], T.pA[:, 0:64], T.K1[:], ["pA", "K1"], A.add)
+        tt(T.TM[:], ["TM"], T.TN[:], T.U[:], ["TN", "U"], A.max)
+        ts(T.FI[:], ["FI"], T.TM[:], ["TM"], 2047, None, A.bitwise_and)
+        cp(T[fl][:], [fl], T.FI[:], ["FI"])
+
+    th = None
+    gx("v", "XA0", 0, "XW", 0, 2048, "SL0", 0, 1024)
+    for k in range(6):
+        sl, sn, pg = "SL%d" % (k % 2), "SL%d" % ((k + 1) % 2), "PG%d" % (k % 2)
+        n = 1024 if k < 5 else 128
+        gx("s", pg, 0, "PW", 0, 2048, sl, 0, n)
+        if k:
+            gx("s", "XA0", 1024 * k, "XW", 0, 2048, sl, XV, 1024)
+        if k == 5:
+            tables()
+        kgather(k)
+        zcmp(0, k)
+        if k == 0:
+            re, ro, ce, co, rb, c02, c02d, kbs, kcs = more_columns()
+        wrap("pP", "VP", pg, 0, n)
+        wraps(k)
+        cp(T[sn][:, 0:n // 16], [(sn, 0, n // 16)], T.pP[:, 0:n // 16], ["pP"])
+        if k < 5:
+            gx("v", "XA0", 1024 * k + 1024, "XW", 0, 2048, sn, 0, XV)
+        else:
+            gx("s", "XA0", 6144, "XW", 0, 2048, sn, 0, 128)
+            th = thresholds()
+        if k == 0:
+            hand_ahead()
+        if k == 1:
+            wrap("pS", "VW", "XA0", 0, 1024)
+            codes()
+        if k == 2:
+            cp(T.SWI[:], ["SWI"], T.pS[:, 0:64], ["pS"])
+        select(k)
+
+    def end_of_round(t):
+        xa, x0, fl = "XA%d" % (t % 2), 64 * t, "FL0"
+        gx("s", "CG", 0, "CT", 0, 1792, fl, 0, 128)
+        gx("s", "RN", 0, "RW", 0, 2048, fl, 0, 128)
+        gx("s", "KG6", 0, "KW", 0, TB, fl, 0, 128)
+        for h in range(2):
+            lo, hi = 512 * h, 512 * h + 512
+            tt(T.BT0[:, lo:hi], [("BT0", lo, hi)], T.RW[:].indirect(T[fl][:, lo // 16:hi // 16]), T[xa][:, lo:hi],
+               ["RW", (fl, lo // 16, hi // 16), (xa, lo, hi)], A.is_gt)
+            wrap("pS" if h else "pP", "V97", "BT0", lo, 512)
+
+        def column(h):
+            q0, q1, ps = 32 * h, 32 * h + 32, "pS" if h else "pP"
+            tt(T.QI[:, q0:q1], [("QI", q0, q1)], T[ps][:, 0:32], T.SWI[:, q0:q1], [ps, "SWI"], A.add)
+            ts(T.QI2[:, q0:q1], [("QI2", q0, q1)], T.QI[:, q0:q1], [("QI", q0, q1)], 1023, None, A.bitwise_and)
+            cp(T.IX[:, x0 + q0:x0 + q1], [("IX", x0 + q0, x0 + q1)], T.QI2[:, q0:q1], [("QI2", q0, q1)])
+            send("i%d" % t + "ab"[h], "IXP", x0 + q0, "IX", x0 + q0, x0 + q1)
+        column(0)
+        tt(T.BE[:], ["BE"], T.CG[:], T.SCE[:], ["CG", "SCE"], A.mult)
+        tt(T.BO[:], ["BO"], T.CG[:], T.SCO[:], ["CG", "SCO"], A.mult)
+        column(1)
+        banks = ("pD0", "pD1", "pK", "pN")
+
+        def dots(a):
+            def fn():
+                r = None
+                for i, b in enumerate((T.BE, T.BO)):
+                    r = g.tensor.matmul(T[banks[a]][:, 128 * i:128 * i + 128], T.CG[32 * a:32 * a + 32, :],
+                                        b[32 * a:32 * a + 32, :], True, True)
+                return r
+            op("t", fn, ["CG", "BE", "BO"], [banks[a]])
+        for a in range(4):
+            dots(a)
+        wrap("pA", "VKK", "KG6", 0, 128)
+        for q in range(8):
+            ps, i = banks[q // 2], 128 * (q % 2)
+
+            def relu(q=q, ps=ps, i=i):
+                return g.scalar.activation(T.RJ[:, 128 * q:128 * q + 128], T[ps][:, i:i + 128], F.Relu, bias=rb[0],
+                                           accum_out=T.FM[:, q:q + 1])
+            op("s", relu, [ps, rb[1]], [("RJ", 128 * q, 128 * q + 128), ("FM", q, q + 1)])
+        tt(T.S1[:], ["S1"], T.EM[:].indirect(T.IX[:, x0:x0 + 8]), T[xa][:, 0:128], ["EM", ("IX", x0, x0 + 8), (xa, 0, 128)], A.add)
+        ts(T.V1[:], ["V1"], T.S1[:], ["S1"], 255, None, A.bitwise_and)
+        tt(T.DD[:], ["DD"], T.RN[:, 0:128], T.V1[:], [("RN", 0, 128), "V1"], A.subtract)
+        act(T.DA[:], ["DA"], T.DD[:], ["DD"], F.Abs)
+        if t < 2:
+            l = [(T.L24[:, 8 * i:8 * i + 8], ("L24", 8 * i, 8 * i + 8)) for i in range(5)]
+            tt(T.L24[:, 0:24], [("L24", 0, 24)], T.LF[:, 0:24], T.LF[:, 24:48], ["LF"], A.add)
+            tt(l[3][0], [l[3][1]], l[0][0], l[1][0], [l[0][1], l[1][1]], A.add)
+            tt(l[4][0], [l[4][1]], T.LN[:], l[2][0], [l[2][1], "LN"], A.subtract)
+            tt(l[0][0], [l[0][1]], l[4][0], l[3][0], [l[3][1], l[4][1]], A.subtract)
+            cp(T.XL[:], ["XL"], l[0][0], [l[0][1]])
+            gx("s", "XV6", 0, xa, 0, XAW, "XL", 0, 128)
+        lf, ft, fi, fq, fa, sa, sb, ra, rd = [(T.w8[:, 8 * i:8 * i + 8], ("w8", 8 * i, 8 * i + 8)) for i in range(9)]
+        ts(lf[0], [lf[1]], T.pA[:, 0:8], ["pA"], 4194304.0, None, A.is_ge)
+        tt(ft[0], [ft[1]], T.FI[:, 0:8], T.TL[:], [("FI", 0, 8), "TL"], A.subtract)
+        for q in range(8):
+            ts(T.EE[:, 8 * q:8 * q + 8], [("EE", 8 * q, 8 * q + 8)], T.DM[:], ["DM", ("FM", q, q + 1)], T.FM[:, q:q + 1], None,
+               A.is_gt)
+
+        def conv():
+            r = None
+            for q in range(8):
+                r = g.tensor.matmul(T.pP[:, 0:8], T.G0[:, 112 - 16 * q:240 - 16 * q], T.EE[:, 8 * q:8 * q + 8], q == 0, q == 7)
+            return r
+        wrap("pM", "V4", "DA", 0, 128)
+        op("t", conv, ["G0", "EE"], ["pP"])
+
+        def split_lists():
+            ts(fa[0], [fa[1]], T.pM[:, 0:8], ["pM", th[1]], th[0], None, A.is_ge)
+            tt(fi[0], [fi[1]], T.pP[:, 0:8], lf[0], ["pP", lf[1]], A.mult)
+            tt(sa[0], [sa[1]], fi[0], fa[0], [fi[1], fa[1]], A.mult)
+            tt(fq[0], [fq[1]], sa[0], ft[0], [sa[1], ft[1]], A.mult)
+            tt(sb[0], [sb[1]], fq[0], T.TL[:], [fq[1], "TL"], A.add)
+            cp(T.SCL[:], ["SCL"], sb[0], [sb[1]])
+            lo, hi = 128 * t, 128 * t + 128
+            cp(T.KW[:].indirect(T.SCL[:]), ["KW"], T.KN[:, lo:hi], [("KN", lo, hi), "SCL"])
+
+        def split_z():
+            cp(T.ZW[:].indirect(T.SCL[:]), ["ZW"], T.XV6[:], ["XV6", "SCL"])
+
+        def new_r():
+            ts(ra[0], [ra[1]], sa[0], [sa[1]], 256.0 * t - 768.0, None, A.mult)
+            tt(T.H1[:], ["H1"], T.RN[:, 0:128], T.V1[:], [("RN", 0, 128), "V1"], A.add)
+            tt(rd[0], [rd[1]], ra[0], T.T2[:], [ra[1], "T2"], A.add)
+            ts(T.H2[:], ["H2"], T.H1[:], ["H1"], 1, None, A.arith_shift_right)
+            cp(T.SCR[:, 0:8], [("SCR", 0, 8)], rd[0], [rd[1]])
+            ts(T.SCR[:, 8:16], [("SCR", 8, 16)], rd[0], [rd[1]], 1.0, None, A.add)
+            cp(T.RN[:, 128:256], [("RN", 128, 256)], T.H2[:], ["H2"])
+
+        def split_r():
+            cp(T.RW[:].indirect(T.SCR[:]), ["RW"], T.RN[:], ["RN", "SCR"])
+            if t == 1:
+                dma("y", "o_yr0", T.yr[:, 0:512], T.RW[:, 1024:1536], [("RW", 1024, 1536)], [])
+            if t == 2:
+                dma("y", "o_yr1", T.yr[:, 512:768], T.RW[:, 1536:1792], [("RW", 1536, 1792)], [])
+        return split_lists, split_z, new_r, split_r
+
+    def arrive(t, h):
+        lo, hi, x0, c0 = 512 * h, 512 * h + 512, 64 * t, 1024 * t
+        tt(T.SP[:, lo:hi], [("SP", lo, hi)], T.EP[:].indirect(T.IXP[:, x0 + lo // 16:x0 + hi // 16]), T.CP[:, c0 + lo:c0 + hi],
+           ["EP", ("IXP", x0 + lo // 16, x0 + hi // 16), ("CP", c0, c0 + 1024)], A.add)
+        ts(T.TT[:, lo:hi], [("TT", lo, hi)], T.SP[:, lo:hi], [("SP", lo, hi)], 0.0, 256.0, A.is_lt, A.mult)
+
+    def preds():
+        wrap("pN", "VW", "SP", 0, 1024, True, False, True)
+        wrap("pN", "VW", "TT", 0, 1024, False, True, True)
+
+    def preds_out(t):
+        yf = "YF%d" % t
+        cp(T.YI[:], ["YI"], T.pN[:, 0:64], ["pN"])
+        ts(T.YI2[:], ["YI2"], T.YI[:], ["YI"], 1023, None, A.bitwise_and)
+        ts(T[yf][:], [yf], T.YI2[:], ["YI2"], 1024.0 + 1024 * t, None, A.add)
+        dma("y", "o_yp%d" % t, T.yp[:, 1024 * t:1024 * t + 1024], T[yf][:], [yf], [])
+
+    late = end_of_round(0)
+    for t in (1, 2):
+        xo, xa = "XA%d" % ((t - 1) % 2), "XA%d" % (t % 2)
+        for h in range(2):
+            lo, hi, pd = 512 * h, 512 * h + 512, "pD%d" % h
+            arrive(t - 1, h)
+
+            def vsum(pd=pd, lo=lo, hi=hi):
+                g.tensor.matmul(T[pd][:], T.EY[:], T.SP[:, lo:hi], True, False)
+                return g.tensor.matmul(T[pd][:], T.EY[:], T.TT[:, lo:hi], False, True)
+            op("t", vsum, ["EY", ("SP", lo, hi), ("TT", lo, hi)], [pd])
+            act(T[xa][:, lo:hi], [(xa, lo, hi)], T[pd][:], [pd])
+            if h == 0:
+                late[0]()
+                kgather(0)
+        late[1]()
+        wrap("pS", "VW", "SP", 0, 1024, True, False)
+        wrap("pS", "VW", "TT", 0, 1024, False, True)
+        send("c%d" % t, "CP", 1024 * t, xa, 0, 1024)
+        zcmp(t, 0)
+        cp(T.SWI[:], ["SWI"], T.pS[:, 0:64], ["pS"])
+        ts(T.HI[:], ["HI"], T.SWI[:], ["SWI"], 1023, None, A.bitwise_and)
+        cp(T.HL[:], ["HL"], T.HI[:], ["HI"])
+        for k in range(6):
+            if k:
+                kgather(k, KS)
+                zcmp(t, k)
+            wraps(k)
+            d0 = 1024 * k
+            if k < 5:
+                gx("s", xa, d0 + 1024, xo, d0, d0 + 1024, "HL", 0, 1024)
+            elif t < 2:
+                gx("s", xa, d0 + 1024, xo, d0, d0 + 1024, "HL", 0, 128)
+            if k == 1:
+                late[2]()
+            if k == 2:
+                late[3]()
+            if k == 3 and t == 2:
+                preds()
+            if k == 4 and t == 2:
+                preds_out(1)
+            if k == 3 and t == 1:
+                oa, ob, oc, od = [(T.OA[:, 64 * i:64 * i + 64], ("OA", 64 * i, 64 * i + 64)) for i in range(4)]
+                ts(oa[0], [oa[1]], T.HI[:], ["HI"], 15, None, A.bitwise_and)
+                ts(ob[0], [ob[1]], T.HI[:], ["HI"], 4, None, A.arith_shift_right)
+                ts(oc[0], [oc[1]], oa[0], [oa[1]], 64.0, None, A.mult)
+                tt(od[0], [od[1]], oc[0], ob[0], [oc[1], ob[1]], A.add)
+                cp(T.OL[:], ["OL"], od[0], [od[1]])
+            select(k)
+        late = end_of_round(t)
+        if t == 1:
+            gx("s", "YPC", 0, "CURW", 0, 1024, "OL", 0, 1024)
+            dma("y", "o_yp0", T.yp[:, 0:1024], T.YPC[0:128:16, :], ["YPC"], [])
+
+    arrive(2, 0)
+    late[0]()
+    wrap("pK", "VP", "KW", 0, 1792, contiguous=True)
+    wrap("pA", "VK1", "KW", 0, 1792, contiguous=True)
+    act(T.YK0[:], ["YK0"], T.pK[:, 0:112], ["pK"])
+    act(T.YK1[:], ["YK1"], T.pA[:, 0:112], ["pA"])
+    dma("y", "o_yk0", T.yk0[:, :], T.YK0[:], ["YK0"], [])
+    dma("y", "o_yk1", T.yk1[:, :], T.YK1[:], ["YK1"], [])
+    arrive(2, 1)
+    preds()
+    late[2]()
+    late[3]()
+    preds_out(2)
+    for sem in sorted(total):
+        wait("g", (sem, total[sem], {}))

@@ -1,35 +1,44 @@
 from concourse.mybir import AluOpType, AxisListType, ActivationFunctionType
-import comms_topo
 
 A = AluOpType
 F = ActivationFunctionType
+DUP = 2048
 TB = 1920
 XAW = 6272
-XV = 736
-KS = 832
+EW = 2592
+SLOPE = 3968.0
+XV = (320, 192)
+XV0 = [256, 256, 128, 128, 128, 128, 192, 192, 256, 256]
+CYCLE, GATHER, GATHER2, SCATTER, WAKE, AHEAD = 0.87e-3, 1.56, 1.8, 3.8, 0.06, 0.15
+LOCAL, REMOTE = (1.7, 220e3, 0.15), (2.0, 45e3, 0.3)
+ROUND = 14
+PRE = False
+ENVA = 12.78
 
 BUFS = {
-    "bfloat16": dict(XW=2048, PW=2048, ZW=TB, KW=TB, RW=2048, CT=1792, EM=1024, EP=1024, CP=3072, XA0=XAW, XA1=XAW, BT0=1024,
-                     BT1=1024, KG0=1024, KG1=1024, PG0=1024, PG1=1024, SP=1024, TT=1024, PB0=128, PB1=128, KBL=128, KBH=128,
-                     KBF=64, KG6=128, CG=128, BE=128, BO=128, EE=64, RN=256, DD=128, DA=128, XV6=128, V4=144, V97=144, VP=144,
-                     VKK=144, VK1=144, VW=144, EY=128, G0=240, SCE=128, SCO=128, KN=384, ZB=512, CBB=224),
-    "int32": dict(CURI=64, STI=64, PC=128, PCL=128, KC=128, KCL=128, OWN=64, OWN2=64, TM=64, TN=64, FI=64, SWI=64, HI=64, QI=64,
-                  QI2=64, OA=256, YI=64, YI2=64, S1=128, V1=128, H1=128, H2=128, IP=1, IQ=3, I14=14, CBI=154,
-                  WI=1, THB=8, KI=64, K0=64, K1=64, LF=48, L24=40),
-    "uint16": dict(IXP=192, IX=192, SL0=64, SL1=64, ST=64, FL0=64, FL1=64, XL=8, HL=64, OL=64, SCL=8, SCR=16),
-    "float32": dict(CURF=64, CURW=1024, YPC=1024, U=64, YF1=64, YF2=64, YK0=112, YK1=112, RJ=1024,
-                    FM=8, w8=96, col=64, IC=144, IG=240, ID=128, JN=128, J2=256, I8=8, T0=8, TL=8, T2=8, LN=8, DM=8, THM=8),
+    "bfloat16": dict(XW=2048, PW=2048, ZW=DUP + TB, RW=DUP + 1792, CT=DUP + 1792, EM=EW, EP=EW, CP=3072, XA0=XAW, XA1=XAW, BT=1024,
+                     KG=1024, PG=1024, SP=1024, TT=1024, ZB=1024, EE=1024, PB=256, KG6=128, BE=128, BO=128, RN=128, DA=128,
+                     XV6=128, S1=128, T1=128, T5=128, SA=128, SM=128, GS=128, WL=128, WQ=256, NEG=16, ID=128, IDM=128, NL=128,
+                     LM=128, R3=8, WC=8, WA=40, WP=40, WW=40, WK=384, VP=144, VW=144, ON=128, JN=256),
+    "float16": dict(IDN=128, R3H=8, T3=128),
+    "int32": dict(CURI=64, STI=64, PC=256, PCL=256, KC=256, KCL=256, OWN=256, IP=1, IQ=3, WI=1, THP=1, THL=1, HI=64, HJ=64,
+                  H2=128, OA=128, YI=128),
+    "uint16": dict(IXP=192, IX=192, SL=448, ST=64, FL=64, XL=8, HL=64, OL=64, SCL=8),
+    "float32": dict(KW=DUP + TB, KB=256, KF=256, KN=384, D0=64, S2=128, MD=128, MB=128, SJ=16, col=40, I16=128, IG=128, IC=144,
+                    IDI=128, J2=256, N0=4, BN=4, BK=4, PF=1, RB=1, CURF=64, CURW=1024, YPC=1024, OB=128, YF1=64, YF2=64),
 }
-PSUM = ("pA", "pK", "pP", "pS", "pD0", "pD1", "pM", "pN")
+PSUM = ("pA", "pB", "pL", "pM", "pD0", "pD1", "pD2", "pD3")
 SCRATCH = {n: ("sbuf", [128, w], d) for d, b in BUFS.items() for n, w in b.items()}
-SCRATCH["THR"] = ("sbuf", [1, 8], "int32")
-SCRATCH["CD"] = ("dram", [16, 1792], "bfloat16")
+for _n in ("HS", "HH", "HX"):
+    SCRATCH[_n] = ("sbuf", [128, 70, 4], "float16")
 for _n in PSUM:
     SCRATCH[_n] = ("psum", [128, 512], "float32")
-LOADS = ["l_cur", "l_start", "l_prev", "l_kid0", "l_kid1", "l_x", "l_z", "l_env", "l_w", "l_th", "l_rs"]
+LOADS = ["l_cur", "l_start", "l_prev", "l_kid", "l_x", "l_z", "l_z2", "l_env", "l_w", "l_th", "l_rs"]
 TAGS = ("e", "c0", "c1", "c2", "i0a", "i0b", "i1a", "i1b", "i2a", "i2b")
-SEMAPHORES = ["c_v", "c_s", "c_t", "c_g", "d_p", "d_k", "d_cw", "d_c1", "d_c2", "o_yp0", "o_yp1", "o_yp2", "o_yr0", "o_yr1",
-              "o_yk0", "o_yk1"] + LOADS + [a + b for a in ("r_", "q_") for b in TAGS]
+SEMAPHORES = ["c_v", "c_s", "c_t", "c_g", "d_p", "d_k", "d_k2", "d_cw", "d_ct", "d_m1", "d_m2", "d_e1", "d_e2", "o_yp0", "o_yp1",
+              "o_yp2", "o_yr0", "o_yr1", "o_yk0", "o_yk1"] + LOADS + [a + b for a in ("r_", "q_") for b in TAGS]
+KIB = dict(l_prev=64, l_x=512, l_z=256, l_z2=256, l_env=256, l_rs=256, d_ct=448, d_m1=256, d_e1=256, d_m2=136, d_e2=136, l_w=1, l_th=1)
+ORDER = []
 
 
 def rank_program(g, core, T, topo):
@@ -39,20 +48,13 @@ def rank_program(g, core, T, topo):
     nxt = T.cores[(rank + 1) % len(T.cores)]
     prv = T.cores[(rank - 1) % len(T.cores)]
     queues = {"v": g.vector, "s": g.scalar, "t": g.tensor, "y": g.sync, "g": g}
-    clock = {q: {} for q in queues}
-    total = {}
-    hist = {}
 
-    def wait(q, ev):
-        sem, val, snap = ev
-        c = clock[q]
-        if c.get(sem, 0) >= val:
-            return
-        queues[q].wait_ge(T.sem[sem], val)
-        for k, v in snap.items():
-            if c.get(k, 0) < v:
-                c[k] = v
-        c[sem] = val
+    calls = []
+    seen = {}
+    now = [-100.0]
+
+    def at(turn):
+        now[0] = turn
 
     def meets(r, s):
         if r[1] >= s[2] or s[1] >= r[2]:
@@ -62,484 +64,607 @@ def rank_program(g, core, T, topo):
     def spec(r):
         if not isinstance(r, tuple):
             r = (r,)
-        r = tuple(r) + (0, 1 << 20, None)[len(r) - 1:]
-        return (r[0], 0, 1 << 20, None) if r[0] in PSUM else r
+        return tuple(r) + (0, 1 << 20, None)[len(r) - 1:]
 
-    def need(q, reads, writes):
-        own = "c_" + q
-        evs = []
+    def op(q, fn, reads, writes, cost, sem=None, group=None, move=None):
+        reads, writes = [spec(r) for r in reads], [spec(r) for r in writes]
+        me, deps = len(calls), set()
         for wr, regs in ((False, reads), (True, writes)):
             for r in regs:
-                for s, kind, ev in hist.get(r[0], ()):
-                    if meets(r, s) and (ev[0] != own if kind == "p" else (wr or kind == "w")):
-                        evs.append(ev)
-        evs.sort(key=lambda e: -sum(e[2].values()))
-        for ev in evs:
-            wait(q, ev)
-
-    def note(ev, reads, writes):
+                for s, w, i in seen.get(r[0], ()):
+                    if (meets(r, s) and (wr or w)) or (r[0] in PSUM and q == "t" and calls[i]["q"] == "t"):
+                        deps.add(i)
         for wr, regs in ((False, reads), (True, writes)):
             for r in regs:
-                h = hist.setdefault(r[0], [])
-                p = r[0] in PSUM
-                if wr and not p:
-                    h[:] = [e for e in h if not (r[3] is None and r[1] <= e[0][1] and e[0][2] <= r[2])]
-                else:
-                    kd = "p" if p else "r"
-                    h[:] = [e for e in h if not (e[1] == kd and e[0] == r and e[2][0] == ev[0] and e[2][1] <= ev[1])]
-                h.append((r, "p" if p else ("w" if wr else "r"), ev))
-
-    def op(q, fn, reads, writes, sem=None, inc=1, group=None):
-        reads = [spec(r) for r in reads]
-        writes = [spec(r) for r in writes]
-        need(q, reads, writes)
-        ins = fn()
-        sem = sem or "c_" + q
-        ins.then_inc(T.sem[sem], inc)
-        total[sem] = total.get(sem, 0) + inc
-        note((sem, group or total[sem], dict(clock[q])), reads, writes)
+                h = seen.setdefault(r[0], [])
+                if wr:
+                    h[:] = [x for x in h if not (r[3] is None and r[1] <= x[0][1] and x[0][2] <= r[2])]
+                h.append((r, wr, me))
+        calls.append(dict(q=q, fn=fn, reads=reads, writes=writes, sem=sem, group=group, deps=deps, turn=now[0], cost=cost,
+                          move=move, banks={r[0] for r in reads + writes if r[0] in PSUM}))
 
     def dma(q, sem, out, in_, reads, writes, n=1):
-        op(q, lambda: queues[q].dma_start(out, in_), reads, writes, sem=sem, inc=16, group=16 * n)
-
-    def ts(out, w, in0, r, s1, s2, op0, op1=None):
-        def fn():
-            if op1 is None:
-                return g.vector.tensor_scalar(out, in0, s1, None, op0)
-            return g.vector.tensor_scalar(out, in0, s1, s2, op0, op1)
-        op("v", fn, r, w)
-
-    def tt(out, w, in0, in1, r, o):
-        op("v", lambda: g.vector.tensor_tensor(out, in0, in1, o), r, w)
-
-    def cp(out, w, in_, r):
-        op("v", lambda: g.vector.tensor_copy(out, in_), r, w)
-
-    def fill(name, lo, hi, c):
-        op("v", lambda: g.vector.memset(T[name][:, lo:hi], c), [], [(name, lo, hi)])
-
-    def act(out, w, in_, r, func=F.Copy, **kw):
-        op("s", lambda: g.scalar.activation(out, in_, func, **kw), r, w)
-
-    def iota(name, pattern, base, cm, small):
-        if small:
-            op("g", lambda: g.iota(T[name][:], pattern, base, cm, allow_small_or_imprecise_dtypes=True), [], [name])
-        else:
-            op("g", lambda: g.iota(T[name][:], pattern, base, cm), [], [name])
-
-    def wrap(ps, lt, src, base, n, start=True, stop=True, contiguous=False):
-        m = n // 16
-
-        def fn():
-            r = None
-            for k in range(16):
-                if contiguous:
-                    rhs = T[src][:, base + k * m:base + (k + 1) * m]
-                else:
-                    rhs = T[src][:, base + k:base + n:16]
-                r = g.tensor.matmul(T[ps][:, 0:m], T[lt][:, 15 - k:143 - k], rhs, start and k == 0, stop and k == 15)
-            return r
-        op("t", fn, [lt, (src, base, base + n)], [ps])
+        op(q, lambda: queues[q].dma_start(out, in_), reads, writes, 0.05, sem, 16 * n, (LOCAL, KIB.get(sem, 32) << 10))
 
     def send(tag, dst, dlo, src, lo, hi):
-        need("g", [spec((src, lo, hi))], [])
-        rid, pid = topo.addr(nxt, core)
-        g.remote_dma(T[dst][:, dlo:dlo + hi - lo], T[src][:, lo:hi], T.sem["r_" + tag], T.sem["q_" + tag], pid, rid,
-                     topo.mask(core, nxt))
-        n = len(topo.engines(core, nxt))
-        total["q_" + tag] = n
-        note(("q_" + tag, n, dict(clock["g"])), [spec((src, lo, hi))], [])
-        m = len(topo.engines(prv, core))
-        total["r_" + tag] = m
-        note(("r_" + tag, m, {}), [], [spec((dst, dlo, dlo + hi - lo))])
+        def fn():
+            rid, pid = topo.addr(nxt, core)
+            g.remote_dma(T[dst][:, dlo:dlo + hi - lo], T[src][:, lo:hi], T.sem["r_" + tag], T.sem["q_" + tag], pid, rid,
+                         topo.mask(core, nxt))
+        op("g", fn, [(src, lo, hi)], [(dst, dlo, dlo + hi - lo)], 0.3, tag, None, (REMOTE, 256 * (hi - lo)))
 
-    def gx(q, dst, d0, src, s0, s1, lst, lo, hi):
-        if lo >= hi:
-            return
-        out, w = T[dst][:, d0 + lo:d0 + hi], [(dst, d0 + lo, d0 + hi)]
-        in_, r = T[src][:, s0:s1].indirect(T[lst][:, lo // 16:hi // 16]), [(src, s0, s1), (lst, lo // 16, hi // 16)]
-        if q == "v":
-            cp(out, w, in_, r)
-        else:
-            act(out, w, in_, r)
+    def ordered():
+        n = len(calls)
+        for c in calls:
+            for d in list(c["deps"]):
+                if calls[d]["group"] and calls[d]["sem"] != c["sem"]:
+                    c["deps"] |= {i for i in range(n) if calls[i]["sem"] == calls[d]["sem"]}
+        users = [[] for c in calls]
+        for i, c in enumerate(calls):
+            for d in c["deps"]:
+                users[d].append(i)
+        left, ready_at = [len(c["deps"]) for c in calls], [0.0] * n
+        free = {q: 0.0 for q in list(queues) + list(PSUM) + [LOCAL, REMOTE]}
+        ready = {q: [i for i in range(n) if not left[i] and calls[i]["q"] == q] for q in queues}
+        line = sorted((i for i in range(n) if calls[i]["q"] == "y"), key=lambda i: (-calls[i]["turn"], -i))
+        out, last = [], {}
+        while len(out) < n:
+            can = {q: [i for i in ready[q] if q != "y" or i == line[-1]] for q in queues}
+            t, q = min((max(free[e], min(ready_at[i] for i in can[e])), e) for e in queues if can[e])
+            i = min((j for j in can[q] if ready_at[j] <= t + AHEAD), key=lambda j: (calls[j]["turn"], j))
+            c = calls[i]
+            t = max([free[q], ready_at[i]] + [free[b] + (WAKE if last.get(b, q) != q else 0) for b in c["banks"]])
+            end = t + c["cost"]
+            for b in [q] + list(c["banks"]):
+                free[b], last[b] = end, q
+            if c["move"]:
+                way, nbytes = c["move"]
+                free[way] = max(free[way], t + way[0] / 2) + nbytes / way[1] + way[2]
+                end = free[way] + way[0] / 2
+            ready[q].remove(i)
+            if q == "y":
+                line.pop()
+            out.append((t, i))
+            for u in users[i]:
+                ready_at[u] = max(ready_at[u], end + WAKE + (0.03 if q == "t" else 0))
+                left[u] -= 1
+                if not left[u]:
+                    ready[calls[u]["q"]].append(u)
+        return [i for t, i in sorted(out)]
+
+    def issue():
+        clock = {q: {} for q in queues}
+        total, hist = {}, {}
+
+        def wait(q, ev):
+            sem, val, snap = ev
+            c = clock[q]
+            if c.get(sem, 0) >= val:
+                return
+            queues[q].wait_ge(T.sem[sem], val)
+            for k, v in snap.items():
+                if c.get(k, 0) < v:
+                    c[k] = v
+            c[sem] = val
+
+        def whole(regs):
+            return [spec(r[0]) if r[0] in PSUM else r for r in regs]
+
+        def note(ev, reads, writes):
+            for wr, regs in ((False, reads), (True, writes)):
+                for r in regs:
+                    h = hist.setdefault(r[0], [])
+                    p = r[0] in PSUM
+                    if wr and not p:
+                        h[:] = [x for x in h if not (r[3] is None and r[1] <= x[0][1] and x[0][2] <= r[2])]
+                    else:
+                        kd = "p" if p else "r"
+                        h[:] = [x for x in h if not (x[1] == kd and x[0] == r and x[2][0] == ev[0] and x[2][1] <= ev[1])]
+                    h.append((r, "p" if p else ("w" if wr else "r"), ev))
+
+        if not ORDER:
+            ORDER.extend(ordered())
+        for i in ORDER:
+            c = calls[i]
+            q, reads, writes, evs = c["q"], whole(c["reads"]), whole(c["writes"]), []
+            for wr, regs in ((False, reads), (True, writes)):
+                for r in regs:
+                    for s, kind, ev in hist.get(r[0], ()):
+                        if meets(r, s) and (ev[0] != "c_" + q if kind == "p" else (wr or kind == "w")) and ev[0] != c["sem"]:
+                            evs.append(ev)
+            evs.sort(key=lambda x: -sum(x[2].values()))
+            for ev in evs:
+                wait(q, ev)
+            ins = c["fn"]()
+            if c["sem"] in TAGS:
+                a, b = "q_" + c["sem"], "r_" + c["sem"]
+                total[a], total[b] = len(topo.engines(core, nxt)), len(topo.engines(prv, core))
+                note((a, total[a], dict(clock[q])), reads, [])
+                note((b, total[b], {}), [], writes)
+                continue
+            sem, inc = c["sem"] or "c_" + q, 16 if c["sem"] else 1
+            ins.then_inc(T.sem[sem], inc)
+            total[sem] = total.get(sem, 0) + inc
+            note((sem, c["group"] or total[sem], dict(clock[q])), reads, writes)
+        for sem in sorted(total):
+            wait("g", (sem, total[sem], {}))
+
+    def S(name, lo=0, hi=None, step=1):
+        hi = T[name].shape[1] if hi is None else hi
+        kind = "p" if name in PSUM else 4 if SCRATCH[name][2].endswith("32") else 2
+        return (T[name][:, lo:hi:step] if step > 1 else T[name][:, lo:hi]), [(name, lo, hi)], (hi - lo + step - 1) // step, kind
+
+    def G(name, lo, hi, lst, l0, l1):
+        return T[name][:, lo:hi].indirect(T[lst][:, l0 // 16:l1 // 16]), [(name, lo, hi), (lst, l0 // 16, l1 // 16)], l1 - l0, "g"
+
+    def cycles(n, more=0.02):
+        return more + max(64, n) * CYCLE
+
+    def plain(out, in_):
+        return cycles(in_[2] * GATHER, 0.05) if in_[3] == "g" else cycles(out[2] * (0.5 if out[3] == in_[3] == 2 else 1))
+
+    def num(a):
+        return a if isinstance(a, tuple) else (a, [])
+
+    def ts(out, in0, s1, op0, s2=None, op1=None):
+        s1, s2 = num(s1), num(s2)
+
+        def fn():
+            if op1 is None:
+                return g.vector.tensor_scalar(out[0], in0[0], s1[0], None, op0)
+            return g.vector.tensor_scalar(out[0], in0[0], s1[0], s2[0], op0, op1)
+        op("v", fn, in0[1] + s1[1] + s2[1], out[1], plain(out, in0))
+
+    def tt(out, in0, in1, o):
+        c = cycles(out[2] * GATHER2, 0.05) if in0[3] == "g" else cycles(out[2] * (1 if "p" in (in0[3], in1[3]) else 2))
+        op("v", lambda: g.vector.tensor_tensor(out[0], in0[0], in1[0], o), in0[1] + in1[1], out[1], c)
+
+    def cp(out, in_):
+        op("v", lambda: g.vector.tensor_copy(out[0], in_[0]), in_[1], out[1], plain(out, in_))
+
+    def scatter(name, lo, src):
+        op("v", lambda: g.vector.tensor_copy(T[name][:, lo:lo + TB].indirect(T.SCL[:]), src[0]), src[1] + ["SCL"],
+           [(name, lo, lo + TB)], cycles(128 * SCATTER, 0.05))
+
+    def fill(out, c):
+        op("v", lambda: g.vector.memset(out[0], c), [], out[1], plain(out, out))
+
+    def act(out, in_, func=F.Copy, scale=None, bias=None):
+        kw = {k: v[0] for k, v in (("scale", scale), ("bias", bias)) if v}
+        op("s", lambda: g.scalar.activation(out[0], in_[0], func, **kw), in_[1] + num(scale)[1] + num(bias)[1], out[1],
+           cycles(out[2] * (GATHER if in_[3] == "g" else 1), 0.08))
+
+    def iota(out, pattern, base=0, cm=0):
+        kw = {} if out[1][0][0] in BUFS["int32"] else dict(allow_small_or_imprecise_dtypes=True)
+        op("g", lambda: g.iota(out[0], pattern, base, cm, **kw), [], out[1], 0.13 + 2 * out[2] * CYCLE)
+
+    def mms(parts, start=True, stop=True):
+        def fn():
+            r = None
+            for i, (o, l, m) in enumerate(parts):
+                r = g.tensor.matmul(o[0], l[0], m[0], start and i == 0, stop and i == len(parts) - 1)
+            return r
+        op("t", fn, [r for o, l, m in parts for r in l[1] + m[1]], [r for o, l, m in parts for r in o[1]],
+           sum(cycles(o[2], 0) for o, l, m in parts))
+
+    def gx(q, dst, d0, src, s0, s1, lst, l0, lo, hi):
+        if lo < hi:
+            (cp if q == "v" else act)(S(dst, d0 + lo, d0 + hi), G(src, s0, s1, lst, l0 + lo, l0 + hi))
 
     ncol = [0]
 
-    def col():
-        ncol[0] += 1
-        return T.col[:, ncol[0] - 1:ncol[0]], ("col", ncol[0] - 1, ncol[0])
+    def col(n=1):
+        ncol[0] += n
+        return S("col", ncol[0] - n, ncol[0])
 
-    def colop(a, s1, s2, op0, op1=None):
-        c, w = col()
-        ts(c, [w], a[0], [a[1]], s1, s2, op0, op1)
-        return c, w
+    def colop(a, s1, op0, s2=None, op1=None):
+        c = col()
+        ts(c, a, s1, op0, s2, op1)
+        return c
 
-    def colsum(a, b, o=A.add):
-        c, w = col()
-        tt(c, [w], a[0], b[0], [a[1], b[1]], o)
-        return c, w
+    def colsum(in_):
+        c = col()
+        op("v", lambda: g.vector.tensor_reduce(c[0], in_[0], AxisListType.X, A.add), in_[1], c[1], cycles(64))
+        return c
 
+    def rows(name, r, lo, hi):
+        return T[name][r:128:16, lo:hi], [(name, lo, hi, r)]
+
+    def part(name, lo, hi, own=True):
+        return T[name][lo:hi, :], [(name, 0, 256, lo if own else None)], 256, 4
+
+    for i in range(2):
+        dma("y", "l_prev", T.PC[64 * i:64 * i + 64, :], T.prev[:, :], [], part("PC", 64 * i, 0)[1], 2)
+    for i in range(4):
+        dma("s", "l_kid", T.KC[32 * i:32 * i + 32, :], (T.kid0, T.kid1)[i % 2][:, :], [], part("KC", 32 * i, 0)[1], 4)
     dma("y", "l_cur", T.CURI[:], T.cur[:, :], [], ["CURI"])
-    dma("s", "l_kid0", T.KC[:, 0:64], T.kid0[:, :], [], [("KC", 0, 64)])
-    dma("y", "l_prev", T.PC[:], T.prev[:, :], [], ["PC"])
-    dma("s", "l_kid1", T.KC[:, 64:128], T.kid1[:, :], [], [("KC", 64, 128)])
-    dma("s", "l_start", T.STI[:], T.start[:, :], [], ["STI"])
+    dma("y", "l_start", T.STI[:], T.start[:, :], [], ["STI"])
     dma("y", "l_x", T.XW[:], T.x[:, :], [], ["XW"])
+    dma("s", "l_z", T.ZW[:, 0:1024], T.z[:, :], [], [("ZW", 0, 1024)])
 
-    iota("IP", [[0, 1]], 0, 1, False)
-    iota("IC", [[1, 144]], -15, 0, True)
-    iota("OWN", [[1, 64]], 0, 64, False)
-    iota("I14", [[1, 14]], 0, 14, False)
-    iota("I8", [[1, 8]], 0, 0, True)
-    iota("T0", [[16, 8]], 1792, 0, True)
-    iota("J2", [[1, 256]], 0, 0, True)
-    iota("JN", [[-1, 128]], -1, 0, True)
-    iota("ID", [[1, 128]], 0, -1, True)
-    iota("IG", [[1, 240]], -112, 0, True)
-    iota("CURW", [[1, 1024]], 0, 0, True)
+    iota(S("IP"), [[0, 1]], 0, 1)
+    iota(S("I16"), [[0, 8], [1, 16]])
+    iota(S("N0"), [[256, 4]], 1024)
+    iota(S("J2"), [[1, 256]])
+    iota(S("THP"), [[0, 1]])
+    iota(S("OWN"), [[1, 256]], 0, 256)
+    iota(S("WK"), [[0, 384]])
+    iota(S("D0"), [[0, 32], [66000 - int(8 * SLOPE) - DUP, 2]], -66000)
+    iota(S("IDI"), [[1, 128]], 0, -1)
+    iota(S("IG"), [[1, 8], [0, 16]])
+    for b in ("WP", "WW", "WA"):
+        iota(S(b), [[0, 40]])
+    for lo, hi in ((1024, DUP), (DUP + 1024, DUP + TB)):
+        iota(S("ZW", lo, hi), [[0, hi - lo]])
+    iota(S("IC"), [[1, 144]], -15)
+    iota(S("PF"), [[0, 1]], 0, 1)
+    iota(S("CURW"), [[0, 1024]])
 
-    fill("ZB", 0, 512, 0.0)
-    for b, lo, hi in (("KW", 0, 512), ("KW", 512, 1024), ("KW", 1024, 1536), ("KW", 1536, TB), ("ZW", 1024, 1536),
-                      ("ZW", 1536, TB), ("RW", 1024, 1536), ("RW", 1536, 2048)):
-        act(T[b][:, lo:hi], [(b, lo, hi)], T.ZB[:, 0:hi - lo], ["ZB"])
-    fill("PW", 0, 2048, 0.0)
-    ip = (T.IP[:], ("IP", 0, 1))
-    for i, (n, o) in enumerate(((4, A.arith_shift_right), (15, A.bitwise_and), (31, A.bitwise_and))):
-        ts(T.IQ[:, i:i + 1], [("IQ", i, i + 1)], T.IP[:], ["IP"], n, None, o)
-    ts(T.OWN2[:], ["OWN2"], T.OWN[:], ["OWN"], 1023, None, A.bitwise_and)
-    iq = [(T.IQ[:, i:i + 1], ("IQ", i, i + 1)) for i in range(3)]
-    p4, p16 = colop(iq[0], 1.0, None, A.mult), colop(iq[0], 16.0, None, A.mult)
-    p15, p31 = colop(iq[1], 1.0, None, A.mult), colop(iq[2], 1.0, None, A.mult)
+    fill(S("ZB"), 0.0)
+    fill(S("PW"), 0.0)
+    for i, (n, o) in enumerate(((15, A.bitwise_and), (4, A.arith_shift_right), (31, A.bitwise_and))):
+        ts(S("IQ", i, i + 1), S("IP"), n, o)
+    cp(col(3), S("IQ"))
+    p15, p4, p31 = [S("col", i, i + 1) for i in range(3)]
+    ts(S("MD"), S("I16"), p15, A.is_equal)
+    e = [S("MD", r, r + 1) for r in range(16)]
+    m78, lt4 = colsum(S("MD", 7, 9)), colop(p15, 4.0, A.is_lt)
+    m25, m68 = colsum(S("MD", 2, 6)), colsum(S("MD", 6, 9))
+    ts(S("BN"), S("N0"), m25, A.mult, m68, A.add)
+    for lo in (0, DUP):
+        act(S("KW", lo, lo + 1024), S("ZB"), F.Identity, bias=m78)
+    for lo in (0, DUP):
+        for t in range(4):
+            n = 128 if lo and t == 3 else 256
+            act(S("KW", lo + 1024 + 256 * t, lo + 1024 + 256 * t + n), S("J2", 0, n), F.Identity, lt4, S("BN", t, t + 1))
 
-    cp(T.SL0[:], ["SL0"], T.CURI[:], ["CURI"])
-    ts(T.PCL[:], ["PCL"], T.PC[:], ["PC"], 255, None, A.bitwise_and)
-    cp(T.PB0[:], ["PB0"], T.PCL[:], ["PCL"])
-    tt(T.PB1[:], ["PB1"], T.PC[:], T.PCL[:], ["PC", "PCL"], A.subtract)
-    dma("y", "d_p", T.PW[0:128:16, :], T.PB0[:], ["PB0"], [("PW", 0, 2048, 0)], 2)
-    dma("y", "d_p", T.PW[1:128:16, :], T.PB1[:], ["PB1"], [("PW", 0, 2048, 1)], 2)
-    ts(T.KCL[:], ["KCL"], T.KC[:], ["KC"], 255, None, A.bitwise_and)
-    tt(T.KBF[:], ["KBF"], T.KC[:, 0:64], T.OWN2[:], [("KC", 0, 64), "OWN2"], A.is_equal)
-    cp(T.KBL[:], ["KBL"], T.KCL[:], ["KCL"])
-    tt(T.KBH[:], ["KBH"], T.KC[:], T.KCL[:], ["KC", "KCL"], A.subtract)
-    for q, b, lo in ((15, "KBF", 0), (0, "KBL", 0), (2, "KBL", 64), (1, "KBH", 0), (3, "KBH", 64)):
-        dma("y", "d_k", T.KW[q:128:16, 0:1024], T[b][:, lo:lo + 64], [(b, lo, lo + 64)], [("KW", 0, 1024, q)], 5)
-    dma("y", "l_z", T.ZW[:, 0:1024], T.z[:, :], [], [("ZW", 0, 1024)])
+    ts(part("OWN", 64, 96), part("OWN", 64, 96), 1023, A.bitwise_and)
+    for src, mid, dst in (("PC", "PCL", "PB"), ("KC", "KCL", "KB")):
+        for lo, bits in ((0, 255), (64, 2047 - 255)):
+            ts(part(mid, lo, lo + 64), part(src, lo, lo + 64, False), bits, A.bitwise_and)
+        cp(S(dst), S(mid))
+    cp(part("KF", 0, 64), part("KC", 0, 64, False))
+    tt(part("KF", 64, 96), part("KC", 64, 96, False), part("OWN", 64, 96), A.is_equal)
+    cp(S("SL", 0, 64), S("CURI"))
+    cp(S("ST"), S("STI"))
+    for r in range(2):
+        dma("y", "d_p", rows("PW", r, 0, 2048)[0], T.PB[64 * r:64 * r + 64, :], ["PB"], rows("PW", r, 0, 2048)[1], 2)
+    for sem, lo in (("d_k", 0), ("d_k2", DUP)):
+        for r, (b, i) in enumerate((("KB", 0), ("KB", 1), ("KB", 2), ("KB", 3), ("KF", 0), ("KF", 1), ("KF", 2))):
+            r = (0, 1, 4, 5, 2, 3, 6)[r]
+            dma("y", sem, rows("KW", r, lo, lo + 1024)[0], T[b][32 * i:32 * i + 32, :], [b], rows("KW", r, lo, lo + 1024)[1], 7)
+    dma("y", "l_z2", T.ZW[:, DUP:DUP + 1024], T.z[:, :], [], [("ZW", DUP, DUP + 1024)])
     dma("y", "l_w", T.WI[:], T.w[:, :], [], ["WI"])
-    dma("y", "l_th", T.THR[:], T.th[:, :], [], ["THR"])
-    dma("y", "l_env", T.EM[:], T.env[:, :], [], ["EM"])
-    dma("y", "l_rs", T.RW[:, 0:1024], T.rs[:, :], [], [("RW", 0, 1024)])
+    for r in (7, 8):
+        dma("y", "l_th", rows("THP", r, 0, 1)[0], T.th[:, :], [], rows("THP", r, 0, 1)[1], 2)
+    dma("y", "l_env", T.EM[:, 0:1024], T.env[:, :], [], [("EM", 0, 1024)])
+    for lo in (0, DUP):
+        dma("y", "l_rs", T.RW[:, lo:lo + 1024], T.rs[:, :], [], [("RW", lo, lo + 1024)], 2)
 
-    def vmat(name, s2, more=()):
-        ts(T[name][:], [name], T.IC[:], ["IC", p16[1]] + list(more), p16[0], s2, A.is_equal, A.mult)
+    wp = colop(p15, 2.0, A.is_lt)
+    ts(S("R3"), S("I16", 0, 8), p4, A.is_equal)
+    tt(col(2), S("MD", 0, 2), S("MD", 4, 6), A.add)
+    wk0, wk1 = S("col", ncol[0] - 2, ncol[0] - 1), S("col", ncol[0] - 1, ncol[0])
+    ts(S("WP", 3, 35, 4), S("R3"), wp, A.mult)
+    wk0s = colop(e[7], -float(DUP), A.mult, wk0, A.add)
+    ts(S("IDN"), S("IDI"), 0.0, A.is_equal, -1.0, A.mult)
+    ts(S("WC"), S("R3"), -SLOPE, A.mult)
+    for b in ("HX", "HS"):
+        cp((T[b][:], [b], 280, 2), S("ZB", 0, 280))
+    for i in range(4):
+        ts(S("WK", 98 * i + 1, 96 * i + 64, 8), S("R3"), wk0s, A.mult)
+        ts(S("WK", 97 * i + 64, 96 * i + 96, 4), S("R3"), wk1, A.mult)
+    ts(S("GS"), S("IG"), p4, A.is_equal)
+    ts(S("SJ"), S("MD", 0, 16), -2.0, A.mult, 1.0, A.add)
+    fill(S("CT", 0, 1), -1.0)
+    ts(S("WL"), S("GS"), e[6], A.mult, -1024.0, A.mult)
 
-    wp, lt4 = colop(p15, 2.0, None, A.is_lt), colop(p15, 4.0, None, A.is_lt)
-    eq15 = colop(p15, 15.0, None, A.is_equal)
-    m15 = colop(eq15, 4194304.0, None, A.mult)
-    wk1 = colsum(lt4, wp, A.subtract)
-    ws = colsum(wp, m15)
-    wk2 = colop(wk1, 2048.0, None, A.mult)
-    cp(T.ST[:], ["ST"], T.STI[:], ["STI"])
-    vmat("VP", wp[0], [wp[1]])
-    vmat("V4", 4096.0)
-    wkk = colsum(ws, wk2)
-    vmat("VK1", wk1[0], [wk1[1]])
-    vmat("VKK", wkk[0], [wkk[1]])
+    at(-2.9)
+    for b in range(11):
+        at(-2.9 if b < 8 else b - 7.75)
+        ts(S("CT", 1 << b, 2 << b), S("CT", 0, 1 << b), S("SJ", b, b + 1), A.mult)
+    at(0.25)
+    cp(S("CURF"), S("CURI"))
+    cp((T.HH[:], ["HH"], 280, 2), S("ZB", 0, 280))
+    dma("y", "d_cw", T.CURW[0:128:16, :], T.CURF[:], ["CURF"], ["CURW"])
+    at(1.25)
+    p16 = colop(p4, 16.0, A.mult)
+    wf = colop(S("WI"), 1.0, A.mult)
+    ts(S("WA", 3, 35, 4), S("R3"), 97.0, A.mult)
+    ts(S("WW", 3, 35, 4), S("R3"), wf, A.mult)
+    at(2.25)
+    dma("y", "d_ct", T.CT[:, DUP:DUP + 1792], T.CT[:, 0:1792], [("CT", 0, 1792)], [("CT", DUP, DUP + 1792)])
+    at(3.25)
+    ts(S("EM", 0, 1024), S("EM", 0, 1024), -256.0, A.add)
+    send("e", "EP", 0, "EM", 0, 1024)
+    for b in ("EM", "EP"):
+        for i, n in ((1, 1024), (2, EW - 2048)):
+            dma("y", "d_%s%d" % ("m" if b == "EM" else "e", i), T[b][:, 1024 * i:1024 * i + n], T[b][:, 0:n], [(b, 0, n)],
+                [(b, 1024 * i, 1024 * i + n)])
+    for lo, hi in ((1024, DUP), (DUP + 1024, DUP + 1792)):
+        iota(S("RW", lo, hi), [[0, hi - lo]])
+    iota(S("JN"), [[0, 2], [1, 128]])
+    iota(S("ON"), [[0, 128]], 1)
+    iota(S("NEG"), [[0, 16]], -8192)
+    iota(S("NL"), [[0, 128]], 0, -1)
+    iota(S("RB"), [[0, 1]], -11 * 4096, -32)
+    at(4.25)
+    ts(S("VP"), S("IC"), p16, A.is_equal, wp, A.mult)
+    ts(S("VW"), S("IC"), p16, A.is_equal, wf, A.mult)
+    ts(S("THL"), S("THP"), 255, A.bitwise_and)
+    at(5.25)
+    ce = colop(p31, 11.0, A.is_lt, 64.0, A.mult)
+    c27, c16 = colop(p31, 27.0, A.is_lt, 64.0, A.mult), colop(p31, 16.0, A.is_lt, 64.0, A.mult)
+    thh = col()
+    tt(thh, S("THP"), S("THL"), A.subtract)
+    wa, m13 = colop(S("THL"), e[8], A.mult), colsum(S("MD", 1, 4, 2))
+    at(6.25)
+    co, wb = colop(c27, c16, A.subtract), colop(thh, 8192.0, A.add, e[7], A.mult)
+    wc, wd = colop(e[6], 8192.0, A.mult, wa, A.subtract), colop(e[7], -1792.0, A.mult, wk0, A.add)
+    mk, two = colop(m13, m78, A.add), colop(lt4, 2.0, A.mult)
+    at(7.25)
+    wq = colop(wc, wb, A.subtract)
+    ts(S("WQ", 128, 256), S("GS"), wd, A.mult)
+    ts(S("BK"), S("N0"), m25, A.mult, mk, A.add)
+    ts(S("ID"), S("IDI"), 0.0, A.is_equal)
+    ts(S("WQ", 0, 128), S("GS"), wq, A.mult)
+    at(8.25)
+    ts(S("IDM"), S("IDI"), 0.0, A.is_equal, -1.0, A.mult)
+    ts(S("LM"), S("MD"), S("PF"), A.mult)
+    ts(S("MB"), S("MD"), -1e9, A.mult, 1e9, A.add)
+    cp(S("R3H"), S("R3"))
+    for t in range(3):
+        at(9.35 + ROUND * t)
+        act(S("KN", 128 * t, 128 * t + 128), S("J2", 0, 128), F.Identity, two, S("BK", t, t + 1))
 
-    def more_columns():
-        re, ro = colop(p31, 15.0, None, A.is_equal), colop(p31, 31.0, None, A.is_equal)
-        ce, c27 = colop(p31, 11.0, 64.0, A.is_lt, A.mult), colop(p31, 27.0, 64.0, A.is_lt, A.mult)
-        c16 = colop(p31, 16.0, 64.0, A.is_lt, A.mult)
-        rb = colop(ip, -703.0, None, A.add)
-        e0, e1 = colop(p15, 0.0, None, A.is_equal), colop(p15, 1.0, None, A.is_equal)
-        e2, e3 = colop(p15, 2.0, None, A.is_equal), colop(p15, 3.0, None, A.is_equal)
-        co, c13, c02 = colsum(c27, c16, A.subtract), colsum(e1, e3), colsum(e0, e2)
-        c02d = colop(c02, 2.0, None, A.mult)
-        his = [colop(c13, 1024.0 + 256 * t, None, A.mult) for t in range(3)]
-        return re, ro, ce, co, rb, c02, c02d, [colsum(h, e2) for h in his], [colsum(h, eq15) for h in his]
+    W = ("pA", "pB")
 
-    def scaled(out, w, in_, r, s, b):
-        act(out, [w], in_, [r, s[1], b[1]], F.Identity, scale=s[0], bias=b[0])
+    def blocks(src, h):
+        return [S(src, 512 * h + i, 512 * h + 512, 4) for i in range(4)]
 
-    def tables():
-        scaled(T.SCE[:], "SCE", T.JN[:], "JN", re, ce)
-        scaled(T.SCO[:], "SCO", T.JN[:], "JN", ro, co)
-        for t in range(3):
-            lo, hi = 128 * t, 1024 + 256 * t
-            scaled(T.KN[:, lo:lo + 128], ("KN", lo, lo + 128), T.J2[:, 0:128], "J2", c02d, kbs[t])
-            scaled(T.KW[:, hi:hi + 256], ("KW", hi, hi + 256), T.J2[:], "J2", c02, kcs[t])
+    def words(bank, c0, src, h, wt):
+        mms([(S(bank, c0, c0 + 32), b, S(wt, 3 - i, 35 - i)) for i, b in enumerate(blocks(src, h))])
 
-    def hand_ahead():
-        wf = colop((T.WI[:], "WI"), 1.0, None, A.mult)
-        vmat("VW", wf[0], [wf[1]])
-        ts(T.EM[:], ["EM"], T.EM[:], ["EM"], -256.0, None, A.add)
-        send("c0", "CP", 0, "XA0", 0, 1024)
-        send("e", "EP", 0, "EM", 0, 1024)
+    def slots(buf, h):
+        return T[buf][:, 35 * h + 3:35 * h + 35:4, :], [(buf, 35 * h, 35 * h + 35)], 32, 2
 
-    def codes():
-        for b in range(11):
-            ts(T.CBI[:, 14 * b:14 * b + 14], [("CBI", 14 * b, 14 * b + 14)], T.I14[:], ["I14"], b, 1, A.arith_shift_right,
-               A.bitwise_and)
-        fill("CBB", 154, 210, 0.0)
-        fill("CBB", 210, 224, 1.0)
-        ts(T.CBB[:, 0:154], [("CBB", 0, 154)], T.CBI[:], ["CBI"], 2.0, -1.0, A.mult, A.add)
-        for q in range(16):
-            dma("y", "d_c1", T.CD[q, :], T.CBB[:, 14 * q:14 * q + 14], [("CBB", 14 * q, 14 * q + 14)], [("CD", 0, 1792, q)], 16)
-        for q in range(8):
-            dma("y", "d_c2", T.CT[16 * q:16 * q + 16, :], T.CD[:, :], ["CD"], [("CT", 0, 1792, q)], 8)
-        cp(T.CURF[:], ["CURF"], T.CURI[:], ["CURI"])
-        dma("y", "d_cw", T.CURW[0:128:16, :], T.CURF[:], ["CURF"], ["CURW"])
+    def back(bank, c0, buf, h):
+        mms([(S(bank, c0, c0 + 32), (T[buf][:, 35 * h + 3 - j:35 * h + 35 - j, :], [(buf, 35 * h, 35 * h + 35)]),
+              S("IDN", j, 128, 4)) for j in range(4)])
 
-    def thresholds():
-        vmat("V97", 97.0)
-        ts(T.DM[:], ["DM"], T.I8[:], ["I8", p4[1]], p4[0], None, A.is_equal)
-        op("g", lambda: g.partition_broadcast(T.THB[:], T.THR[:], 128), ["THR"], ["THB"])
-        ts(T.TL[:], ["TL"], T.T0[:], ["T0", p15[1]], p15[0], None, A.add)
-        ts(T.EY[:], ["EY"], T.ID[:], ["ID"], 0.0, None, A.is_equal)
-        ts(T.G0[:], ["G0"], T.IG[:], ["IG", p15[1]], p15[0], None, A.is_equal)
-        tt(T.THM[:], ["THM"], T.THB[:], T.DM[:], ["THB", "DM"], A.mult)
-        ts(T.T2[:], ["T2"], T.TL[:], ["TL"], 2.0, -1792.0, A.mult, A.add)
-        ts(T.LN[:], ["LN"], T.TL[:], ["TL"], 4352.0, None, A.add)
-        c, w = col()
-        op("v", lambda: g.vector.tensor_reduce(c, T.THM[:], AxisListType.X, A.add), ["THM"], [w])
-        return colop((c, w), 4096.0, None, A.mult)
+    def wrap(bank, lt, src, m, ks, start, stop, contiguous=False):
+        mms([(S(bank, 0, m), S(lt, 15 - k, 143 - k), S(src, k * m, (k + 1) * m) if contiguous else S(src, k, 16 * m, 16))
+             for k in ks], start, stop)
 
-    def zcmp(t, k):
-        xa, lst, b = "XA%d" % (t % 2), "FL%d" % (k % 2) if k else "ST", "BT%d" % (k % 2)
-        lo, hi = 1024 * k, 1024 * k + 1024
-        tt(T[b][:], [b], T.ZW[:].indirect(T[lst][:]), T[xa][:, lo:hi], ["ZW", lst, (xa, lo, hi)], A.is_le)
-
-    def kgather(k, ks=1024):
-        for q, lo, hi in (("s", 0, ks), ("v", ks, 1024)):
-            gx(q, "KG%d" % (k % 2), 0, "KW", 0, TB, "FL%d" % (k % 2) if k else "ST", lo, hi)
-
-    def wraps(k):
-        wrap("pK", "VKK", "KG%d" % (k % 2), 0, 1024)
-        wrap("pA", "V4", "BT%d" % (k % 2), 0, 1024)
-
-    def select(k):
-        fl = "FL%d" % ((k + 1) % 2)
-        cp(T.KI[:], ["KI"], T.pK[:, 0:64], ["pK"])
-        ts(T.K0[:], ["K0"], T.KI[:], ["KI"], 2047, None, A.bitwise_and)
-        ts(T.K1[:], ["K1"], T.KI[:], ["KI"], 11, 2047, A.arith_shift_right, A.bitwise_and)
-        ts(T.U[:], ["U"], T.K0[:], ["K0"], 34816.0, None, A.add)
-        ts(T.LF[:, 8 * k:8 * k + 8], [("LF", 8 * k, 8 * k + 8)], T.KI[:, 0:8], ["KI"], 12, 1024, A.arith_shift_right, A.bitwise_and)
-        tt(T.TN[:], ["TN"], T.pA[:, 0:64], T.K1[:], ["pA", "K1"], A.add)
-        tt(T.TM[:], ["TM"], T.TN[:], T.U[:], ["TN", "U"], A.max)
-        ts(T.FI[:], ["FI"], T.TM[:], ["TM"], 2047, None, A.bitwise_and)
-        cp(T[fl][:], [fl], T.FI[:], ["FI"])
-
-    th = None
-    gx("v", "XA0", 0, "XW", 0, 2048, "SL0", 0, 1024)
-    for k in range(6):
-        sl, sn, pg = "SL%d" % (k % 2), "SL%d" % ((k + 1) % 2), "PG%d" % (k % 2)
-        n = 1024 if k < 5 else 128
-        gx("s", pg, 0, "PW", 0, 2048, sl, 0, n)
-        if k:
-            gx("s", "XA0", 1024 * k, "XW", 0, 2048, sl, XV, 1024)
-        if k == 5:
-            tables()
-        kgather(k)
-        zcmp(0, k)
-        if k == 0:
-            re, ro, ce, co, rb, c02, c02d, kbs, kcs = more_columns()
-        wrap("pP", "VP", pg, 0, n)
-        wraps(k)
-        cp(T[sn][:, 0:n // 16], [(sn, 0, n // 16)], T.pP[:, 0:n // 16], ["pP"])
-        if k < 5:
-            gx("v", "XA0", 1024 * k + 1024, "XW", 0, 2048, sn, 0, XV)
+    def step(t, h, k):
+        n, lo, hi = ROUND * t + 2 * k + h, 512 * h, 512 * h + 512
+        top, lst = (DUP + TB, "FL") if k else (1024, "ST")
+        at(n - 0.9 if k or not t else n - 1.04 - 0.85 * h)
+        gx("s", "KG", 0, "KW", 0, top, lst, 0, lo, hi)
+        at(n)
+        if PRE and t and not k:
+            tt(S("BT", lo, hi), S("PG", lo, hi), S("pD%d" % h), A.is_le)
         else:
-            gx("s", "XA0", 6144, "XW", 0, 2048, sn, 0, 128)
-            th = thresholds()
-        if k == 0:
-            hand_ahead()
-        if k == 1:
-            wrap("pS", "VW", "XA0", 0, 1024)
-            codes()
-        if k == 2:
-            cp(T.SWI[:], ["SWI"], T.pS[:, 0:64], ["pS"])
-        select(k)
+            tt(S("BT", lo, hi), G("ZW", 0, top, lst, lo, hi), S("XA%d" % (t % 2), 1024 * k + lo, 1024 * k + hi), A.is_le)
+        mms([(S(W[h], 0, 96), b, S("WK", 96 * i, 96 * i + 96)) for i, b in enumerate(blocks("KG", h))], True, False)
+        mms([(S(W[h], 2 * i, 64, 8), b, S("WC")) for i, b in enumerate(blocks("BT", h))], False, True)
+        if t < 2 and h == 0:
+            mms([(S("pL", 0, 128), S("KG", 0, 128), S("WL"))], k == 0, k == 5)
+        at(n + 0.5)
+        o = S("S2", 64 * h, 64 * h + 64)
+        op("v", lambda: g.vector.tensor_tensor_scan(o[0], T.D0[:], T[W[h]][:, 0:64], 0.0, A.subtract, A.max),
+           ["D0", (W[h], 0, 64)], o[1], cycles(64))
+        at(n + 0.6)
+        tt(slots("HS", h), S(W[h], 64, 96), S("S2", 64 * h + 1, 64 * h + 64, 2), A.min)
+        back(W[h], 96, "HS", h)
+        at(n + (0.8 if (h, k) == (1, 5) else 1.1))
+        ts(S("FL", 32 * h, 32 * h + 32), S(W[h], 96, 128), -1.0, A.mult, float(DUP), A.add)
 
-    def end_of_round(t):
-        xa, x0, fl = "XA%d" % (t % 2), 64 * t, "FL0"
-        gx("s", "CG", 0, "CT", 0, 1792, fl, 0, 128)
-        gx("s", "RN", 0, "RW", 0, 2048, fl, 0, 128)
-        gx("s", "KG6", 0, "KW", 0, TB, fl, 0, 128)
-        for h in range(2):
-            lo, hi = 512 * h, 512 * h + 512
-            tt(T.BT0[:, lo:hi], [("BT0", lo, hi)], T.RW[:].indirect(T[fl][:, lo // 16:hi // 16]), T[xa][:, lo:hi],
-               ["RW", (fl, lo // 16, hi // 16), (xa, lo, hi)], A.is_gt)
-            wrap("pS" if h else "pP", "V97", "BT0", lo, 512)
+    def hsum(t, h, n, n2):
+        lo, hi, bank = 32 * h, 32 * h + 32, "pD%d" % (2 + h)
+        at(n)
+        words(bank, 0, "XA%d" % (t % 2), h, "WW")
+        cp(S("HI", lo, hi), S(bank, 0, 32))
+        at(n + 0.03)
+        ts(S("HJ", lo, hi), S("HI", lo, hi), 1023, A.bitwise_and)
+        at(n + 0.06)
+        ts(slots("HH", h), S("HJ", lo, hi), -1024.0, A.add)
+        if t:
+            back(bank, 32, "HH", h)
+            at(n2)
+            ts(S("HL", lo, hi), S(bank, 32, 64), -1.0, A.mult, 1024.0, A.add)
 
-        def column(h):
-            q0, q1, ps = 32 * h, 32 * h + 32, "pS" if h else "pP"
-            tt(T.QI[:, q0:q1], [("QI", q0, q1)], T[ps][:, 0:32], T.SWI[:, q0:q1], [ps, "SWI"], A.add)
-            ts(T.QI2[:, q0:q1], [("QI2", q0, q1)], T.QI[:, q0:q1], [("QI", q0, q1)], 1023, None, A.bitwise_and)
-            cp(T.IX[:, x0 + q0:x0 + q1], [("IX", x0 + q0, x0 + q1)], T.QI2[:, q0:q1], [("QI2", q0, q1)])
-            send("i%d" % t + "ab"[h], "IXP", x0 + q0, "IX", x0 + q0, x0 + q1)
-        column(0)
-        tt(T.BE[:], ["BE"], T.CG[:], T.SCE[:], ["CG", "SCE"], A.mult)
-        tt(T.BO[:], ["BO"], T.CG[:], T.SCO[:], ["CG", "SCO"], A.mult)
-        column(1)
-        banks = ("pD0", "pD1", "pK", "pN")
+    def outcome(t, h):
+        n, lo, hi, x0 = ROUND * t + 11 + h, 512 * h, 512 * h + 512, 64 * t + 32 * h
+        at(n + 0.2)
+        tt(S("BT", lo, hi), G("RW", 0, DUP + 1792, "FL", lo, hi), S("XA%d" % (t % 2), lo, hi), A.is_gt)
+        words(W[h], 128, "BT", h, "WA")
+        at(n + (0.4 if h else 0.7))
+        tt(slots("HX", h), S(W[h], 128, 160), slots("HH", h), A.add)
+        back(W[h], 160, "HX", h)
+        at(n + (0.5 if h else 1.15))
+        ts(S("IX", x0, x0 + 32), S(W[h], 160, 192), -1.0, A.mult, 1024.0, A.add)
+        send("i%d" % t + "ab"[h], "IXP", x0, "IX", x0, x0 + 32)
 
-        def dots(a):
-            def fn():
-                r = None
-                for i, b in enumerate((T.BE, T.BO)):
-                    r = g.tensor.matmul(T[banks[a]][:, 128 * i:128 * i + 128], T.CG[32 * a:32 * a + 32, :],
-                                        b[32 * a:32 * a + 32, :], True, True)
-                return r
-            op("t", fn, ["CG", "BE", "BO"], [banks[a]])
+    def band(name, a):
+        return T[name][32 * a:32 * a + 32, :], [name]
+
+    def splits(t):
+        xa, n0, n = "XA%d" % (t % 2), 1024 + 256 * t, ROUND * t
+        at(n + 11.11)
+        act(S("BE"), G("CT", 0, DUP + 1792, "FL", 0, 128), F.Identity, ce)
+        act(S("BO"), G("CT", 0, DUP + 1792, "FL", 0, 128), F.Identity, co)
+        act(S("RN"), G("RW", 0, DUP + 1792, "FL", 0, 128))
+        act(S("KG6"), G("KW", 0, DUP + TB, "FL", 0, 128))
+        at(n + 11.9)
+        mms([(S("pM", 0, 256), S("KG6"), S("WQ")), (S("pM", 128, 256), S("ID"), S("NL"))], True, False)
         for a in range(4):
-            dots(a)
-        wrap("pA", "VKK", "KG6", 0, 128)
-        for q in range(8):
-            ps, i = banks[q // 2], 128 * (q % 2)
-
-            def relu(q=q, ps=ps, i=i):
-                return g.scalar.activation(T.RJ[:, 128 * q:128 * q + 128], T[ps][:, i:i + 128], F.Relu, bias=rb[0],
-                                           accum_out=T.FM[:, q:q + 1])
-            op("s", relu, [ps, rb[1]], [("RJ", 128 * q, 128 * q + 128), ("FM", q, q + 1)])
-        tt(T.S1[:], ["S1"], T.EM[:].indirect(T.IX[:, x0:x0 + 8]), T[xa][:, 0:128], ["EM", ("IX", x0, x0 + 8), (xa, 0, 128)], A.add)
-        ts(T.V1[:], ["V1"], T.S1[:], ["S1"], 255, None, A.bitwise_and)
-        tt(T.DD[:], ["DD"], T.RN[:, 0:128], T.V1[:], [("RN", 0, 128), "V1"], A.subtract)
-        act(T.DA[:], ["DA"], T.DD[:], ["DD"], F.Abs)
+            bank = "pD%d" % a
+            at(n + 9.06 + a // 2)
+            mms([(S(bank, 0, 256), band("ON", a), band("JN", a))], True, False)
+            at(n + (11.15 if a < 2 else 11.8))
+            mms([(S(bank, 128 * i, 128 * i + 128), band(b, a), band(b, a)) for i, b in enumerate(("BE", "BO"))], False, True)
+            at(n + 11.85)
+            act(S("EE", 256 * a, 256 * a + 256), S(bank, 0, 256), F.Relu, bias=S("RB"))
+            at(n + (12.0 if a < 2 else 12.27))
+            mms([(S("pM", 16 * q, 16 * q + 16), S("EE", 128 * q, 128 * q + 128), S("NEG")) for q in (2 * a, 2 * a + 1)], False, False)
         if t < 2:
-            l = [(T.L24[:, 8 * i:8 * i + 8], ("L24", 8 * i, 8 * i + 8)) for i in range(5)]
-            tt(T.L24[:, 0:24], [("L24", 0, 24)], T.LF[:, 0:24], T.LF[:, 24:48], ["LF"], A.add)
-            tt(l[3][0], [l[3][1]], l[0][0], l[1][0], [l[0][1], l[1][1]], A.add)
-            tt(l[4][0], [l[4][1]], T.LN[:], l[2][0], [l[2][1], "LN"], A.subtract)
-            tt(l[0][0], [l[0][1]], l[4][0], l[3][0], [l[3][1], l[4][1]], A.subtract)
-            cp(T.XL[:], ["XL"], l[0][0], [l[0][1]])
-            gx("s", "XV6", 0, xa, 0, XAW, "XL", 0, 128)
-        lf, ft, fi, fq, fa, sa, sb, ra, rd = [(T.w8[:, 8 * i:8 * i + 8], ("w8", 8 * i, 8 * i + 8)) for i in range(9)]
-        ts(lf[0], [lf[1]], T.pA[:, 0:8], ["pA"], 4194304.0, None, A.is_ge)
-        tt(ft[0], [ft[1]], T.FI[:, 0:8], T.TL[:], [("FI", 0, 8), "TL"], A.subtract)
-        for q in range(8):
-            ts(T.EE[:, 8 * q:8 * q + 8], [("EE", 8 * q, 8 * q + 8)], T.DM[:], ["DM", ("FM", q, q + 1)], T.FM[:, q:q + 1], None,
-               A.is_gt)
-
-        def conv():
-            r = None
-            for q in range(8):
-                r = g.tensor.matmul(T.pP[:, 0:8], T.G0[:, 112 - 16 * q:240 - 16 * q], T.EE[:, 8 * q:8 * q + 8], q == 0, q == 7)
-            return r
-        wrap("pM", "V4", "DA", 0, 128)
-        op("t", conv, ["G0", "EE"], ["pP"])
-
-        def split_lists():
-            ts(fa[0], [fa[1]], T.pM[:, 0:8], ["pM", th[1]], th[0], None, A.is_ge)
-            tt(fi[0], [fi[1]], T.pP[:, 0:8], lf[0], ["pP", lf[1]], A.mult)
-            tt(sa[0], [sa[1]], fi[0], fa[0], [fi[1], fa[1]], A.mult)
-            tt(fq[0], [fq[1]], sa[0], ft[0], [sa[1], ft[1]], A.mult)
-            tt(sb[0], [sb[1]], fq[0], T.TL[:], [fq[1], "TL"], A.add)
-            cp(T.SCL[:], ["SCL"], sb[0], [sb[1]])
-            lo, hi = 128 * t, 128 * t + 128
-            cp(T.KW[:].indirect(T.SCL[:]), ["KW"], T.KN[:, lo:hi], [("KN", lo, hi), "SCL"])
-
-        def split_z():
-            cp(T.ZW[:].indirect(T.SCL[:]), ["ZW"], T.XV6[:], ["XV6", "SCL"])
-
-        def new_r():
-            ts(ra[0], [ra[1]], sa[0], [sa[1]], 256.0 * t - 768.0, None, A.mult)
-            tt(T.H1[:], ["H1"], T.RN[:, 0:128], T.V1[:], [("RN", 0, 128), "V1"], A.add)
-            tt(rd[0], [rd[1]], ra[0], T.T2[:], [ra[1], "T2"], A.add)
-            ts(T.H2[:], ["H2"], T.H1[:], ["H1"], 1, None, A.arith_shift_right)
-            cp(T.SCR[:, 0:8], [("SCR", 0, 8)], rd[0], [rd[1]])
-            ts(T.SCR[:, 8:16], [("SCR", 8, 16)], rd[0], [rd[1]], 1.0, None, A.add)
-            cp(T.RN[:, 128:256], [("RN", 128, 256)], T.H2[:], ["H2"])
-
-        def split_r():
-            cp(T.RW[:].indirect(T.SCR[:]), ["RW"], T.RN[:], ["RN", "SCR"])
-            if t == 1:
-                dma("y", "o_yr0", T.yr[:, 0:512], T.RW[:, 1024:1536], [("RW", 1024, 1536)], [])
-            if t == 2:
-                dma("y", "o_yr1", T.yr[:, 512:768], T.RW[:, 1536:1792], [("RW", 1536, 1792)], [])
-        return split_lists, split_z, new_r, split_r
+            at(n + 11.75)
+            tt(S("T5"), S("pL", 0, 128), S("MD"), A.mult)
+            at(n + 11.95)
+            mms([(S("pL", 128, 136), S("LM"), S("R3")), (S("pL", 128, 136), S("T5"), S("R3"))])
+            at(n + 12.32)
+            ts(S("XL"), S("pL", 128, 136), 6144.0, A.add)
+            gx("s", "XV6", 0, xa, 0, XAW, "XL", 0, 0, 128)
+        at(n + 12.3)
+        tt(S("S1"), G("EM", 0, EW, "IX", 1024 * t, 1024 * t + 128), S(xa, 0, 128), A.add)
+        at(n + 12.35)
+        ts(S("T1"), S("S1"), 0.0, A.is_lt, 256.0, A.mult)
+        mms([(S("pL", 256, 384), S(i), S(b)) for i, b in (("IDM", "RN"), ("ID", "S1"), ("ID", "T1"))])
+        act(S("DA"), S("pL", 256, 384), F.Abs)
+        at(n + 12.55)
+        mms([(S("pM", 0, 128), S("DA"), S("GS"))], False, True)
+        mms([(S("pL", 384, 512), S("ID"), S(b)) for b in ("RN", "S1", "T1")])
+        at(n + 12.7)
+        tt(S("SM"), S("pM", 0, 128), S("MB"), A.is_ge)
+        at(n + 12.75)
+        tt(S("T3"), S("pM", 128, 256), S("SM"), A.mult)
+        mms([(S("pM", 256, 264), S("LM"), S("R3")), (S("pM", 256, 264), S("T3"), S("R3H"))])
+        at(n + 12.85)
+        ts(S("SCL"), S("pM", 256, 264), 1792.0, A.add)
+        for lo in (0, DUP) if t < 2 else (0,):
+            at(n + (14.2 if lo else 12.9))
+            scatter("KW", lo, S("KN", 128 * t, 128 * t + 128))
+            at(n + (15.3 if lo else 12.95))
+            if t < 2:
+                scatter("ZW", lo, S("XV6"))
+        at(n + (16.2 if t < 2 else 12.72))
+        ts(S("SA"), S("pM", 0, 128), 0.0, A.is_ge)
+        at(n + (16.21 if t < 2 else 12.76))
+        mms([(S("pM", 384, 512), S("SA"), S("ID"))])
+        ts(S("H2"), S("pL", 384, 512), 0.5, A.mult, -0.25, A.add)
+        at(n + (17.2 if t < 2 else 12.95))
+        tt(S("RW", n0, n0 + 256, 2), S("pM", 384, 512), S("RN"), A.mult)
+        tt(S("RW", n0 + 1, n0 + 256, 2), S("pM", 384, 512), S("H2"), A.mult)
+        if t < 2:
+            at(n + 18.35)
+            act(S("RW", DUP + n0, DUP + n0 + 256), S("RW", n0, n0 + 256))
+        if t:
+            lo = 1024 if t == 1 else n0
+            dma("y", "o_yr%d" % (t - 1), T.yr[:, lo - 1024:n0 - 768], T.RW[:, lo:n0 + 256], [("RW", lo, n0 + 256)], [])
 
     def arrive(t, h):
-        lo, hi, x0, c0 = 512 * h, 512 * h + 512, 64 * t, 1024 * t
-        tt(T.SP[:, lo:hi], [("SP", lo, hi)], T.EP[:].indirect(T.IXP[:, x0 + lo // 16:x0 + hi // 16]), T.CP[:, c0 + lo:c0 + hi],
-           ["EP", ("IXP", x0 + lo // 16, x0 + hi // 16), ("CP", c0, c0 + 1024)], A.add)
-        ts(T.TT[:, lo:hi], [("TT", lo, hi)], T.SP[:, lo:hi], [("SP", lo, hi)], 0.0, 256.0, A.is_lt, A.mult)
+        n, lo, hi = ROUND * t, 512 * h, 512 * h + 512
+        at(n + (13.0 if h else ENVA))
+        tt(S("SP", lo, hi), G("EP", 0, EW, "IXP", 1024 * t + lo, 1024 * t + hi), S("CP", 1024 * t + lo, 1024 * t + hi), A.add)
+        at(n + (13.1 if h else 12.87))
+        ts(S("TT", lo, hi), S("SP", lo, hi), 0.0, A.is_lt, 256.0, A.mult)
 
-    def preds():
-        wrap("pN", "VW", "SP", 0, 1024, True, False, True)
-        wrap("pN", "VW", "TT", 0, 1024, False, True, True)
-
-    def preds_out(t):
+    def preds_out(t, bank):
         yf = "YF%d" % t
-        cp(T.YI[:], ["YI"], T.pN[:, 0:64], ["pN"])
-        ts(T.YI2[:], ["YI2"], T.YI[:], ["YI"], 1023, None, A.bitwise_and)
-        ts(T[yf][:], [yf], T.YI2[:], ["YI2"], 1024.0 + 1024 * t, None, A.add)
+        cp(S("YI", 0, 64), S(bank, 0, 64))
+        ts(S("YI", 64, 128), S("YI", 0, 64), 1023, A.bitwise_and)
+        ts(S(yf), S("YI", 64, 128), 1024.0 + 1024 * t, A.add)
         dma("y", "o_yp%d" % t, T.yp[:, 1024 * t:1024 * t + 1024], T[yf][:], [yf], [])
 
-    late = end_of_round(0)
-    for t in (1, 2):
-        xo, xa = "XA%d" % ((t - 1) % 2), "XA%d" % (t % 2)
+    def first_preds():
+        at(ROUND + 4.2)
+        cp(S("OA", 0, 64), S("HL"))
+        ts(S("OB", 0, 64), S("HL"), 64.0, A.mult)
+        ts(S("OA", 64, 128), S("OA", 0, 64), 4, A.arith_shift_right)
+        at(ROUND + 5.2)
+        ts(S("OB", 64, 128), S("OA", 64, 128), -1023.0, A.mult)
+        tt(S("OB", 0, 64), S("OB", 0, 64), S("OB", 64, 128), A.add)
+        cp(S("OL"), S("OB", 0, 64))
         for h in range(2):
-            lo, hi, pd = 512 * h, 512 * h + 512, "pD%d" % h
-            arrive(t - 1, h)
+            at(ROUND + 9.3 + h)
+            gx("s", "YPC", 0, "CURW", 0, 1024, "OL", 0, 512 * h, 512 * h + 512)
+        dma("y", "o_yp0", T.yp[:, 0:1024], T.YPC[0:128:16, :], ["YPC"], [])
 
-            def vsum(pd=pd, lo=lo, hi=hi):
-                g.tensor.matmul(T[pd][:], T.EY[:], T.SP[:, lo:hi], True, False)
-                return g.tensor.matmul(T[pd][:], T.EY[:], T.TT[:, lo:hi], False, True)
-            op("t", vsum, ["EY", ("SP", lo, hi), ("TT", lo, hi)], [pd])
-            act(T[xa][:, lo:hi], [(xa, lo, hi)], T[pd][:], [pd])
-            if h == 0:
-                late[0]()
-                kgather(0)
-        late[1]()
-        wrap("pS", "VW", "SP", 0, 1024, True, False)
-        wrap("pS", "VW", "TT", 0, 1024, False, True)
-        send("c%d" % t, "CP", 1024 * t, xa, 0, 1024)
-        zcmp(t, 0)
-        cp(T.SWI[:], ["SWI"], T.pS[:, 0:64], ["pS"])
-        ts(T.HI[:], ["HI"], T.SWI[:], ["SWI"], 1023, None, A.bitwise_and)
-        cp(T.HL[:], ["HL"], T.HI[:], ["HI"])
-        for k in range(6):
-            if k:
-                kgather(k, KS)
-                zcmp(t, k)
-            wraps(k)
-            d0 = 1024 * k
+    def items(dst, k, h, src, s0, s1, lst, l0, n, xv):
+        lo = 512 * h
+        at(n + 0.2)
+        gx("v", dst, 1024 * k, src, s0, s1, lst, l0, lo, lo + xv)
+        at(n + 0.3)
+        gx("s", dst, 1024 * k, src, s0, s1, lst, l0, lo + xv, lo + 512)
+
+    for k in range(6):
+        for h in range(2):
+            n = 2 * k + h - 2
+            items("XA0", k, h, "XW", 0, 2048, "SL", 1024 * k, n if k else -5, XV0[n] if k else 0)
             if k < 5:
-                gx("s", xa, d0 + 1024, xo, d0, d0 + 1024, "HL", 0, 1024)
-            elif t < 2:
-                gx("s", xa, d0 + 1024, xo, d0, d0 + 1024, "HL", 0, 128)
-            if k == 1:
-                late[2]()
-            if k == 2:
-                late[3]()
-            if k == 3 and t == 2:
-                preds()
-            if k == 4 and t == 2:
-                preds_out(1)
-            if k == 3 and t == 1:
-                oa, ob, oc, od = [(T.OA[:, 64 * i:64 * i + 64], ("OA", 64 * i, 64 * i + 64)) for i in range(4)]
-                ts(oa[0], [oa[1]], T.HI[:], ["HI"], 15, None, A.bitwise_and)
-                ts(ob[0], [ob[1]], T.HI[:], ["HI"], 4, None, A.arith_shift_right)
-                ts(oc[0], [oc[1]], oa[0], [oa[1]], 64.0, None, A.mult)
-                tt(od[0], [od[1]], oc[0], ob[0], [oc[1], ob[1]], A.add)
-                cp(T.OL[:], ["OL"], od[0], [od[1]])
-            select(k)
-        late = end_of_round(t)
-        if t == 1:
-            gx("s", "YPC", 0, "CURW", 0, 1024, "OL", 0, 1024)
-            dma("y", "o_yp0", T.yp[:, 0:1024], T.YPC[0:128:16, :], ["YPC"], [])
+                bank = "pD%d" % h
+                at(n + 0.2 if k else -3)
+                gx("s", "PG", 0, "PW", 0, 2048, "SL", 1024 * k, 512 * h, 512 * h + 512)
+                at(n + 1.06 if k else -0.5 + 0.51 * h)
+                words(bank, 0, "PG", h, "WP")
+                at(n + 1.4 if k else 0.06 + 0.2 * h)
+                cp(slots("HX", h), S(bank, 0, 32))
+                back(bank, 32, "HX", h)
+                at(n + 1.65 if k else 0.1 + 0.5 * h)
+                ts(S("SL", 64 * k + 64 + 32 * h, 64 * k + 96 + 32 * h), S(bank, 32, 64), -1.0, A.mult)
+    at(8.3)
+    gx("s", "PG", 0, "PW", 0, 2048, "SL", 5120, 0, 128)
+    at(9.07)
+    wrap("pM", "VP", "PG", 8, range(16), True, True)
+    at(9.65)
+    cp(S("SL", 384, 392), S("pM", 0, 8))
+    at(10.3)
+    gx("s", "XA0", 6144, "XW", 0, 2048, "SL", 6144, 0, 128)
+    at(-1)
+    send("c0", "CP", 0, "XA0", 0, 1024)
 
-    arrive(2, 0)
-    late[0]()
-    wrap("pK", "VP", "KW", 0, 1792, contiguous=True)
-    wrap("pA", "VK1", "KW", 0, 1792, contiguous=True)
-    act(T.YK0[:], ["YK0"], T.pK[:, 0:112], ["pK"])
-    act(T.YK1[:], ["YK1"], T.pA[:, 0:112], ["pA"])
-    dma("y", "o_yk0", T.yk0[:, :], T.YK0[:], ["YK0"], [])
-    dma("y", "o_yk1", T.yk1[:, :], T.YK1[:], ["YK1"], [])
-    arrive(2, 1)
-    preds()
-    late[2]()
-    late[3]()
-    preds_out(2)
-    for sem in sorted(total):
-        wait("g", (sem, total[sem], {}))
+    for t in range(3):
+        xo, xa, n = "XA%d" % ((t - 1) % 2), "XA%d" % (t % 2), ROUND * t
+        for h in range(2):
+            lo, hi = 512 * h, 512 * h + 512
+            if t:
+                if PRE:
+                    at(n - 1.03 + 0.1 * h)
+                    gx("s", "PG", 0, "ZW", 0, 1024, "ST", 0, lo, hi)
+                arrive(t - 1, h)
+                at(n - (0.95 if h else 1.2))
+                mms([(S("pD%d" % h), S("ID"), S("SP", lo, hi))], True, False)
+                at(n - (0.89 if h else 1.12))
+                mms([(S("pD%d" % h), S("ID"), S("TT", lo, hi))], False, True)
+                act(S(xa, lo, hi), S("pD%d" % h))
+                hsum(t, h, n + 1.12 if h else n - 0.8, n + (1.7 if h else 0.1))
+                for k in range(1, 6):
+                    items(xa, k, h, xo, 1024 * k - 1024, 1024 * k, "HL", 0, n + 2 * k + h - (2 if k > 1 else 2.2 - 0.7 * h),
+                          XV[1] if 2 < k else 0)
+            else:
+                hsum(t, h, 4.06 + h, 0)
+        if t:
+            at(n)
+            send("c%d" % t, "CP", 1024 * t, xa, 0, 1024)
+        if t == 1:
+            at(n + 10.3)
+            gx("s", xa, 6144, xo, 5120, 6144, "HL", 0, 0, 128)
+            first_preds()
+        if t == 2:
+            for j in range(2):
+                at(n + 4.06 + j)
+                wrap("pM", "VW", xa, 64, range(8 * j, 8 * j + 8), j == 0, j == 1, True)
+            at(n + 6.2)
+            preds_out(1, "pM")
+        for k in range(6):
+            for h in range(2):
+                step(t, h, k)
+        for h in range(2):
+            outcome(t, h)
+        splits(t)
+
+    n = 2 * ROUND
+    at(n + 12.91)
+    dma("y", "o_yk0", T.yk0[:, :], T.KW[2:128:16, 0:1792], [("KW", 0, 1792)], [])
+    dma("s", "o_yk1", T.yk1[:, :], T.KW[3:128:16, 0:1792], [("KW", 0, 1792)], [])
+    for h in range(2):
+        arrive(2, h)
+        ks = range(8 * h, 8 * h + 8)
+        at(n + 12.8 + 0.25 * h)
+        wrap("pA", "VW", "SP", 64, ks, h == 0, False, True)
+        at(n + 12.88 + 0.25 * h)
+        wrap("pA", "VW", "TT", 64, ks, False, h == 1, True)
+    at(n + 14)
+    preds_out(2, "pA")
+    issue()

@@ -7,22 +7,27 @@ TB = 1920
 XAW = 6272
 EW = 2592
 SLOPE = 3968.0
-XV = (320, 192)
-XV0 = [256, 256, 128, 128, 128, 128, 192, 192, 256, 256]
+ROUND = 14
 CYCLE, GATHER, GATHER2, SCATTER, WAKE, AHEAD = 0.87e-3, 1.56, 1.8, 3.8, 0.06, 0.15
 LOCAL, REMOTE = (1.7, 220e3, 0.15), (2.0, 45e3, 0.3)
-ROUND = 14
-PRE = False
-ENVA = 12.78
+KIB = dict(l_prev=64, l_x=512, l_z=256, l_z2=256, l_env=256, l_rs=256, d_ct=448, d_m1=256, d_e1=256, d_m2=136, d_e2=136, l_w=1, l_th=1)
+TN = dict(
+    kg=-1.53, mm=-0.57, scan=0.46, tt=0.5, fl=1.1, flb=0.66, xv=0.2, xs=0.3, pg=-0.93, pw=1.06, px=1.4, pl=1.65,
+    ra=0.06, hxa=0.7, ixa=1.19, rb=0.2, hxb=0.4, ixb=0.5,
+    d0=11.75, d2=11.28, ee=11.85, n0=12.0, n2=12.47, va=11.9, t5=11.75, xm=11.95, xl=12.25, rn=11.96, s1=12.3, t1=12.35, pd=12.35,
+    far=12.55, ph=12.6, sm=12.7, t3=12.75, scl=12.85, sk=12.9, sz=12.73, sk2=13.2, sz2=15.3, sa=16.2, rw=17.2, sa2=13.03, rw2=13.49,
+    enva=12.6, tta=12.88, envb=13.0, ttb=12.79, pga=-1.03, pgb=-0.93, v1a=-1.2, v2a=-1.12, v1b=-1.93, v2b=-1.51, eva=3.5, evb=4.5,
+    ha=-0.8, hla=0.1, hb=1.12, hlb=1.7, kg0=-1.04, kg1=0.3, x1=2.2,
+    w5=9.07, ol=40.2, ypc=40.4, p1=10.5,
+    xv0=224, xv1=224)
 
 BUFS = {
     "bfloat16": dict(XW=2048, PW=2048, ZW=DUP + TB, RW=DUP + 1792, CT=DUP + 1792, EM=EW, EP=EW, CP=3072, XA0=XAW, XA1=XAW, BT=1024,
                      KG=1024, PG=1024, SP=1024, TT=1024, ZB=1024, EE=1024, PB=256, KG6=128, BE=128, BO=128, RN=128, DA=128,
-                     XV6=128, S1=128, T1=128, T5=128, SA=128, SM=128, GS=128, WL=128, WQ=256, NEG=16, ID=128, IDM=128, NL=128,
-                     LM=128, R3=8, WC=8, WA=40, WP=40, WW=40, WK=384, VP=144, VW=144, ON=128, JN=256),
-    "float16": dict(IDN=128, R3H=8, T3=128),
-    "int32": dict(CURI=64, STI=64, PC=256, PCL=256, KC=256, KCL=256, OWN=256, IP=1, IQ=3, WI=1, THP=1, THL=1, HI=64, HJ=64,
-                  H2=128, OA=128, YI=128),
+                     XV6=128, S1=128, T1=128, T5=128, SA=128, SM=128, GS=128, WL=128, WQ=256, NEG=16, ID=128, IDM=128, M1=128,
+                     NL=128, LM=128, R3=8, WC=8, WA=40, WP=40, WW=40, WK=16, VP=144, VW=144, ON=128, C8=32, JN=256),
+    "float16": dict(IDN=128, R3H=8, T3=128, HQ=64),
+    "int32": dict(CURI=64, STI=64, PC=256, PCL=256, KC=256, KCL=256, OWN=256, IP=1, IQ=3, WI=1, THP=1, THL=1, H2=128, OA=128, YI=128),
     "uint16": dict(IXP=192, IX=192, SL=448, ST=64, FL=64, XL=8, HL=64, OL=64, SCL=8),
     "float32": dict(KW=DUP + TB, KB=256, KF=256, KN=384, D0=64, S2=128, MD=128, MB=128, SJ=16, col=40, I16=128, IG=128, IC=144,
                     IDI=128, J2=256, N0=4, BN=4, BK=4, PF=1, RB=1, CURF=64, CURW=1024, YPC=1024, OB=128, YF1=64, YF2=64),
@@ -37,7 +42,6 @@ LOADS = ["l_cur", "l_start", "l_prev", "l_kid", "l_x", "l_z", "l_z2", "l_env", "
 TAGS = ("e", "c0", "c1", "c2", "i0a", "i0b", "i1a", "i1b", "i2a", "i2b")
 SEMAPHORES = ["c_v", "c_s", "c_t", "c_g", "d_p", "d_k", "d_k2", "d_cw", "d_ct", "d_m1", "d_m2", "d_e1", "d_e2", "o_yp0", "o_yp1",
               "o_yp2", "o_yr0", "o_yr1", "o_yk0", "o_yk1"] + LOADS + [a + b for a in ("r_", "q_") for b in TAGS]
-KIB = dict(l_prev=64, l_x=512, l_z=256, l_z2=256, l_env=256, l_rs=256, d_ct=448, d_m1=256, d_e1=256, d_m2=136, d_e2=136, l_w=1, l_th=1)
 ORDER = []
 
 
@@ -83,8 +87,8 @@ def rank_program(g, core, T, topo):
         calls.append(dict(q=q, fn=fn, reads=reads, writes=writes, sem=sem, group=group, deps=deps, turn=now[0], cost=cost,
                           move=move, banks={r[0] for r in reads + writes if r[0] in PSUM}))
 
-    def dma(q, sem, out, in_, reads, writes, n=1):
-        op(q, lambda: queues[q].dma_start(out, in_), reads, writes, 0.05, sem, 16 * n, (LOCAL, KIB.get(sem, 32) << 10))
+    def dma(q, sem, out, in_, reads, writes, n=1, **kw):
+        op(q, lambda: queues[q].dma_start(out, in_, **kw), reads, writes, 0.05, sem, 16 * n, (LOCAL, KIB.get(sem, 32) << 10))
 
     def send(tag, dst, dlo, src, lo, hi):
         def fn():
@@ -238,6 +242,9 @@ def rank_program(g, core, T, topo):
         kw = {} if out[1][0][0] in BUFS["int32"] else dict(allow_small_or_imprecise_dtypes=True)
         op("g", lambda: g.iota(out[0], pattern, base, cm, **kw), [], out[1], 0.13 + 2 * out[2] * CYCLE)
 
+    def diagonal(out, in_):
+        op("g", lambda: g.affine_select(T[out][:], T[in_][:], [[-1, 128]], A.is_equal, 0.0, 0, 1), [in_], [out], 0.4)
+
     def mms(parts, start=True, stop=True):
         def fn():
             r = None
@@ -280,7 +287,6 @@ def rank_program(g, core, T, topo):
     dma("y", "l_cur", T.CURI[:], T.cur[:, :], [], ["CURI"])
     dma("y", "l_start", T.STI[:], T.start[:, :], [], ["STI"])
     dma("y", "l_x", T.XW[:], T.x[:, :], [], ["XW"])
-    dma("s", "l_z", T.ZW[:, 0:1024], T.z[:, :], [], [("ZW", 0, 1024)])
 
     iota(S("IP"), [[0, 1]], 0, 1)
     iota(S("I16"), [[0, 8], [1, 16]])
@@ -288,7 +294,6 @@ def rank_program(g, core, T, topo):
     iota(S("J2"), [[1, 256]])
     iota(S("THP"), [[0, 1]])
     iota(S("OWN"), [[1, 256]], 0, 256)
-    iota(S("WK"), [[0, 384]])
     iota(S("D0"), [[0, 32], [66000 - int(8 * SLOPE) - DUP, 2]], -66000)
     iota(S("IDI"), [[1, 128]], 0, -1)
     iota(S("IG"), [[1, 8], [0, 16]])
@@ -296,12 +301,15 @@ def rank_program(g, core, T, topo):
         iota(S(b), [[0, 40]])
     for lo, hi in ((1024, DUP), (DUP + 1024, DUP + TB)):
         iota(S("ZW", lo, hi), [[0, hi - lo]])
+    iota(S("ON"), [[0, 128]], 1)
+    iota(S("C8"), [[0, 32]], 8)
     iota(S("IC"), [[1, 144]], -15)
     iota(S("PF"), [[0, 1]], 0, 1)
     iota(S("CURW"), [[0, 1024]])
 
     fill(S("ZB"), 0.0)
-    fill(S("PW"), 0.0)
+    for lo in (0, 1024):
+        act(S("PW", lo, lo + 1024), S("ZB"))
     for i, (n, o) in enumerate(((15, A.bitwise_and), (4, A.arith_shift_right), (31, A.bitwise_and))):
         ts(S("IQ", i, i + 1), S("IP"), n, o)
     cp(col(3), S("IQ"))
@@ -317,8 +325,8 @@ def rank_program(g, core, T, topo):
         for t in range(4):
             n = 128 if lo and t == 3 else 256
             act(S("KW", lo + 1024 + 256 * t, lo + 1024 + 256 * t + n), S("J2", 0, n), F.Identity, lt4, S("BN", t, t + 1))
-
     ts(part("OWN", 64, 96), part("OWN", 64, 96), 1023, A.bitwise_and)
+
     for src, mid, dst in (("PC", "PCL", "PB"), ("KC", "KCL", "KB")):
         for lo, bits in ((0, 255), (64, 2047 - 255)):
             ts(part(mid, lo, lo + 64), part(src, lo, lo + 64, False), bits, A.bitwise_and)
@@ -330,14 +338,12 @@ def rank_program(g, core, T, topo):
     for r in range(2):
         dma("y", "d_p", rows("PW", r, 0, 2048)[0], T.PB[64 * r:64 * r + 64, :], ["PB"], rows("PW", r, 0, 2048)[1], 2)
     for sem, lo in (("d_k", 0), ("d_k2", DUP)):
-        for r, (b, i) in enumerate((("KB", 0), ("KB", 1), ("KB", 2), ("KB", 3), ("KF", 0), ("KF", 1), ("KF", 2))):
-            r = (0, 1, 4, 5, 2, 3, 6)[r]
+        for r, b, i in ((0, "KB", 0), (1, "KB", 1), (4, "KB", 2), (5, "KB", 3), (2, "KF", 0), (3, "KF", 1), (6, "KF", 2)):
             dma("y", sem, rows("KW", r, lo, lo + 1024)[0], T[b][32 * i:32 * i + 32, :], [b], rows("KW", r, lo, lo + 1024)[1], 7)
-    dma("y", "l_z2", T.ZW[:, DUP:DUP + 1024], T.z[:, :], [], [("ZW", DUP, DUP + 1024)])
+        dma("y", "l_z2" if lo else "l_z", T.ZW[:, lo:lo + 1024], T.z[:, :], [], [("ZW", lo, lo + 1024)])
     dma("y", "l_w", T.WI[:], T.w[:, :], [], ["WI"])
     for r in (7, 8):
         dma("y", "l_th", rows("THP", r, 0, 1)[0], T.th[:, :], [], rows("THP", r, 0, 1)[1], 2)
-    dma("y", "l_env", T.EM[:, 0:1024], T.env[:, :], [], [("EM", 0, 1024)])
     for lo in (0, DUP):
         dma("y", "l_rs", T.RW[:, lo:lo + 1024], T.rs[:, :], [], [("RW", lo, lo + 1024)], 2)
 
@@ -351,15 +357,13 @@ def rank_program(g, core, T, topo):
     ts(S("WC"), S("R3"), -SLOPE, A.mult)
     for b in ("HX", "HS"):
         cp((T[b][:], [b], 280, 2), S("ZB", 0, 280))
-    for i in range(4):
-        ts(S("WK", 98 * i + 1, 96 * i + 64, 8), S("R3"), wk0s, A.mult)
-        ts(S("WK", 97 * i + 64, 96 * i + 96, 4), S("R3"), wk1, A.mult)
+    ts(S("WK", 0, 8), S("R3"), wk0s, A.mult)
+    ts(S("WK", 8, 16), S("R3"), wk1, A.mult)
     ts(S("GS"), S("IG"), p4, A.is_equal)
     ts(S("SJ"), S("MD", 0, 16), -2.0, A.mult, 1.0, A.add)
     fill(S("CT", 0, 1), -1.0)
     ts(S("WL"), S("GS"), e[6], A.mult, -1024.0, A.mult)
 
-    at(-2.9)
     for b in range(11):
         at(-2.9 if b < 8 else b - 7.75)
         ts(S("CT", 1 << b, 2 << b), S("CT", 0, 1 << b), S("SJ", b, b + 1), A.mult)
@@ -370,12 +374,13 @@ def rank_program(g, core, T, topo):
     at(1.25)
     p16 = colop(p4, 16.0, A.mult)
     wf = colop(S("WI"), 1.0, A.mult)
-    ts(S("WA", 3, 35, 4), S("R3"), 97.0, A.mult)
-    ts(S("WW", 3, 35, 4), S("R3"), wf, A.mult)
+    ts(S("WA", 3, 35, 4), S("R3"), 97.0 / 1024, A.mult)
+    ts(S("WW", 3, 35, 4), S("R3"), wf, A.mult, 1.0 / 1024, A.mult)
     at(2.25)
     dma("y", "d_ct", T.CT[:, DUP:DUP + 1792], T.CT[:, 0:1792], [("CT", 0, 1792)], [("CT", DUP, DUP + 1792)])
     at(3.25)
-    ts(S("EM", 0, 1024), S("EM", 0, 1024), -256.0, A.add)
+    iota(S("EM", 0, 1024), [[0, 1024]], -256)
+    dma("g", "l_env", T.EM[:, 0:1024], T.env[:, :], [("EM", 0, 1024)], [("EM", 0, 1024)], accum_op=A.add)
     send("e", "EP", 0, "EM", 0, 1024)
     for b in ("EM", "EP"):
         for i, n in ((1, 1024), (2, EW - 2048)):
@@ -384,7 +389,9 @@ def rank_program(g, core, T, topo):
     for lo, hi in ((1024, DUP), (DUP + 1024, DUP + 1792)):
         iota(S("RW", lo, hi), [[0, hi - lo]])
     iota(S("JN"), [[0, 2], [1, 128]])
-    iota(S("ON"), [[0, 128]], 1)
+    iota(S("M1"), [[0, 128]], -1)
+    diagonal("ID", "ON")
+    diagonal("IDM", "M1")
     iota(S("NEG"), [[0, 16]], -8192)
     iota(S("NL"), [[0, 128]], 0, -1)
     iota(S("RB"), [[0, 1]], -11 * 4096, -32)
@@ -406,10 +413,8 @@ def rank_program(g, core, T, topo):
     wq = colop(wc, wb, A.subtract)
     ts(S("WQ", 128, 256), S("GS"), wd, A.mult)
     ts(S("BK"), S("N0"), m25, A.mult, mk, A.add)
-    ts(S("ID"), S("IDI"), 0.0, A.is_equal)
     ts(S("WQ", 0, 128), S("GS"), wq, A.mult)
     at(8.25)
-    ts(S("IDM"), S("IDI"), 0.0, A.is_equal, -1.0, A.mult)
     ts(S("LM"), S("MD"), S("PF"), A.mult)
     ts(S("MB"), S("MD"), -1e9, A.mult, 1e9, A.add)
     cp(S("R3H"), S("R3"))
@@ -422,8 +427,8 @@ def rank_program(g, core, T, topo):
     def blocks(src, h):
         return [S(src, 512 * h + i, 512 * h + 512, 4) for i in range(4)]
 
-    def words(bank, c0, src, h, wt):
-        mms([(S(bank, c0, c0 + 32), b, S(wt, 3 - i, 35 - i)) for i, b in enumerate(blocks(src, h))])
+    def words(bank, c0, src, h, wt, start=True, stop=True):
+        mms([(S(bank, c0, c0 + 32), b, S(wt, 3 - i, 35 - i)) for i, b in enumerate(blocks(src, h))], start, stop)
 
     def slots(buf, h):
         return T[buf][:, 35 * h + 3:35 * h + 35:4, :], [(buf, 35 * h, 35 * h + 35)], 32, 2
@@ -439,51 +444,52 @@ def rank_program(g, core, T, topo):
     def step(t, h, k):
         n, lo, hi = ROUND * t + 2 * k + h, 512 * h, 512 * h + 512
         top, lst = (DUP + TB, "FL") if k else (1024, "ST")
-        at(n - 0.9 if k or not t else n - 1.04 - 0.85 * h)
+        at(n + TN["kg"] if k or not t else n + TN["kg0"] + TN["kg1"] * h)
         gx("s", "KG", 0, "KW", 0, top, lst, 0, lo, hi)
         at(n)
-        if PRE and t and not k:
+        if t and not k:
             tt(S("BT", lo, hi), S("PG", lo, hi), S("pD%d" % h), A.is_le)
         else:
             tt(S("BT", lo, hi), G("ZW", 0, top, lst, lo, hi), S("XA%d" % (t % 2), 1024 * k + lo, 1024 * k + hi), A.is_le)
-        mms([(S(W[h], 0, 96), b, S("WK", 96 * i, 96 * i + 96)) for i, b in enumerate(blocks("KG", h))], True, False)
+            at(n + TN["mm"])
+        mms([(S(W[h], 2 * i + 1, 128, 8), b, S("WK")) for i, b in enumerate(blocks("KG", h))], True, False)
         mms([(S(W[h], 2 * i, 64, 8), b, S("WC")) for i, b in enumerate(blocks("BT", h))], False, True)
         if t < 2 and h == 0:
             mms([(S("pL", 0, 128), S("KG", 0, 128), S("WL"))], k == 0, k == 5)
-        at(n + 0.5)
+        at(n + TN["scan"])
         o = S("S2", 64 * h, 64 * h + 64)
         op("v", lambda: g.vector.tensor_tensor_scan(o[0], T.D0[:], T[W[h]][:, 0:64], 0.0, A.subtract, A.max),
            ["D0", (W[h], 0, 64)], o[1], cycles(64))
-        at(n + 0.6)
-        tt(slots("HS", h), S(W[h], 64, 96), S("S2", 64 * h + 1, 64 * h + 64, 2), A.min)
-        back(W[h], 96, "HS", h)
-        at(n + (0.8 if (h, k) == (1, 5) else 1.1))
-        ts(S("FL", 32 * h, 32 * h + 32), S(W[h], 96, 128), -1.0, A.mult, float(DUP), A.add)
+        at(n + TN["tt"])
+        tt(slots("HS", h), S(W[h], 65, 128, 2), S("S2", 64 * h + 1, 64 * h + 64, 2), A.min)
+        back(W[h], 128, "HS", h)
+        at(n + (TN["flb"] if (h, k) == (1, 5) else TN["fl"]))
+        ts(S("FL", 32 * h, 32 * h + 32), S(W[h], 128, 160), -1.0, A.mult, float(DUP), A.add)
 
     def hsum(t, h, n, n2):
         lo, hi, bank = 32 * h, 32 * h + 32, "pD%d" % (2 + h)
         at(n)
-        words(bank, 0, "XA%d" % (t % 2), h, "WW")
-        cp(S("HI", lo, hi), S(bank, 0, 32))
+        mms([(S(bank, 0, 32), S("ON"), S("C8"))], True, False)
+        for src in ("SP", "TT") if t else ("XA0",):
+            words(bank, 0, src, h, "WW", False, src != "SP")
+        ts(S("HQ", lo, hi), S(bank, 0, 32), 0.5005, A.add)
         at(n + 0.03)
-        ts(S("HJ", lo, hi), S("HI", lo, hi), 1023, A.bitwise_and)
-        at(n + 0.06)
-        ts(slots("HH", h), S("HJ", lo, hi), -1024.0, A.add)
+        tt(slots("HH", h), S(bank, 0, 32), S("HQ", lo, hi), A.subtract)
         if t:
             back(bank, 32, "HH", h)
             at(n2)
-            ts(S("HL", lo, hi), S(bank, 32, 64), -1.0, A.mult, 1024.0, A.add)
+            ts(S("HL", lo, hi), S(bank, 32, 64), -1024.0, A.mult, 1024.0, A.add)
 
     def outcome(t, h):
         n, lo, hi, x0 = ROUND * t + 11 + h, 512 * h, 512 * h + 512, 64 * t + 32 * h
-        at(n + 0.2)
+        at(n + TN["r" + "ab"[h]])
         tt(S("BT", lo, hi), G("RW", 0, DUP + 1792, "FL", lo, hi), S("XA%d" % (t % 2), lo, hi), A.is_gt)
-        words(W[h], 128, "BT", h, "WA")
-        at(n + (0.4 if h else 0.7))
-        tt(slots("HX", h), S(W[h], 128, 160), slots("HH", h), A.add)
-        back(W[h], 160, "HX", h)
-        at(n + (0.5 if h else 1.15))
-        ts(S("IX", x0, x0 + 32), S(W[h], 160, 192), -1.0, A.mult, 1024.0, A.add)
+        words(W[h], 160, "BT", h, "WA")
+        at(n + TN["hx" + "ab"[h]])
+        tt(slots("HX", h), S(W[h], 160, 192), slots("HH", h), A.add)
+        back(W[h], 192, "HX", h)
+        at(n + TN["ix" + "ab"[h]])
+        ts(S("IX", x0, x0 + 32), S(W[h], 192, 224), -1024.0, A.mult, 1024.0, A.add)
         send("i%d" % t + "ab"[h], "IXP", x0, "IX", x0, x0 + 32)
 
     def band(name, a):
@@ -496,54 +502,59 @@ def rank_program(g, core, T, topo):
         act(S("BO"), G("CT", 0, DUP + 1792, "FL", 0, 128), F.Identity, co)
         act(S("RN"), G("RW", 0, DUP + 1792, "FL", 0, 128))
         act(S("KG6"), G("KW", 0, DUP + TB, "FL", 0, 128))
-        at(n + 11.9)
+        at(n + TN["va"])
         mms([(S("pM", 0, 256), S("KG6"), S("WQ")), (S("pM", 128, 256), S("ID"), S("NL"))], True, False)
         for a in range(4):
             bank = "pD%d" % a
             at(n + 9.06 + a // 2)
             mms([(S(bank, 0, 256), band("ON", a), band("JN", a))], True, False)
-            at(n + (11.15 if a < 2 else 11.8))
+            at(n + TN["d0" if a < 2 else "d2"])
             mms([(S(bank, 128 * i, 128 * i + 128), band(b, a), band(b, a)) for i, b in enumerate(("BE", "BO"))], False, True)
-            at(n + 11.85)
+            at(n + TN["ee"])
             act(S("EE", 256 * a, 256 * a + 256), S(bank, 0, 256), F.Relu, bias=S("RB"))
-            at(n + (12.0 if a < 2 else 12.27))
+            at(n + TN["n0" if a < 2 else "n2"])
             mms([(S("pM", 16 * q, 16 * q + 16), S("EE", 128 * q, 128 * q + 128), S("NEG")) for q in (2 * a, 2 * a + 1)], False, False)
         if t < 2:
-            at(n + 11.75)
+            at(n + TN["t5"])
             tt(S("T5"), S("pL", 0, 128), S("MD"), A.mult)
-            at(n + 11.95)
+            at(n + TN["xm"])
             mms([(S("pL", 128, 136), S("LM"), S("R3")), (S("pL", 128, 136), S("T5"), S("R3"))])
-            at(n + 12.32)
+            at(n + TN["xl"])
             ts(S("XL"), S("pL", 128, 136), 6144.0, A.add)
             gx("s", "XV6", 0, xa, 0, XAW, "XL", 0, 0, 128)
-        at(n + 12.3)
+        at(n + TN["s1"])
         tt(S("S1"), G("EM", 0, EW, "IX", 1024 * t, 1024 * t + 128), S(xa, 0, 128), A.add)
-        at(n + 12.35)
+        at(n + TN["t1"])
         ts(S("T1"), S("S1"), 0.0, A.is_lt, 256.0, A.mult)
-        mms([(S("pL", 256, 384), S(i), S(b)) for i, b in (("IDM", "RN"), ("ID", "S1"), ("ID", "T1"))])
+        at(n + TN["rn"])
+        mms([(S("pL", 256, 384), S("IDM"), S("RN"))], True, False)
+        at(n + TN["pd"])
+        mms([(S("pL", 256, 384), S("ID"), S("S1"))], False, False)
+        mms([(S("pL", 256, 384), S("ID"), S("T1"))], False, True)
         act(S("DA"), S("pL", 256, 384), F.Abs)
-        at(n + 12.55)
+        at(n + TN["far"])
         mms([(S("pM", 0, 128), S("DA"), S("GS"))], False, True)
+        at(n + (13.9 if t < 2 else TN["ph"]))
         mms([(S("pL", 384, 512), S("ID"), S(b)) for b in ("RN", "S1", "T1")])
-        at(n + 12.7)
+        at(n + TN["sm"])
         tt(S("SM"), S("pM", 0, 128), S("MB"), A.is_ge)
-        at(n + 12.75)
+        at(n + TN["t3"])
         tt(S("T3"), S("pM", 128, 256), S("SM"), A.mult)
         mms([(S("pM", 256, 264), S("LM"), S("R3")), (S("pM", 256, 264), S("T3"), S("R3H"))])
-        at(n + 12.85)
+        at(n + TN["scl"])
         ts(S("SCL"), S("pM", 256, 264), 1792.0, A.add)
         for lo in (0, DUP) if t < 2 else (0,):
-            at(n + (14.2 if lo else 12.9))
+            at(n + TN["sk2" if lo else "sk"])
             scatter("KW", lo, S("KN", 128 * t, 128 * t + 128))
-            at(n + (15.3 if lo else 12.95))
+            at(n + TN["sz2" if lo else "sz"])
             if t < 2:
                 scatter("ZW", lo, S("XV6"))
-        at(n + (16.2 if t < 2 else 12.72))
+        at(n + TN["sa" if t < 2 else "sa2"])
         ts(S("SA"), S("pM", 0, 128), 0.0, A.is_ge)
-        at(n + (16.21 if t < 2 else 12.76))
+        at(now[0] + 0.01)
         mms([(S("pM", 384, 512), S("SA"), S("ID"))])
         ts(S("H2"), S("pL", 384, 512), 0.5, A.mult, -0.25, A.add)
-        at(n + (17.2 if t < 2 else 12.95))
+        at(n + TN["rw" if t < 2 else "rw2"])
         tt(S("RW", n0, n0 + 256, 2), S("pM", 384, 512), S("RN"), A.mult)
         tt(S("RW", n0 + 1, n0 + 256, 2), S("pM", 384, 512), S("H2"), A.mult)
         if t < 2:
@@ -555,9 +566,9 @@ def rank_program(g, core, T, topo):
 
     def arrive(t, h):
         n, lo, hi = ROUND * t, 512 * h, 512 * h + 512
-        at(n + (13.0 if h else ENVA))
+        at(n + TN["env" + "ab"[h]])
         tt(S("SP", lo, hi), G("EP", 0, EW, "IXP", 1024 * t + lo, 1024 * t + hi), S("CP", 1024 * t + lo, 1024 * t + hi), A.add)
-        at(n + (13.1 if h else 12.87))
+        at(n + TN["tt" + "ab"[h]])
         ts(S("TT", lo, hi), S("SP", lo, hi), 0.0, A.is_lt, 256.0, A.mult)
 
     def preds_out(t, bank):
@@ -572,40 +583,40 @@ def rank_program(g, core, T, topo):
         cp(S("OA", 0, 64), S("HL"))
         ts(S("OB", 0, 64), S("HL"), 64.0, A.mult)
         ts(S("OA", 64, 128), S("OA", 0, 64), 4, A.arith_shift_right)
-        at(ROUND + 5.2)
+        at(TN["ol"])
         ts(S("OB", 64, 128), S("OA", 64, 128), -1023.0, A.mult)
         tt(S("OB", 0, 64), S("OB", 0, 64), S("OB", 64, 128), A.add)
         cp(S("OL"), S("OB", 0, 64))
         for h in range(2):
-            at(ROUND + 9.3 + h)
+            at(TN["ypc"] + h)
             gx("s", "YPC", 0, "CURW", 0, 1024, "OL", 0, 512 * h, 512 * h + 512)
         dma("y", "o_yp0", T.yp[:, 0:1024], T.YPC[0:128:16, :], ["YPC"], [])
 
     def items(dst, k, h, src, s0, s1, lst, l0, n, xv):
         lo = 512 * h
-        at(n + 0.2)
+        at(n + TN["xv"])
         gx("v", dst, 1024 * k, src, s0, s1, lst, l0, lo, lo + xv)
-        at(n + 0.3)
+        at(n + TN["xs"])
         gx("s", dst, 1024 * k, src, s0, s1, lst, l0, lo + xv, lo + 512)
 
     for k in range(6):
         for h in range(2):
             n = 2 * k + h - 2
-            items("XA0", k, h, "XW", 0, 2048, "SL", 1024 * k, n if k else -5, XV0[n] if k else 0)
+            items("XA0", k, h, "XW", 0, 2048, "SL", 1024 * k, n if k else -5, TN["xv0"] if k else 0)
             if k < 5:
                 bank = "pD%d" % h
-                at(n + 0.2 if k else -3)
+                at(n + TN["pg"] if k else -3)
                 gx("s", "PG", 0, "PW", 0, 2048, "SL", 1024 * k, 512 * h, 512 * h + 512)
-                at(n + 1.06 if k else -0.5 + 0.51 * h)
+                at(n + TN["pw"] if k else -0.5 + 0.51 * h)
                 words(bank, 0, "PG", h, "WP")
-                at(n + 1.4 if k else 0.06 + 0.2 * h)
+                at(n + TN["px"] if k else 0.06 + 0.2 * h)
                 cp(slots("HX", h), S(bank, 0, 32))
                 back(bank, 32, "HX", h)
-                at(n + 1.65 if k else 0.1 + 0.5 * h)
+                at(n + TN["pl"] if k else 0.1 + 0.5 * h)
                 ts(S("SL", 64 * k + 64 + 32 * h, 64 * k + 96 + 32 * h), S(bank, 32, 64), -1.0, A.mult)
     at(8.3)
     gx("s", "PG", 0, "PW", 0, 2048, "SL", 5120, 0, 128)
-    at(9.07)
+    at(TN["w5"])
     wrap("pM", "VP", "PG", 8, range(16), True, True)
     at(9.65)
     cp(S("SL", 384, 392), S("pM", 0, 8))
@@ -617,25 +628,25 @@ def rank_program(g, core, T, topo):
     for t in range(3):
         xo, xa, n = "XA%d" % ((t - 1) % 2), "XA%d" % (t % 2), ROUND * t
         for h in range(2):
-            lo, hi = 512 * h, 512 * h + 512
+            lo, hi, x = 512 * h, 512 * h + 512, "ab"[h]
             if t:
-                if PRE:
-                    at(n - 1.03 + 0.1 * h)
-                    gx("s", "PG", 0, "ZW", 0, 1024, "ST", 0, lo, hi)
+                at(n + TN["pg" + x])
+                gx("s", "PG", 0, "ZW", 0, 1024, "ST", 0, lo, hi)
                 arrive(t - 1, h)
-                at(n - (0.95 if h else 1.2))
+                at(n + TN["v1" + x])
                 mms([(S("pD%d" % h), S("ID"), S("SP", lo, hi))], True, False)
-                at(n - (0.89 if h else 1.12))
+                at(n + TN["v2" + x])
                 mms([(S("pD%d" % h), S("ID"), S("TT", lo, hi))], False, True)
+                at(n + TN["ev" + x])
                 act(S(xa, lo, hi), S("pD%d" % h))
-                hsum(t, h, n + 1.12 if h else n - 0.8, n + (1.7 if h else 0.1))
+                hsum(t, h, n + TN["h" + x], n + TN["hl" + x])
                 for k in range(1, 6):
-                    items(xa, k, h, xo, 1024 * k - 1024, 1024 * k, "HL", 0, n + 2 * k + h - (2 if k > 1 else 2.2 - 0.7 * h),
-                          XV[1] if 2 < k else 0)
+                    items(xa, k, h, xo, 1024 * k - 1024, 1024 * k, "HL", 0, n + 2 * k + h - (2 if k > 1 else TN["x1"] - 0.7 * h),
+                          TN["xv1"] if 2 < k else 0)
             else:
                 hsum(t, h, 4.06 + h, 0)
         if t:
-            at(n)
+            at(n + TN["evb"])
             send("c%d" % t, "CP", 1024 * t, xa, 0, 1024)
         if t == 1:
             at(n + 10.3)
@@ -643,12 +654,12 @@ def rank_program(g, core, T, topo):
             first_preds()
         if t == 2:
             for j in range(2):
-                at(n + 4.06 + j)
+                at(n + TN["p1"] + j)
                 wrap("pM", "VW", xa, 64, range(8 * j, 8 * j + 8), j == 0, j == 1, True)
-            at(n + 6.2)
+            at(n + TN["p1"] + 2.14)
             preds_out(1, "pM")
-        for k in range(6):
-            for h in range(2):
+        for h in range(2):
+            for k in range(6):
                 step(t, h, k)
         for h in range(2):
             outcome(t, h)

@@ -6,43 +6,46 @@ DUP = 2048
 TB = 1920
 XAW = 6272
 EW = 2592
-SLOPE = 3968.0
-ROUND = 14
-CYCLE, GATHER, GATHER2, SCATTER, WAKE, AHEAD = 0.87e-3, 1.56, 1.8, 3.8, 0.06, 0.15
-LOCAL, REMOTE = (1.7, 220e3, 0.15), (2.0, 45e3, 0.3)
-KIB = dict(l_prev=64, l_x=512, l_z=256, l_z2=256, l_env=256, l_rs=256, d_ct=448, d_m1=256, d_e1=256, d_m2=136, d_e2=136, l_w=1, l_th=1)
-TN = dict(
-    kg=-1.53, mm=-0.57, scan=0.46, tt=0.5, fl=1.1, flb=0.66, xv=0.2, xs=0.3, pg=-0.93, pw=1.06, px=1.4, pl=1.65,
-    ra=0.06, hxa=0.7, ixa=1.19, rb=0.2, hxb=0.4, ixb=0.5,
-    d0=11.75, d2=11.28, ee=11.85, n0=12.0, n2=12.47, va=11.9, t5=11.75, xm=11.95, xl=12.25, rn=11.96, s1=12.3, t1=12.35, pd=12.35,
-    far=12.55, ph=12.6, sm=12.7, t3=12.75, scl=12.85, sk=12.9, sz=12.73, sk2=13.2, sz2=15.3, sa=16.2, rw=17.2, sa2=13.03, rw2=13.49,
-    enva=12.6, tta=12.88, envb=13.0, ttb=12.79, pga=-1.03, pgb=-0.93, v1a=-1.2, v2a=-1.12, v1b=-1.93, v2b=-1.51, eva=3.5, evb=4.5,
-    ha=-0.8, hla=0.1, hb=1.12, hlb=1.7, kg0=-1.04, kg1=0.3, x1=2.2,
-    w5=9.07, ol=40.2, ypc=40.4, p1=10.5,
-    xv0=224, xv1=224)
+UNIT = 1.0 / 512
+HALF = 0.5 - UNIT / 2
+LEVELS = (320, 704, 1088, 1472)
+CYCLE, GATHER, GATHER2, SCATTER, WAKE = 0.87e-3, 1.4, 2.0, 3.8, 0.08
+LOCAL, REMOTE = (1.7, 220e3, 0.15), (2.0, 35e3, 0.3)
+CASES = ((1.1, 0.09, 1.0), (1.6, 0.065, 1.3))
+TRIES, MEAN, SEED, AIM, HEAT = 35000, 1.0, 11, 0.5, 0.25
+KIB = dict(l_prev=64, l_x=256, l_z=256, l_env=256, l_rs=256, d_ct=448, d_m1=256, d_e1=256, d_m2=136, d_e2=136, l_w=1, l_th=1)
+P = dict(cut=256, c1=192, zs0=0, zs1=160, last=13)
+PIN = dict(t0=7.37, p0=1.28, p=1.1, gap=6.99, lag0=1.61, lag=3.27, end=84.1, setup=35.73, leaves=2.13, codes=19.16, e=9, c=3.0,
+           lead=2.84, two0=0.76, two=1.15, sh=0.85, ra0=0, ra1=0.21, rb0=-0.11, rb1=1.07, senda=1.56, sendb=1.74, s1=1.98,
+           scl=6.02, sc1=5.24, sc2=9.51, pz=4.96, env=5.67, tt=5.97, hl=7.95, cu=8.64)
 
 BUFS = {
-    "bfloat16": dict(XW=2048, PW=2048, ZW=DUP + TB, RW=DUP + 1792, CT=DUP + 1792, EM=EW, EP=EW, CP=3072, XA0=XAW, XA1=XAW, BT=1024,
-                     KG=1024, PG=1024, SP=1024, TT=1024, ZB=1024, EE=1024, PB=256, KG6=128, BE=128, BO=128, RN=128, DA=128,
-                     XV6=128, S1=128, T1=128, T5=128, SA=128, SM=128, GS=128, WL=128, WQ=256, NEG=16, ID=128, IDM=128, M1=128,
-                     NL=128, LM=128, R3=8, WC=8, WA=40, WP=40, WW=40, WK=16, VP=144, VW=144, ON=128, C8=32, JN=256),
-    "float16": dict(IDN=128, R3H=8, T3=128, HQ=64),
-    "int32": dict(CURI=64, STI=64, PC=256, PCL=256, KC=256, KCL=256, OWN=256, IP=1, IQ=3, WI=1, THP=1, THL=1, H2=128, OA=128, YI=128),
-    "uint16": dict(IXP=192, IX=192, SL=448, ST=64, FL=64, XL=8, HL=64, OL=64, SCL=8),
-    "float32": dict(KW=DUP + TB, KB=256, KF=256, KN=384, D0=64, S2=128, MD=128, MB=128, SJ=16, col=40, I16=128, IG=128, IC=144,
-                    IDI=128, J2=256, N0=4, BN=4, BK=4, PF=1, RB=1, CURF=64, CURW=1024, YPC=1024, OB=128, YF1=64, YF2=64),
+    "bfloat16": dict(XW=2048, PW=2048, ZL=1024, RW=DUP + 1792, CT=DUP + 1792, EM=EW, EP=EW, CP=3072, CU=3072, XA0=XAW, XA1=XAW,
+                     BT=1024, PG=1024, SP=1024, TT=1024, EE=1024, PB=256, PL=256, BE=128, BO=128, RN=128, DA=128,
+                     S1=128, T1=128, T5=256, SA=128, SM=128, GS=128, TW=256, NEG=16, ID=128, IDM=128, IDS=128, IDQ=128, M1=128,
+                     NL=128, LM=128, R3=8, R3N=16, WA=40, WP=40, WW=112, VP=144, VW=288, ON=128, C8=32, C96=96, JN=256),
+    "float16": dict(J=1024, J6=128, QA=256, QB=256, W3=106, WL=128, WQ=256, CL=128, IDN=128, R3H=8, T3=128, HQ=64, HS=800, HH=260,
+                    M15=128, M12=128, M63=128),
+    "int32": dict(CURI=64, STI=64, PC=256, KC=256, IP=1, IQ=7, WI=1, THP=1, THL=1, H2=128, YI=128),
+    "uint16": dict(IXP=192, IX=192, SL=448, ST=64, FL=64, XL=8, HL=64, HM=64, OL=64, SCL=8),
+    "float32": dict(ZK=DUP + TB, KO=DUP, PZ=1024, KF=256, OWN=256, KN=256, KM=384, XV6=128, D0=96, MD=256, MB=128, SJ=16, col=64,
+                    I16=128, IG=128, IC=144, SG=3, SC=3, B1=3, B3=3, B4=3, PF=1, RB=1, CURF=64, CURW=1024, YPC=1024,
+                    YF1=64, YF2=64),
 }
 PSUM = ("pA", "pB", "pL", "pM", "pD0", "pD1", "pD2", "pD3")
 SCRATCH = {n: ("sbuf", [128, w], d) for d, b in BUFS.items() for n, w in b.items()}
-for _n in ("HS", "HH", "HX"):
-    SCRATCH[_n] = ("sbuf", [128, 70, 4], "float16")
+SCRATCH["HX"] = ("sbuf", [128, 196, 4], "float16")
+for _n in ("ZA", "ZC"):
+    SCRATCH[_n] = ("sbuf", [128, 32, 16], "float16")
+SCRATCH["CV"] = ("sbuf", [128, 16, 16], "bfloat16")
 for _n in PSUM:
     SCRATCH[_n] = ("psum", [128, 512], "float32")
-LOADS = ["l_cur", "l_start", "l_prev", "l_kid", "l_x", "l_z", "l_z2", "l_env", "l_w", "l_th", "l_rs"]
+LOADS = ["l_cur", "l_start", "l_prev", "l_kid", "l_x", "l_z", "l_env", "l_w", "l_th", "l_rs"]
 TAGS = ("e", "c0", "c1", "c2", "i0a", "i0b", "i1a", "i1b", "i2a", "i2b")
-SEMAPHORES = ["c_v", "c_s", "c_t", "c_g", "d_p", "d_k", "d_k2", "d_cw", "d_ct", "d_m1", "d_m2", "d_e1", "d_e2", "o_yp0", "o_yp1",
+SEMAPHORES = ["c_v", "c_s", "c_t", "c_g", "d_p", "d_k", "d_cw", "d_ct", "d_m1", "d_m2", "d_e1", "d_e2", "o_yp0", "o_yp1",
               "o_yp2", "o_yr0", "o_yr1", "o_yk0", "o_yk1"] + LOADS + [a + b for a in ("r_", "q_") for b in TAGS]
 ORDER = []
+EST = []
 
 
 def rank_program(g, core, T, topo):
@@ -55,10 +58,19 @@ def rank_program(g, core, T, topo):
 
     calls = []
     seen = {}
-    now = [-100.0]
 
-    def at(turn):
-        now[0] = turn
+    def when(t, k, h):
+        if t == 0:
+            return PIN["t0"] + 2 * PIN["p0"] * k + PIN["lag0"] * h
+        return PIN["t0"] + 12 * PIN["p0"] + PIN["gap"] * t + PIN["p"] * (12 * t - 12 + 2 * k) + PIN["lag"] * h
+
+    def due(time):
+        calls[-1]["pin"] = time
+
+    def follow(*ids):
+        calls[-1]["deps"] |= set(ids)
+        calls[-1]["soft"] |= set(ids)
+        return len(calls) - 1
 
     def meets(r, s):
         if r[1] >= s[2] or s[1] >= r[2]:
@@ -70,7 +82,7 @@ def rank_program(g, core, T, topo):
             r = (r,)
         return tuple(r) + (0, 1 << 20, None)[len(r) - 1:]
 
-    def op(q, fn, reads, writes, cost, sem=None, group=None, move=None):
+    def op(q, fn, reads, writes, cost, sem=None, group=None, move=None, picks=0):
         reads, writes = [spec(r) for r in reads], [spec(r) for r in writes]
         me, deps = len(calls), set()
         for wr, regs in ((False, reads), (True, writes)):
@@ -84,57 +96,179 @@ def rank_program(g, core, T, topo):
                 if wr:
                     h[:] = [x for x in h if not (r[3] is None and r[1] <= x[0][1] and x[0][2] <= r[2])]
                 h.append((r, wr, me))
-        calls.append(dict(q=q, fn=fn, reads=reads, writes=writes, sem=sem, group=group, deps=deps, turn=now[0], cost=cost,
-                          move=move, banks={r[0] for r in reads + writes if r[0] in PSUM}))
+        calls.append(dict(q=q, fn=fn, reads=reads, writes=writes, sem=sem, group=group, deps=deps, soft=set(), cost=cost,
+                          picks=picks, pin=PIN["end"], move=move, banks={r[0] for r in reads + writes if r[0] in PSUM}))
 
     def dma(q, sem, out, in_, reads, writes, n=1, **kw):
-        op(q, lambda: queues[q].dma_start(out, in_, **kw), reads, writes, 0.05, sem, 16 * n, (LOCAL, KIB.get(sem, 32) << 10))
+        op(q, lambda: queues[q].dma_start(out, in_, **kw), reads, writes, 3.0 if q == "g" else 0.05, sem, 16 * n,
+           (LOCAL, KIB.get(sem, 32) << 10))
 
     def send(tag, dst, dlo, src, lo, hi):
         def fn():
             rid, pid = topo.addr(nxt, core)
             g.remote_dma(T[dst][:, dlo:dlo + hi - lo], T[src][:, lo:hi], T.sem["r_" + tag], T.sem["q_" + tag], pid, rid,
                          topo.mask(core, nxt))
-        op("g", fn, [(src, lo, hi)], [(dst, dlo, dlo + hi - lo)], 0.3, tag, None, (REMOTE, 256 * (hi - lo)))
+        op("g", fn, [(src, lo, hi)], [(dst, dlo, dlo + hi - lo)], 4.0 if tag == "e" else 0.3, tag, None, (REMOTE, 256 * (hi - lo)))
 
     def ordered():
         n = len(calls)
         for c in calls:
-            for d in list(c["deps"]):
+            for d in list(c["deps"] - c["soft"]):
                 if calls[d]["group"] and calls[d]["sem"] != c["sem"]:
                     c["deps"] |= {i for i in range(n) if calls[i]["sem"] == calls[d]["sem"]}
+        for c in calls:
+            if c["q"] == "t":
+                c["soft"] |= {d for d in c["deps"] if calls[d]["q"] == "t"}
         users = [[] for c in calls]
         for i, c in enumerate(calls):
             for d in c["deps"]:
                 users[d].append(i)
-        left, ready_at = [len(c["deps"]) for c in calls], [0.0] * n
-        free = {q: 0.0 for q in list(queues) + list(PSUM) + [LOCAL, REMOTE]}
-        ready = {q: [i for i in range(n) if not left[i] and calls[i]["q"] == q] for q in queues}
-        line = sorted((i for i in range(n) if calls[i]["q"] == "y"), key=lambda i: (-calls[i]["turn"], -i))
-        out, last = [], {}
-        while len(out) < n:
-            can = {q: [i for i in ready[q] if q != "y" or i == line[-1]] for q in queues}
-            t, q = min((max(free[e], min(ready_at[i] for i in can[e])), e) for e in queues if can[e])
-            i = min((j for j in can[q] if ready_at[j] <= t + AHEAD), key=lambda j: (calls[j]["turn"], j))
-            c = calls[i]
-            t = max([free[q], ready_at[i]] + [free[b] + (WAKE if last.get(b, q) != q else 0) for b in c["banks"]])
-            end = t + c["cost"]
-            for b in [q] + list(c["banks"]):
-                free[b], last[b] = end, q
+        span = [c["cost"] + WAKE + (0.06 if c["q"] == "t" else 0) for c in calls]
+        for i, c in enumerate(calls):
             if c["move"]:
                 way, nbytes = c["move"]
-                free[way] = max(free[way], t + way[0] / 2) + nbytes / way[1] + way[2]
-                end = free[way] + way[0] / 2
-            ready[q].remove(i)
-            if q == "y":
-                line.pop()
-            out.append((t, i))
-            for u in users[i]:
-                ready_at[u] = max(ready_at[u], end + WAKE + (0.03 if q == "t" else 0))
-                left[u] -= 1
-                if not left[u]:
-                    ready[calls[u]["q"]].append(u)
-        return [i for t, i in sorted(out)]
+                span[i] = way[0] + nbytes / way[1] + way[2] + WAKE
+        key, todo = [None] * n, list(range(n))
+        while todo:
+            i = todo[-1]
+            more = [u for u in users[i] if key[u] is None]
+            if more:
+                todo.extend(more)
+                continue
+            todo.pop()
+            key[i] = min([key[u] - (0.05 if i in calls[u]["soft"] else span[i]) for u in users[i]] + [calls[i]["pin"]])
+        deps = [[(b, b in c["soft"]) for b in sorted(c["deps"])] for c in calls]
+        holds = [[c["q"]] + sorted(c["banks"]) for c in calls]
+
+        def seek(line, x):
+            lo, hi = 0, len(line)
+            while lo < hi:
+                mid = (lo + hi) // 2
+                lo, hi = (mid + 1, hi) if line[mid] < x else (lo, mid)
+            return lo
+
+        def place(key):
+            left, start, end, busy = [len(d) for d in deps], [0.0] * n, [0.0] * n, {}
+            ready = sorted((-key[i], -i) for i in range(n) if not left[i])
+            while ready:
+                i = -ready.pop()[1]
+                c, q, moved = calls[i]["cost"], calls[i]["q"], True
+                t = max([start[b] + 0.05 if soft else end[b] for b, soft in deps[i]] + [0.0])
+                while moved:
+                    moved = False
+                    for r in holds[i]:
+                        line = busy.setdefault(r, [])
+                        for k in range(seek(line, (t - 4.5,)), len(line)):
+                            s, e, other = line[k]
+                            if s >= t + c + WAKE:
+                                break
+                            w = WAKE if other != q else 0.0
+                            if s < t + c + w - 1e-9 and t < e + w - 1e-9:
+                                t, moved = e + w, True
+                for r in holds[i]:
+                    busy[r].insert(seek(busy[r], (t,)), (t, t + c, q))
+                start[i], end[i] = t, t + span[i]
+                if calls[i]["move"]:
+                    way, nbytes = calls[i]["move"]
+                    a, d = t + way[0] / 2, nbytes / way[1] + way[2]
+                    for s, e in sorted(busy.get(way, ())):
+                        if s < a + d and a < e:
+                            a = e
+                    busy.setdefault(way, []).append((a, a + d))
+                    end[i] = a + d + way[0] / 2 + WAKE
+                for u in users[i]:
+                    left[u] -= 1
+                    if not left[u]:
+                        ready.insert(seek(ready, (-key[u], -u)), (-key[u], -u))
+            return start, end
+
+        start, end = place(key)
+        EST.append(max(end))
+        line = sorted(range(n), key=lambda i: (start[i], i))
+        names = sorted({r for h in holds for r in h} | {LOCAL, REMOTE}, key=str)
+        cases = []
+        for rate, wake, slow in CASES:
+            cases.append((wake, []))
+            for i, c in enumerate(calls):
+                mv, cost = c["move"], c["cost"] + c["picks"] * CYCLE * (rate - GATHER)
+                if mv:
+                    mv = (names.index(mv[0]), mv[0][0] / 2, mv[1] / mv[0][1] * (slow if mv[0] == REMOTE else 1) + mv[0][2])
+                cases[-1][1].append(([b for b, soft in deps[i] if not soft], [b for b, soft in deps[i] if soft], names.index(c["q"]),
+                                     [names.index(b) for b in holds[i][1:]], cost, cost + wake * (2 if c["q"] == "t" else 1), mv))
+
+        def run(line, wake, facts):
+            start, end, why = [0.0] * n, [0.0] * n, [-1] * n
+            free, user, by = [0.0] * len(names), [-1] * len(names), [-1] * len(names)
+            for i in line:
+                dep, soft, q, banks, c, sp, mv = facts[i]
+                t, w = free[q], user[q]
+                for b in dep:
+                    if end[b] > t:
+                        t, w = end[b], b
+                for b in banks:
+                    e = free[b] + wake if by[b] != q else free[b]
+                    if e > t:
+                        t, w = e, user[b]
+                for b in soft:
+                    if start[b] > t:
+                        t, w = start[b], b
+                start[i], why[i] = t, w
+                free[q], user[q] = t + c, i
+                for b in banks:
+                    free[b], user[b], by[b] = t + c, i, q
+                if mv:
+                    free[mv[0]] = max(free[mv[0]], t + mv[1]) + mv[2]
+                    end[i] = free[mv[0]] + mv[1] + wake
+                else:
+                    end[i] = t + sp
+            return max(end) + MEAN * sum(end) / n, end, why
+
+        def replay(line):
+            runs = [run(line, *case) for case in cases]
+            return sum(r[0] for r in runs) / len(runs), runs
+
+        now = replay(line)
+        best, x = (now[0], line), SEED
+        for k in range(TRIES):
+            end, why = now[1][k % len(cases)][1:]
+            x = (x * 1103515245 + 12345) % 2147483648
+            i, waits = end.index(max(end)) if x % 1024 < 1024 * AIM else (x >> 10) % n, []
+            while i >= 0:
+                if why[i] >= 0 and why[i] not in calls[i]["deps"]:
+                    waits.append(i)
+                i = why[i]
+            if not waits:
+                continue
+            x = (x * 1103515245 + 12345) % 2147483648
+            a = waits[(x >> 8) % len(waits)]
+            b = why[a]
+            lo, hi = line.index(b), line.index(a)
+            mid = line[lo:hi + 1]
+            if x >> 30:
+                group = {a}
+                for i in reversed(mid):
+                    if i in group:
+                        group.update(calls[i]["deps"])
+                if b in group:
+                    continue
+                mid = [i for i in mid if i in group] + [i for i in mid if i not in group]
+            else:
+                group = {b}
+                for i in mid:
+                    if i in group:
+                        group.update(users[i])
+                if a in group:
+                    continue
+                mid = [i for i in mid if i not in group] + [i for i in mid if i in group]
+            tried = line[:lo] + mid + line[hi + 1:]
+            new = replay(tried)
+            x = (x * 1103515245 + 12345) % 2147483648
+            if new[0] <= now[0] + HEAT * (1 - k / TRIES) * (x / 2147483648) ** 3:
+                now, line = new, tried
+                if new[0] < best[0]:
+                    best = (new[0], tried)
+        EST.extend(max(r[1]) for r in replay(best[1])[1])
+        return best[1]
 
     def issue():
         clock = {q: {} for q in queues}
@@ -201,7 +335,7 @@ def rank_program(g, core, T, topo):
     def G(name, lo, hi, lst, l0, l1):
         return T[name][:, lo:hi].indirect(T[lst][:, l0 // 16:l1 // 16]), [(name, lo, hi), (lst, l0 // 16, l1 // 16)], l1 - l0, "g"
 
-    def cycles(n, more=0.02):
+    def cycles(n, more=0.03):
         return more + max(64, n) * CYCLE
 
     def plain(out, in_):
@@ -217,7 +351,7 @@ def rank_program(g, core, T, topo):
             if op1 is None:
                 return g.vector.tensor_scalar(out[0], in0[0], s1[0], None, op0)
             return g.vector.tensor_scalar(out[0], in0[0], s1[0], s2[0], op0, op1)
-        op("v", fn, in0[1] + s1[1] + s2[1], out[1], plain(out, in0))
+        op("v", fn, in0[1] + s1[1] + s2[1], out[1], plain(out, in0), picks=in0[2] * (in0[3] == "g"))
 
     def tt(out, in0, in1, o):
         c = cycles(out[2] * GATHER2, 0.05) if in0[3] == "g" else cycles(out[2] * (1 if "p" in (in0[3], in1[3]) else 2))
@@ -226,24 +360,26 @@ def rank_program(g, core, T, topo):
     def cp(out, in_):
         op("v", lambda: g.vector.tensor_copy(out[0], in_[0]), in_[1], out[1], plain(out, in_))
 
-    def scatter(name, lo, src):
-        op("v", lambda: g.vector.tensor_copy(T[name][:, lo:lo + TB].indirect(T.SCL[:]), src[0]), src[1] + ["SCL"],
-           [(name, lo, lo + TB)], cycles(128 * SCATTER, 0.05))
+    def scatter(name, lo, src, more=None):
+        def fn():
+            out = T[name][:, lo:lo + TB].indirect(T.SCL[:])
+            return g.vector.tensor_tensor(out, src[0], more[0], A.add) if more else g.vector.tensor_copy(out, src[0])
+        op("v", fn, src[1] + (more[1] if more else []) + ["SCL"], [(name, lo, lo + TB)], cycles(128 * SCATTER, 0.05))
 
     def fill(out, c):
         op("v", lambda: g.vector.memset(out[0], c), [], out[1], plain(out, out))
 
     def act(out, in_, func=F.Copy, scale=None, bias=None):
-        kw = {k: v[0] for k, v in (("scale", scale), ("bias", bias)) if v}
+        kw = {k: num(v)[0] for k, v in (("scale", scale), ("bias", bias)) if v}
         op("s", lambda: g.scalar.activation(out[0], in_[0], func, **kw), in_[1] + num(scale)[1] + num(bias)[1], out[1],
-           cycles(out[2] * (GATHER if in_[3] == "g" else 1), 0.08))
+           cycles(out[2] * (GATHER if in_[3] == "g" else 1), 0.08), picks=in_[2] * (in_[3] == "g"))
 
     def iota(out, pattern, base=0, cm=0):
         kw = {} if out[1][0][0] in BUFS["int32"] else dict(allow_small_or_imprecise_dtypes=True)
         op("g", lambda: g.iota(out[0], pattern, base, cm, **kw), [], out[1], 0.13 + 2 * out[2] * CYCLE)
 
-    def diagonal(out, in_):
-        op("g", lambda: g.affine_select(T[out][:], T[in_][:], [[-1, 128]], A.is_equal, 0.0, 0, 1), [in_], [out], 0.4)
+    def diagonal(out, c):
+        op("g", lambda: g.affine_select(T[out][:], T.M1[:], [[-1, 128]], A.not_equal, c, 0, 1), ["M1"], [out], 0.4)
 
     def mms(parts, start=True, stop=True):
         def fn():
@@ -254,9 +390,8 @@ def rank_program(g, core, T, topo):
         op("t", fn, [r for o, l, m in parts for r in l[1] + m[1]], [r for o, l, m in parts for r in o[1]],
            sum(cycles(o[2], 0) for o, l, m in parts))
 
-    def gx(q, dst, d0, src, s0, s1, lst, l0, lo, hi):
-        if lo < hi:
-            (cp if q == "v" else act)(S(dst, d0 + lo, d0 + hi), G(src, s0, s1, lst, l0 + lo, l0 + hi))
+    def gx(dst, d0, src, s0, s1, lst, l0, lo, hi, scale=None):
+        act(S(dst, d0 + lo, d0 + hi), G(src, s0, s1, lst, l0 + lo, l0 + hi), scale=scale)
 
     ncol = [0]
 
@@ -269,9 +404,9 @@ def rank_program(g, core, T, topo):
         ts(c, a, s1, op0, s2, op1)
         return c
 
-    def colsum(in_):
+    def colact(a, scale, bias=None):
         c = col()
-        op("v", lambda: g.vector.tensor_reduce(c[0], in_[0], AxisListType.X, A.add), in_[1], c[1], cycles(64))
+        act(c, a, F.Identity, scale, bias)
         return c
 
     def rows(name, r, lo, hi):
@@ -280,108 +415,154 @@ def rank_program(g, core, T, topo):
     def part(name, lo, hi, own=True):
         return T[name][lo:hi, :], [(name, 0, 256, lo if own else None)], 256, 4
 
-    for i in range(2):
-        dma("y", "l_prev", T.PC[64 * i:64 * i + 64, :], T.prev[:, :], [], part("PC", 64 * i, 0)[1], 2)
+    dma("y", "l_prev", T.PC[0:64, :], T.prev[:, :], [], ["PC"])
+    last = follow()
     for i in range(4):
-        dma("s", "l_kid", T.KC[32 * i:32 * i + 32, :], (T.kid0, T.kid1)[i % 2][:, :], [], part("KC", 32 * i, 0)[1], 4)
-    dma("y", "l_cur", T.CURI[:], T.cur[:, :], [], ["CURI"])
-    dma("y", "l_start", T.STI[:], T.start[:, :], [], ["STI"])
-    dma("y", "l_x", T.XW[:], T.x[:, :], [], ["XW"])
-
-    iota(S("IP"), [[0, 1]], 0, 1)
-    iota(S("I16"), [[0, 8], [1, 16]])
-    iota(S("N0"), [[256, 4]], 1024)
-    iota(S("J2"), [[1, 256]])
-    iota(S("THP"), [[0, 1]])
-    iota(S("OWN"), [[1, 256]], 0, 256)
-    iota(S("D0"), [[0, 32], [66000 - int(8 * SLOPE) - DUP, 2]], -66000)
-    iota(S("IDI"), [[1, 128]], 0, -1)
-    iota(S("IG"), [[1, 8], [0, 16]])
-    for b in ("WP", "WW", "WA"):
-        iota(S(b), [[0, 40]])
-    for lo, hi in ((1024, DUP), (DUP + 1024, DUP + TB)):
-        iota(S("ZW", lo, hi), [[0, hi - lo]])
-    iota(S("ON"), [[0, 128]], 1)
-    iota(S("C8"), [[0, 32]], 8)
-    iota(S("IC"), [[1, 144]], -15)
-    iota(S("PF"), [[0, 1]], 0, 1)
-    iota(S("CURW"), [[0, 1024]])
-
-    fill(S("ZB"), 0.0)
+        dma("ys"[i % 2], "l_kid", T.KC[32 * i:32 * i + 32, :], (T.kid0, T.kid1)[i % 2][:, :], [], part("KC", 32 * i, 0)[1], 4)
+        last = follow(last)
+    for sem, dst, src in (("l_cur", "CURI", T.cur), ("l_start", "STI", T.start), ("l_z", "ZL", T.z)):
+        dma("y", sem, T[dst][:], src[:, :], [], [dst])
+        last = follow(last)
+    dma("y", "l_x", T.XW[:, 0:1024], T.x[:, 0:1024], [], [("XW", 0, 1024)], 2)
+    last = follow(last)
+    cp(part("PB", 0, 64), part("PC", 0, 64, False))
+    tt(part("PL", 0, 64), part("PC", 0, 64, False), part("PB", 0, 64, False), A.subtract)
+    fill(S("EM", 0, 1024), -256.0)
     for lo in (0, 1024):
-        act(S("PW", lo, lo + 1024), S("ZB"))
-    for i, (n, o) in enumerate(((15, A.bitwise_and), (4, A.arith_shift_right), (31, A.bitwise_and))):
-        ts(S("IQ", i, i + 1), S("IP"), n, o)
-    cp(col(3), S("IQ"))
-    p15, p4, p31 = [S("col", i, i + 1) for i in range(3)]
-    ts(S("MD"), S("I16"), p15, A.is_equal)
-    e = [S("MD", r, r + 1) for r in range(16)]
-    m78, lt4 = colsum(S("MD", 7, 9)), colop(p15, 4.0, A.is_lt)
-    m25, m68 = colsum(S("MD", 2, 6)), colsum(S("MD", 6, 9))
-    ts(S("BN"), S("N0"), m25, A.mult, m68, A.add)
-    for lo in (0, DUP):
-        act(S("KW", lo, lo + 1024), S("ZB"), F.Identity, bias=m78)
-    for lo in (0, DUP):
-        for t in range(4):
-            n = 128 if lo and t == 3 else 256
-            act(S("KW", lo + 1024 + 256 * t, lo + 1024 + 256 * t + n), S("J2", 0, n), F.Identity, lt4, S("BN", t, t + 1))
-    ts(part("OWN", 64, 96), part("OWN", 64, 96), 1023, A.bitwise_and)
-
-    for src, mid, dst in (("PC", "PCL", "PB"), ("KC", "KCL", "KB")):
-        for lo, bits in ((0, 255), (64, 2047 - 255)):
-            ts(part(mid, lo, lo + 64), part(src, lo, lo + 64, False), bits, A.bitwise_and)
-        cp(S(dst), S(mid))
-    cp(part("KF", 0, 64), part("KC", 0, 64, False))
-    tt(part("KF", 64, 96), part("KC", 64, 96, False), part("OWN", 64, 96), A.is_equal)
-    cp(S("SL", 0, 64), S("CURI"))
-    cp(S("ST"), S("STI"))
-    for r in range(2):
-        dma("y", "d_p", rows("PW", r, 0, 2048)[0], T.PB[64 * r:64 * r + 64, :], ["PB"], rows("PW", r, 0, 2048)[1], 2)
-    for sem, lo in (("d_k", 0), ("d_k2", DUP)):
-        for r, b, i in ((0, "KB", 0), (1, "KB", 1), (4, "KB", 2), (5, "KB", 3), (2, "KF", 0), (3, "KF", 1), (6, "KF", 2)):
-            dma("y", sem, rows("KW", r, lo, lo + 1024)[0], T[b][32 * i:32 * i + 32, :], [b], rows("KW", r, lo, lo + 1024)[1], 7)
-        dma("y", "l_z2" if lo else "l_z", T.ZW[:, lo:lo + 1024], T.z[:, :], [], [("ZW", lo, lo + 1024)])
+        act(S("PW", lo, lo + 1024), S("EM", 0, 1024), F.Identity, None, 256.0)
+    for r, b in enumerate(("PB", "PL")):
+        dma("y", "d_p", rows("PW", r, 0, 2048)[0], T[b][0:64, :], [b], rows("PW", r, 0, 2048)[1], 2)
+        last = follow(last)
+    dma("y", "l_x", T.XW[:, 1024:2048], T.x[:, 1024:2048], [], [("XW", 1024, 2048)], 2)
+    last = follow(last)
     dma("y", "l_w", T.WI[:], T.w[:, :], [], ["WI"])
+    last = follow(last)
+    iota(S("THP"), [[0, 1]])
     for r in (7, 8):
         dma("y", "l_th", rows("THP", r, 0, 1)[0], T.th[:, :], [], rows("THP", r, 0, 1)[1], 2)
+        last = follow(last)
     for lo in (0, DUP):
         dma("y", "l_rs", T.RW[:, lo:lo + 1024], T.rs[:, :], [], [("RW", lo, lo + 1024)], 2)
+        last = follow(last)
+
+    iota(S("IP"), [[0, 1]], 0, 1)
+    iota(S("PF"), [[0, 1]], 0, 1)
+    for a in range(2):
+        iota((T.CV[:, a:16:2, :], [("CV", a, a + 1)], 128), [[4, 8], [0, 4], [1, 4]], 32 * a)
+    iota(S("I16"), [[0, 8], [1, 16]])
+    iota(S("OWN"), [[1, 256]])
+    iota(S("KO", 1024, DUP), [[1, 1024]], 1024)
+    for w, d in enumerate((-40000, -7 * 4096 - 1536, 512)):
+        iota(S("D0", w, 96, 3), [[0, 32]], d)
+    iota(S("M1"), [[0, 128]])
+    diagonal("IDS", UNIT)
+    diagonal("ID", 1.0)
+    iota(S("IG"), [[1, 8], [0, 16]])
+    iota(S("SG"), [[1, 3]], 2)
+    iota(S("SC"), [[-768, 3]], -1792 - 1536)
+    iota(S("WP"), [[0, 40]])
+    iota(S("ON"), [[0, 128]], 1)
+    iota(S("C96"), [[0, 32], [-4, 3]])
+    early = [i for i, c in enumerate(calls) if c["q"] == "g"]
+    for b in ("WW", "WA"):
+        iota(S(b, 0, 40), [[0, 40]])
+    iota(S("C8"), [[0, 32]], 8)
+    iota(S("IC"), [[1, 144]], -15)
+    iota(S("CURW"), [[0, 1024]])
+
+    cuts = ((15, A.bitwise_and), (4, A.arith_shift_right), (31, A.bitwise_and), (3, A.bitwise_and), (4, A.bitwise_and),
+            (1, A.bitwise_and), (8, A.bitwise_and))
+    for i, (n, o) in enumerate(cuts):
+        ts(S("IQ", i, i + 1), S("IP"), n, o)
+    cp(col(7), S("IQ"))
+    p15, p4, p31, p3, pb, p1, p8 = [S("col", i, i + 1) for i in range(7)]
+    ts(S("MD", 0, 128), S("I16"), p15, A.is_equal)
+    e = [S("MD", r, r + 1) for r in range(16)]
+
+    hi64 = colop(S("PF"), 64.0, A.is_ge)
+    p63 = colact(hi64, -64.0, S("PF"))
+    level = colact(hi64, float(LEVELS[1] - LEVELS[0]), float(LEVELS[0]))
+
+    def places(buf, b, lo=0, hi=16):
+        return T[buf][:, b:32:2, lo:hi], [(buf, b, b + 1)], 16 * (hi - lo), 2
+
+    def match(lo=0, hi=16):
+        return T.CV[:, :, lo:hi], ["CV"], 16 * (hi - lo), 2
+
+    ts(places("ZA", 0), match(), p63, A.is_equal, colact(hi64, 6.0, 2.0), A.mult)
+    ts(places("ZA", 1), places("ZA", 0), colact(hi64, 2.0, -1.0), A.mult)
+    ts(places("ZC", 0), match(), p63, A.is_equal, -768.0, A.mult)
+    for m, c in enumerate((colact(hi64, -3072.0, 2304.0), colact(hi64, 3072.0, -768.0))):
+        ts(places("ZC", 0, 4 * m, 4 * m + 4), match(0, 4), p63, A.is_equal, c, A.mult)
+    ts(places("ZC", 1), places("ZC", 0), -1.0, A.mult)
+    sign = colact(pb, -0.5, 1.0)
+    zb, two = colact(sign, -1792.0, HALF), colact(sign, 2.0)
+    act(S("OWN"), S("OWN"), F.Identity, None, colact(p3, 256.0))
+    ts(S("QB"), S("KC"), level, A.is_ge)
+    cp(part("QA", 0, 64), part("KC", 0, 64, False))
+    tt(part("QA", 64, 128), part("KC", 64, 128, False), part("OWN", 64, 128), A.is_equal)
+    for c in range(2):
+        bank = "pD%d" % (2 + c)
+        for i, (w, q) in enumerate((("ZC", "QB"), ("ZA", "QA"))):
+            mms([(S(bank, 256 * j, 256 * j + 256), (T[w][:, :, 2 * c + j:16:4], [w]), S(q)) for j in range(2)], i == 0, False)
+        mms([(S(bank), S("IDS"), S("ZL", 512 * c, 512 * c + 512))], False, True)
+        for lo in (0, DUP):
+            out = S("ZK", lo + 512 * c, lo + 512 * c + 512)
+            if lo == c == 0:
+                ts(out, S(bank), zb, A.add)
+            else:
+                act(out, S(bank), F.Identity, bias=zb)
+    ts(S("B1"), S("SG"), p3, A.is_gt, 3072.0, A.mult)
+    tt(S("B1"), S("B1"), S("SC"), A.add)
+    act(S("B3"), S("B1"), F.Identity, sign, 8.0 + HALF)
+    ends, leaves = (1024, LEVELS[2], LEVELS[3]), []
+    for lo, top in ((0, DUP), (DUP, TB)):
+        for i, (a, b) in enumerate(zip(ends, ends[1:] + (top,))):
+            act(S("ZK", lo + a, lo + b), S("KO", a, b), F.Identity, two, S("B3", i, i + 1))
+            leaves.append(len(calls) - 1)
+    up = colact(p8, colact(sign, 0.25))
+    act(S("B4"), S("B3"), F.Identity, None, colact(up, 1.0, -8.0))
+    for i, (a, b) in enumerate(zip(ends, ends[1:] + (1536,))):
+        act(S("KN", a // 2 - 512, b // 2 - 512), S("KO", a, b, 2), F.Identity, two, S("B4", i, i + 1))
+    act(S("KM"), S("KO", 1024, 1792, 2), F.Identity, bias=p1)
+
+    cp(S("SL", 0, 64), S("CURI"))
+    cp(S("ST"), S("STI"))
+    cp(part("KF", 0, 64), part("KC", 0, 64, False))
+    for r in range(2):
+        dma("y", "d_k", rows("KO", r, 0, 1024)[0], T.KF[32 * r:32 * r + 32, :], ["KF"], rows("KO", r, 0, 1024)[1], 2)
 
     wp = colop(p15, 2.0, A.is_lt)
     ts(S("R3"), S("I16", 0, 8), p4, A.is_equal)
-    tt(col(2), S("MD", 0, 2), S("MD", 4, 6), A.add)
-    wk0, wk1 = S("col", ncol[0] - 2, ncol[0] - 1), S("col", ncol[0] - 1, ncol[0])
-    ts(S("WP", 3, 35, 4), S("R3"), wp, A.mult)
-    wk0s = colop(e[7], -float(DUP), A.mult, wk0, A.add)
-    ts(S("IDN"), S("IDI"), 0.0, A.is_equal, -1.0, A.mult)
-    ts(S("WC"), S("R3"), -SLOPE, A.mult)
-    for b in ("HX", "HS"):
-        cp((T[b][:], [b], 280, 2), S("ZB", 0, 280))
-    ts(S("WK", 0, 8), S("R3"), wk0s, A.mult)
-    ts(S("WK", 8, 16), S("R3"), wk1, A.mult)
+    act(S("WP", 3, 35, 4), S("R3"), F.Identity, wp)
+    ts(S("IDN"), S("IDS"), -512.0, A.mult)
+    for out in (S("HH"), S("HS"), S("W3"), (T.HX[:], ["HX"], 784, 2)):
+        ts(out, S("EM", 0, out[2]), 0.0, A.mult)
+    ck1 = colact(up, 1.0 / 32)
+    ck0 = colact(ck1, -1.0, colact(sign, 1.0 / 16))
+    ts(S("W3", 9, 105, 12), S("R3"), -4096.0, A.mult)
+    ts(S("W3", 10, 105, 12), S("R3"), ck1, A.mult)
+    ts(S("W3", 11, 105, 12), S("R3"), ck0, A.mult, -1.0, A.mult)
     ts(S("GS"), S("IG"), p4, A.is_equal)
-    ts(S("SJ"), S("MD", 0, 16), -2.0, A.mult, 1.0, A.add)
+    act(S("SJ"), S("MD", 0, 16), F.Identity, -2.0, 1.0)
     fill(S("CT", 0, 1), -1.0)
-    ts(S("WL"), S("GS"), e[6], A.mult, -1024.0, A.mult)
+    ts(S("WL"), S("GS"), 1.0 / 128, A.mult)
+    ts(S("CL"), S("EM", 0, 128), 256 - 159.625, A.add)
 
     for b in range(11):
-        at(-2.9 if b < 8 else b - 7.75)
         ts(S("CT", 1 << b, 2 << b), S("CT", 0, 1 << b), S("SJ", b, b + 1), A.mult)
-    at(0.25)
     cp(S("CURF"), S("CURI"))
-    cp((T.HH[:], ["HH"], 280, 2), S("ZB", 0, 280))
     dma("y", "d_cw", T.CURW[0:128:16, :], T.CURF[:], ["CURF"], ["CURW"])
-    at(1.25)
-    p16 = colop(p4, 16.0, A.mult)
+    p16 = colact(p4, 16.0)
     wf = colop(S("WI"), 1.0, A.mult)
-    ts(S("WA", 3, 35, 4), S("R3"), 97.0 / 1024, A.mult)
+    act(S("WA", 3, 35, 4), S("R3"), F.Identity, 97.0 / 1024)
     ts(S("WW", 3, 35, 4), S("R3"), wf, A.mult, 1.0 / 1024, A.mult)
-    at(2.25)
     dma("y", "d_ct", T.CT[:, DUP:DUP + 1792], T.CT[:, 0:1792], [("CT", 0, 1792)], [("CT", DUP, DUP + 1792)])
-    at(3.25)
-    iota(S("EM", 0, 1024), [[0, 1024]], -256)
+    codes = len(calls) - 1
     dma("g", "l_env", T.EM[:, 0:1024], T.env[:, :], [("EM", 0, 1024)], [("EM", 0, 1024)], accum_op=A.add)
+    follow(last, *early)
     send("e", "EP", 0, "EM", 0, 1024)
+    sent = len(calls) - 1
     for b in ("EM", "EP"):
         for i, n in ((1, 1024), (2, EW - 2048)):
             dma("y", "d_%s%d" % ("m" if b == "EM" else "e", i), T[b][:, 1024 * i:1024 * i + n], T[b][:, 0:n], [(b, 0, n)],
@@ -389,187 +570,199 @@ def rank_program(g, core, T, topo):
     for lo, hi in ((1024, DUP), (DUP + 1024, DUP + 1792)):
         iota(S("RW", lo, hi), [[0, hi - lo]])
     iota(S("JN"), [[0, 2], [1, 128]])
-    iota(S("M1"), [[0, 128]], -1)
-    diagonal("ID", "ON")
-    diagonal("IDM", "M1")
+    diagonal("IDM", -1.0)
+    diagonal("IDQ", 128 * UNIT)
     iota(S("NEG"), [[0, 16]], -8192)
     iota(S("NL"), [[0, 128]], 0, -1)
     iota(S("RB"), [[0, 1]], -11 * 4096, -32)
-    at(4.25)
     ts(S("VP"), S("IC"), p16, A.is_equal, wp, A.mult)
-    ts(S("VW"), S("IC"), p16, A.is_equal, wf, A.mult)
+    ts(S("VW", 0, 144), S("IC"), p16, A.is_equal, wf, A.mult)
     ts(S("THL"), S("THP"), 255, A.bitwise_and)
-    at(5.25)
     ce = colop(p31, 11.0, A.is_lt, 64.0, A.mult)
     c27, c16 = colop(p31, 27.0, A.is_lt, 64.0, A.mult), colop(p31, 16.0, A.is_lt, 64.0, A.mult)
     thh = col()
     tt(thh, S("THP"), S("THL"), A.subtract)
-    wa, m13 = colop(S("THL"), e[8], A.mult), colsum(S("MD", 1, 4, 2))
-    at(6.25)
-    co, wb = colop(c27, c16, A.subtract), colop(thh, 8192.0, A.add, e[7], A.mult)
-    wc, wd = colop(e[6], 8192.0, A.mult, wa, A.subtract), colop(e[7], -1792.0, A.mult, wk0, A.add)
-    mk, two = colop(m13, m78, A.add), colop(lt4, 2.0, A.mult)
-    at(7.25)
-    wq = colop(wc, wb, A.subtract)
-    ts(S("WQ", 128, 256), S("GS"), wd, A.mult)
-    ts(S("BK"), S("N0"), m25, A.mult, mk, A.add)
-    ts(S("WQ", 0, 128), S("GS"), wq, A.mult)
-    at(8.25)
-    ts(S("LM"), S("MD"), S("PF"), A.mult)
-    ts(S("MB"), S("MD"), -1e9, A.mult, 1e9, A.add)
+    wa = colop(S("THL"), e[8], A.mult)
+    co, wb = colact(c16, -1.0, c27), colop(thh, 8192.0, A.add, e[7], A.mult)
+    wq = colop(wa, wb, A.add, -1.0, A.mult)
+    act(S("TW", 0, 128), S("GS"), F.Identity, wq)
+    act(S("TW", 128, 256), S("GS"), F.Identity, colact(e[7], -896.0))
+    ts(S("WQ", 0, 128), S("GS"), 64.0, A.mult)
+    ts(S("WQ", 128, 256), S("GS"), ck0, A.mult)
+    act(S("WW", 40, 80), S("WW", 0, 40), scale=128.0)
+    act(S("VW", 144, 288), S("VW", 0, 144), scale=128.0)
+    for i in range(4):
+        act(S("WW", 80 + i, 112, 4), S("WW", 43, 75, 4))
+    act(S("LM"), S("MD", 0, 128), F.Identity, S("PF"))
+    act(S("MB"), S("MD", 0, 128), F.Identity, -1e9, 1e9)
+    turned = colact(p3, 4.0, colop(pb, p8, A.add, 0.25, A.mult))
+    ts(S("MD", 128, 256), S("I16"), turned, A.is_equal)
+    act(S("R3N", 8, 16), S("R3"), F.Identity, colact(turned, -1.0, p15))
+    for b, c in (("M15", -15.0), ("M12", 12.0), ("M63", -63.9375)):
+        ts(S(b), S("IDN"), c, A.mult)
     cp(S("R3H"), S("R3"))
-    for t in range(3):
-        at(9.35 + ROUND * t)
-        act(S("KN", 128 * t, 128 * t + 128), S("J2", 0, 128), F.Identity, two, S("BK", t, t + 1))
+    act(S("R3N", 0, 8), S("R3"), scale=-1024.0)
+    for i, c in enumerate(calls):
+        c["pin"] = PIN["t0"] + PIN["setup"] * i / len(calls)
+    calls[sent]["pin"] = PIN["e"]
+    for i in leaves:
+        calls[i]["pin"] = PIN["leaves"]
+    calls[codes]["pin"] = PIN["codes"]
 
     W = ("pA", "pB")
 
-    def blocks(src, h):
-        return [S(src, 512 * h + i, 512 * h + 512, 4) for i in range(4)]
+    def blocks(src, lo):
+        return [S(src, lo + i, lo + 512, 4) for i in range(4)]
 
-    def words(bank, c0, src, h, wt, start=True, stop=True):
-        mms([(S(bank, c0, c0 + 32), b, S(wt, 3 - i, 35 - i)) for i, b in enumerate(blocks(src, h))], start, stop)
+    def words(bank, c0, src, lo, wt, start=True, stop=True, w0=0):
+        mms([(S(bank, c0, c0 + 32), b, S(wt, w0 + 3 - i, w0 + 35 - i)) for i, b in enumerate(blocks(src, lo))], start, stop)
 
-    def slots(buf, h):
-        return T[buf][:, 35 * h + 3:35 * h + 35:4, :], [(buf, 35 * h, 35 * h + 35)], 32, 2
+    def slots(h):
+        return T.HX[:, 32 * h + 3:32 * h + 35:4, :], [("HX", 32 * h + 3, 32 * h + 32)], 32, 2
 
-    def back(bank, c0, buf, h):
-        mms([(S(bank, c0, c0 + 32), (T[buf][:, 35 * h + 3 - j:35 * h + 35 - j, :], [(buf, 35 * h, 35 * h + 35)]),
-              S("IDN", j, 128, 4)) for j in range(4)])
+    def back(bank, c0, parts):
+        mms([(S(bank, c0, c0 + 32), (T.HX[:, 32 * h + 3 - j:32 * h + 35 - j, :], slots(h)[1]), S(m, j, 128, 4))
+             for h, m in parts for j in range(4)])
 
-    def wrap(bank, lt, src, m, ks, start, stop, contiguous=False):
-        mms([(S(bank, 0, m), S(lt, 15 - k, 143 - k), S(src, k * m, (k + 1) * m) if contiguous else S(src, k, 16 * m, 16))
-             for k in ks], start, stop)
+    def spaced(h):
+        return S("HH", 128 * h + 3, 128 * h + 128, 4)
+
+    def turn(bank, c0, buf, first, step, reg):
+        mms([(S(bank, c0, c0 + 32), (T[buf][:, first - step * j:first + step * (127 - j) + 1:step], reg), S("IDN", j, 128, 4))
+             for j in range(4)])
+
+    def wrap(bank, lt, w0, src, ks, start, stop):
+        mms([(S(bank, 0, src(k)[2]), S(lt, w0 + 15 - k, w0 + 143 - k), src(k)) for k in ks], start, stop)
 
     def step(t, h, k):
-        n, lo, hi = ROUND * t + 2 * k + h, 512 * h, 512 * h + 512
+        lo, hi = 512 * h, 512 * h + 512
         top, lst = (DUP + TB, "FL") if k else (1024, "ST")
-        at(n + TN["kg"] if k or not t else n + TN["kg0"] + TN["kg1"] * h)
-        gx("s", "KG", 0, "KW", 0, top, lst, 0, lo, hi)
-        at(n)
+        mms([(S(W[h], 0, 96), S("ON"), S("C96"))], True, False)
         if t and not k:
-            tt(S("BT", lo, hi), S("PG", lo, hi), S("pD%d" % h), A.is_le)
+            tt(S("J", lo, hi), S("PZ", lo, hi), S("pD%d" % h), A.subtract)
+            due(when(t, k, h))
         else:
-            tt(S("BT", lo, hi), G("ZW", 0, top, lst, lo, hi), S("XA%d" % (t % 2), 1024 * k + lo, 1024 * k + hi), A.is_le)
-            at(n + TN["mm"])
-        mms([(S(W[h], 2 * i + 1, 128, 8), b, S("WK")) for i, b in enumerate(blocks("KG", h))], True, False)
-        mms([(S(W[h], 2 * i, 64, 8), b, S("WC")) for i, b in enumerate(blocks("BT", h))], False, True)
+            n, xa = P["zs1" if t else "zs0"], "XA%d" % (t % 2)
+            cut = lo + P["c1" if t else "cut"]
+            for a, b, later in ((lo, cut, 0.0), (cut, hi - n, PIN["two" if t else "two0"])):
+                tt(S("J", a, b), G("ZK", 0, top, lst, a, b), S(xa, 1024 * k + a, 1024 * k + b), A.subtract)
+                due(when(t, k, h) + later)
+            if n:
+                bank = "pD%d" % (2 + h)
+                gx("PZ", 0, "ZK", 0, top, lst, 0, hi - n, hi)
+                mms([(S(bank, 256, 256 + n), S("ID"), S(xa, 1024 * k + hi - n, 1024 * k + hi))])
+                tt(S("J", hi - n, hi), S("PZ", hi - n, hi), S(bank, 256, 256 + n), A.subtract)
+                due(when(t, k, h) + PIN["sh"])
+        mms([(S(W[h], 0, 96), b, S("W3", 9 - 3 * i, 105 - 3 * i)) for i, b in enumerate(blocks("J", lo))], False, True)
         if t < 2 and h == 0:
-            mms([(S("pL", 0, 128), S("KG", 0, 128), S("WL"))], k == 0, k == 5)
-        at(n + TN["scan"])
-        o = S("S2", 64 * h, 64 * h + 64)
-        op("v", lambda: g.vector.tensor_tensor_scan(o[0], T.D0[:], T[W[h]][:, 0:64], 0.0, A.subtract, A.max),
-           ["D0", (W[h], 0, 64)], o[1], cycles(64))
-        at(n + TN["tt"])
-        tt(slots("HS", h), S(W[h], 65, 128, 2), S("S2", 64 * h + 1, 64 * h + 64, 2), A.min)
-        back(W[h], 128, "HS", h)
-        at(n + (TN["flb"] if (h, k) == (1, 5) else TN["fl"]))
-        ts(S("FL", 32 * h, 32 * h + 32), S(W[h], 128, 160), -1.0, A.mult, float(DUP), A.add)
+            if k == 0:
+                mms([(S("pL", i, i + 128), S("IDN"), S("CL")) for i in (0, 128)], True, False)
+            mms([(S("pL", 128 * (k % 2), 128 * (k % 2) + 128), S("J", 0, 128), S("WL"))], False, k == 5)
+        o = S("HS", 400 * h + 4, 400 * h + 388, 4)
+        op("v", lambda: g.vector.tensor_tensor_scan(o[0], T.D0[:], T[W[h]][:, 0:96], 0.0, A.subtract, A.max),
+           ["D0", (W[h], 0, 96)], o[1], cycles(96))
+        turn(W[h], 128, "HS", 400 * h + 12, 3, o[1])
+        ts(S("FL", 32 * h, 32 * h + 32), S(W[h], 128, 160), 1920.0, A.add)
 
-    def hsum(t, h, n, n2):
+    def hsum(t, h):
         lo, hi, bank = 32 * h, 32 * h + 32, "pD%d" % (2 + h)
-        at(n)
-        mms([(S(bank, 0, 32), S("ON"), S("C8"))], True, False)
-        for src in ("SP", "TT") if t else ("XA0",):
-            words(bank, 0, src, h, "WW", False, src != "SP")
+        mms([(S(bank, 0, 32), S("ON"), S("C8"))] + [(S(bank, 0, 32), S("ON"), S("WW", 80, 112))] * (t > 0), True, False)
+        for src in ("SP", "TT") if t else ("CU",):
+            words(bank, 0, src, 512 * h, "WW", False, src != "SP", 40 * (src == "TT"))
         ts(S("HQ", lo, hi), S(bank, 0, 32), 0.5005, A.add)
-        at(n + 0.03)
-        tt(slots("HH", h), S(bank, 0, 32), S("HQ", lo, hi), A.subtract)
+        tt(spaced(h), S(bank, 0, 32), S("HQ", lo, hi), A.subtract)
         if t:
-            back(bank, 32, "HH", h)
-            at(n2)
+            turn(bank, 32, "HH", 128 * h + 3, 1, spaced(h)[1])
             ts(S("HL", lo, hi), S(bank, 32, 64), -1024.0, A.mult, 1024.0, A.add)
+            due(when(t - 1, 6, h) + PIN["hl"])
+
+    def even_lists(t, h):
+        ts(slots(h), spaced(h), 4096.0, A.mult)
+        ts(slots(2 + h), spaced(h), 256.0, A.mult, 1281 - 0.375, A.add)
+        ts(slots(4 + h), spaced(h), 64.0, A.mult, 1089 - 0.46875, A.add)
+        bank, lo = "pD%d" % h, 32 * h
+        back(bank, 64 + lo, [(h, "IDN"), (2 + h, "M15"), (4 + h, "M12")])
+        ts(S("HM", lo, lo + 32), S(bank, 64 + lo, 96 + lo), -1.0, A.mult, 7171.0, A.add)
+        if t == 1:
+            back(bank, 128 + lo, [(h, "IDN"), (4 + h, "M63")])
+            ts(S("OL", lo, lo + 32), S(bank, 128 + lo, 160 + lo), -16.0, A.mult, 1114111.0, A.add)
 
     def outcome(t, h):
-        n, lo, hi, x0 = ROUND * t + 11 + h, 512 * h, 512 * h + 512, 64 * t + 32 * h
-        at(n + TN["r" + "ab"[h]])
-        tt(S("BT", lo, hi), G("RW", 0, DUP + 1792, "FL", lo, hi), S("XA%d" % (t % 2), lo, hi), A.is_gt)
-        words(W[h], 160, "BT", h, "WA")
-        at(n + TN["hx" + "ab"[h]])
-        tt(slots("HX", h), S(W[h], 160, 192), slots("HH", h), A.add)
-        back(W[h], 192, "HX", h)
-        at(n + TN["ix" + "ab"[h]])
+        lo, x0 = 512 * h, 64 * t + 32 * h
+        for i, a in enumerate((lo, lo + 256)):
+            tt(S("BT", a, a + 256), G("RW", 0, DUP + 1792, "FL", a, a + 256), S("CU", 1024 * t + a, 1024 * t + a + 256), A.is_gt)
+            due(when(t, 6, h) + PIN["r" + "ab"[h] + "01"[i]])
+        words(W[h], 160, "BT", lo, "WA")
+        tt(slots(h), S(W[h], 160, 192), spaced(h), A.add)
+        back(W[h], 192, [(h, "IDN")])
         ts(S("IX", x0, x0 + 32), S(W[h], 192, 224), -1024.0, A.mult, 1024.0, A.add)
         send("i%d" % t + "ab"[h], "IXP", x0, "IX", x0, x0 + 32)
+        due(when(t, 6, h) + PIN["send" + "ab"[h]])
 
     def band(name, a):
         return T[name][32 * a:32 * a + 32, :], [name]
 
     def splits(t):
-        xa, n0, n = "XA%d" % (t % 2), 1024 + 256 * t, ROUND * t
-        at(n + 11.11)
+        xa, n0 = "XA%d" % (t % 2), 1024 + 256 * t
         act(S("BE"), G("CT", 0, DUP + 1792, "FL", 0, 128), F.Identity, ce)
         act(S("BO"), G("CT", 0, DUP + 1792, "FL", 0, 128), F.Identity, co)
         act(S("RN"), G("RW", 0, DUP + 1792, "FL", 0, 128))
-        act(S("KG6"), G("KW", 0, DUP + TB, "FL", 0, 128))
-        at(n + TN["va"])
-        mms([(S("pM", 0, 256), S("KG6"), S("WQ")), (S("pM", 128, 256), S("ID"), S("NL"))], True, False)
+        ts(S("J6"), G("ZK", 0, DUP + TB, "FL", 0, 128), -0.5, A.add)
+        mms([(S("pM", 0, 256), S("ON"), S("TW")), (S("pM", 128, 256), S("ID"), S("NL"))], True, False)
+        mms([(S("pM", 0, 256), S("J6"), S("WQ"))], False, False)
         for a in range(4):
             bank = "pD%d" % a
-            at(n + 9.06 + a // 2)
             mms([(S(bank, 0, 256), band("ON", a), band("JN", a))], True, False)
-            at(n + TN["d0" if a < 2 else "d2"])
             mms([(S(bank, 128 * i, 128 * i + 128), band(b, a), band(b, a)) for i, b in enumerate(("BE", "BO"))], False, True)
-            at(n + TN["ee"])
             act(S("EE", 256 * a, 256 * a + 256), S(bank, 0, 256), F.Relu, bias=S("RB"))
-            at(n + TN["n0" if a < 2 else "n2"])
             mms([(S("pM", 16 * q, 16 * q + 16), S("EE", 128 * q, 128 * q + 128), S("NEG")) for q in (2 * a, 2 * a + 1)], False, False)
         if t < 2:
-            at(n + TN["t5"])
-            tt(S("T5"), S("pL", 0, 128), S("MD"), A.mult)
-            at(n + TN["xm"])
-            mms([(S("pL", 128, 136), S("LM"), S("R3")), (S("pL", 128, 136), S("T5"), S("R3"))])
-            at(n + TN["xl"])
-            ts(S("XL"), S("pL", 128, 136), 6144.0, A.add)
-            gx("s", "XV6", 0, xa, 0, XAW, "XL", 0, 0, 128)
-        at(n + TN["s1"])
-        tt(S("S1"), G("EM", 0, EW, "IX", 1024 * t, 1024 * t + 128), S(xa, 0, 128), A.add)
-        at(n + TN["t1"])
+            tt(S("T5"), S("pL", 0, 256), S("MD"), A.mult)
+            mms([(S("pL", 384, 392), S("LM"), S("R3"))] +
+                [(S("pL", 384, 392), S("T5", i, i + 128), S("R3N", b, b + 8)) for i in (0, 128) for b in (0, 8)])
+            ts(S("XL"), S("pL", 384, 392), 6144.0 + 320 * 1024, A.add)
+            gx("XV6", 0, xa, 0, XAW, "XL", 0, 0, 128)
+        tt(S("S1"), G("EM", 0, EW, "IX", 1024 * t, 1024 * t + 128), S("CU", 1024 * t, 1024 * t + 128), A.add)
+        due(when(t, 6, 0) + PIN["s1"])
         ts(S("T1"), S("S1"), 0.0, A.is_lt, 256.0, A.mult)
-        at(n + TN["rn"])
         mms([(S("pL", 256, 384), S("IDM"), S("RN"))], True, False)
-        at(n + TN["pd"])
         mms([(S("pL", 256, 384), S("ID"), S("S1"))], False, False)
         mms([(S("pL", 256, 384), S("ID"), S("T1"))], False, True)
         act(S("DA"), S("pL", 256, 384), F.Abs)
-        at(n + TN["far"])
         mms([(S("pM", 0, 128), S("DA"), S("GS"))], False, True)
-        at(n + (13.9 if t < 2 else TN["ph"]))
         mms([(S("pL", 384, 512), S("ID"), S(b)) for b in ("RN", "S1", "T1")])
-        at(n + TN["sm"])
         tt(S("SM"), S("pM", 0, 128), S("MB"), A.is_ge)
-        at(n + TN["t3"])
         tt(S("T3"), S("pM", 128, 256), S("SM"), A.mult)
         mms([(S("pM", 256, 264), S("LM"), S("R3")), (S("pM", 256, 264), S("T3"), S("R3H"))])
-        at(n + TN["scl"])
         ts(S("SCL"), S("pM", 256, 264), 1792.0, A.add)
-        for lo in (0, DUP) if t < 2 else (0,):
-            at(n + TN["sk2" if lo else "sk"])
-            scatter("KW", lo, S("KN", 128 * t, 128 * t + 128))
-            at(n + TN["sz2" if lo else "sz"])
-            if t < 2:
-                scatter("ZW", lo, S("XV6"))
-        at(n + TN["sa" if t < 2 else "sa2"])
-        ts(S("SA"), S("pM", 0, 128), 0.0, A.is_ge)
-        at(now[0] + 0.01)
+        due(when(t, 6, 0) + PIN["scl"])
+        for lo in (0, DUP) if t < 2 else ():
+            scatter("ZK", lo, S("XV6"), S("KN", 128 * t, 128 * t + 128))
+            due(when(t, 6, 0) + PIN["sc2" if lo else "sc1"])
+        scatter("KO", 0, S("KM", 128 * t, 128 * t + 128))
+        act(S("DA"), S("pM", 0, 128), F.Sign, bias=0.5)
+        act(S("SA"), S("DA"), F.Relu)
         mms([(S("pM", 384, 512), S("SA"), S("ID"))])
         ts(S("H2"), S("pL", 384, 512), 0.5, A.mult, -0.25, A.add)
-        at(n + TN["rw" if t < 2 else "rw2"])
         tt(S("RW", n0, n0 + 256, 2), S("pM", 384, 512), S("RN"), A.mult)
         tt(S("RW", n0 + 1, n0 + 256, 2), S("pM", 384, 512), S("H2"), A.mult)
         if t < 2:
-            at(n + 18.35)
             act(S("RW", DUP + n0, DUP + n0 + 256), S("RW", n0, n0 + 256))
         if t:
             lo = 1024 if t == 1 else n0
             dma("y", "o_yr%d" % (t - 1), T.yr[:, lo - 1024:n0 - 768], T.RW[:, lo:n0 + 256], [("RW", lo, n0 + 256)], [])
 
-    def arrive(t, h):
-        n, lo, hi = ROUND * t, 512 * h, 512 * h + 512
-        at(n + TN["env" + "ab"[h]])
+    def arrive(t, lo, hi):
+        h = lo // 512
         tt(S("SP", lo, hi), G("EP", 0, EW, "IXP", 1024 * t + lo, 1024 * t + hi), S("CP", 1024 * t + lo, 1024 * t + hi), A.add)
-        at(n + TN["tt" + "ab"[h]])
-        ts(S("TT", lo, hi), S("SP", lo, hi), 0.0, A.is_lt, 256.0, A.mult)
+        due(when(t, 6, h) + PIN["env"])
+        if t < 2:
+            act(S("TT", lo, hi), S("SP", lo, hi), F.Sign, -1.0, -0.5)
+            due(when(t, 6, h) + PIN["tt"])
+            mms([(S("pD%d" % h), S("IDS"), S("SP", lo, hi))], True, False)
+            mms([(S("pD%d" % h), S("IDQ"), S("TT", lo, hi))], False, True)
+        else:
+            ts(S("TT", lo, hi), S("SP", lo, hi), 0.0, A.is_lt, 2.0, A.mult)
 
     def preds_out(t, bank):
         yf = "YF%d" % t
@@ -578,104 +771,71 @@ def rank_program(g, core, T, topo):
         ts(S(yf), S("YI", 64, 128), 1024.0 + 1024 * t, A.add)
         dma("y", "o_yp%d" % t, T.yp[:, 1024 * t:1024 * t + 1024], T[yf][:], [yf], [])
 
-    def first_preds():
-        at(ROUND + 4.2)
-        cp(S("OA", 0, 64), S("HL"))
-        ts(S("OB", 0, 64), S("HL"), 64.0, A.mult)
-        ts(S("OA", 64, 128), S("OA", 0, 64), 4, A.arith_shift_right)
-        at(TN["ol"])
-        ts(S("OB", 64, 128), S("OA", 64, 128), -1023.0, A.mult)
-        tt(S("OB", 0, 64), S("OB", 0, 64), S("OB", 64, 128), A.add)
-        cp(S("OL"), S("OB", 0, 64))
-        for h in range(2):
-            at(TN["ypc"] + h)
-            gx("s", "YPC", 0, "CURW", 0, 1024, "OL", 0, 512 * h, 512 * h + 512)
-        dma("y", "o_yp0", T.yp[:, 0:1024], T.YPC[0:128:16, :], ["YPC"], [])
-
-    def items(dst, k, h, src, s0, s1, lst, l0, n, xv):
-        lo = 512 * h
-        at(n + TN["xv"])
-        gx("v", dst, 1024 * k, src, s0, s1, lst, l0, lo, lo + xv)
-        at(n + TN["xs"])
-        gx("s", dst, 1024 * k, src, s0, s1, lst, l0, lo + xv, lo + 512)
-
     for k in range(6):
         for h in range(2):
-            n = 2 * k + h - 2
-            items("XA0", k, h, "XW", 0, 2048, "SL", 1024 * k, n if k else -5, TN["xv0"] if k else 0)
+            lo, hi, bank = 512 * h, 512 * h + 512, "pD%d" % h
+            gx("XA0", 1024 * k, "XW", 0, 2048, "SL", 1024 * k, lo, hi, UNIT)
             if k < 5:
-                bank = "pD%d" % h
-                at(n + TN["pg"] if k else -3)
-                gx("s", "PG", 0, "PW", 0, 2048, "SL", 1024 * k, 512 * h, 512 * h + 512)
-                at(n + TN["pw"] if k else -0.5 + 0.51 * h)
-                words(bank, 0, "PG", h, "WP")
-                at(n + TN["px"] if k else 0.06 + 0.2 * h)
-                cp(slots("HX", h), S(bank, 0, 32))
-                back(bank, 32, "HX", h)
-                at(n + TN["pl"] if k else 0.1 + 0.5 * h)
+                gx("PG", 0, "PW", 0, 2048, "SL", 1024 * k, lo, hi)
+                due(when(0, k, h) - PIN["lead"])
+                words(bank, 0, "PG", lo, "WP")
+                cp(spaced(h), S(bank, 0, 32))
+                turn(bank, 32, "HH", 128 * h + 3, 1, spaced(h)[1])
                 ts(S("SL", 64 * k + 64 + 32 * h, 64 * k + 96 + 32 * h), S(bank, 32, 64), -1.0, A.mult)
-    at(8.3)
-    gx("s", "PG", 0, "PW", 0, 2048, "SL", 5120, 0, 128)
-    at(TN["w5"])
-    wrap("pM", "VP", "PG", 8, range(16), True, True)
-    at(9.65)
+    gx("PG", 0, "PW", 0, 2048, "SL", 5120, 0, 128)
+    wrap("pM", "VP", 0, lambda k: S("PG", 4 * (k % 4) + k // 4, 128, 16), range(16), True, True)
     cp(S("SL", 384, 392), S("pM", 0, 8))
-    at(10.3)
-    gx("s", "XA0", 6144, "XW", 0, 2048, "SL", 6144, 0, 128)
-    at(-1)
-    send("c0", "CP", 0, "XA0", 0, 1024)
+    gx("XA0", 6144, "XW", 0, 2048, "SL", 6144, 0, 128, UNIT)
+    ts(S("CU", 0, 1024), S("XA0", 0, 1024), 512.0, A.mult)
+    send("c0", "CP", 0, "CU", 0, 1024)
+    due(when(0, 0, 1) + PIN["c"])
 
     for t in range(3):
-        xo, xa, n = "XA%d" % ((t - 1) % 2), "XA%d" % (t % 2), ROUND * t
+        xo, xa = "XA%d" % ((t - 1) % 2), "XA%d" % (t % 2)
         for h in range(2):
-            lo, hi, x = 512 * h, 512 * h + 512, "ab"[h]
+            lo, hi = 512 * h, 512 * h + 512
             if t:
-                at(n + TN["pg" + x])
-                gx("s", "PG", 0, "ZW", 0, 1024, "ST", 0, lo, hi)
-                arrive(t - 1, h)
-                at(n + TN["v1" + x])
-                mms([(S("pD%d" % h), S("ID"), S("SP", lo, hi))], True, False)
-                at(n + TN["v2" + x])
-                mms([(S("pD%d" % h), S("ID"), S("TT", lo, hi))], False, True)
-                at(n + TN["ev" + x])
-                act(S(xa, lo, hi), S("pD%d" % h))
-                hsum(t, h, n + TN["h" + x], n + TN["hl" + x])
-                for k in range(1, 6):
-                    items(xa, k, h, xo, 1024 * k - 1024, 1024 * k, "HL", 0, n + 2 * k + h - (2 if k > 1 else TN["x1"] - 0.7 * h),
-                          TN["xv1"] if 2 < k else 0)
-            else:
-                hsum(t, h, 4.06 + h, 0)
+                act(S("PZ", lo, hi), G("ZK", 0, 1024, "ST", lo, hi), F.Identity, None, -128 * UNIT)
+                due(when(t - 1, 6, 0) + 0.8 * h + PIN["pz"])
+                arrive(t - 1, lo, hi)
+                act(S("CU", 1024 * t + lo, 1024 * t + hi), S("pD%d" % h), F.Identity, 512.0, 128.0)
+                due(when(t - 1, 6, h) + PIN["cu"])
+                if t == 1 and h == 0:
+                    act(S(xa, 0, 128), S("pD0", 0, 128), F.Identity, None, 128 * UNIT)
+            hsum(t, h)
+            if t:
+                gx(xa, 1024, "CU", 1024 * t - 1024, 1024 * t, "HL", 0, lo, hi, UNIT)
+        for h in range(2):
+            step(t, h, 0)
         if t:
-            at(n + TN["evb"])
-            send("c%d" % t, "CP", 1024 * t, xa, 0, 1024)
+            for h in range(2):
+                even_lists(t, h)
+            for k in range(2, 6):
+                for lo in (0, 512):
+                    gx(xa, 1024 * k, xo, 1024 * k - 1024, 1024 * k, "HL" if k % 2 else "HM", 0, lo, lo + 512)
+            send("c%d" % t, "CP", 1024 * t, "CU", 1024 * t, 1024 * t + 1024)
+            due(when(t, 0, 1) + PIN["c"])
         if t == 1:
-            at(n + 10.3)
-            gx("s", xa, 6144, xo, 5120, 6144, "HL", 0, 0, 128)
-            first_preds()
+            gx(xa, 6144, xo, 5120, 6144, "HM", 0, 0, 128)
+            for lo in (0, 512):
+                gx("YPC", 0, "CURW", 0, 1024, "OL", 0, lo, lo + 512)
+            dma("y", "o_yp0", T.yp[:, 0:1024], T.YPC[0:128:16, :], ["YPC"], [])
         if t == 2:
             for j in range(2):
-                at(n + TN["p1"] + j)
-                wrap("pM", "VW", xa, 64, range(8 * j, 8 * j + 8), j == 0, j == 1, True)
-            at(n + TN["p1"] + 2.14)
+                wrap("pM", "VW", 0, lambda k: S("CU", 2048 + 64 * k, 2112 + 64 * k), range(8 * j, 8 * j + 8), j == 0, j == 1)
             preds_out(1, "pM")
         for h in range(2):
-            for k in range(6):
+            for k in range(1, 6):
                 step(t, h, k)
         for h in range(2):
             outcome(t, h)
         splits(t)
 
-    n = 2 * ROUND
-    at(n + 12.91)
-    dma("y", "o_yk0", T.yk0[:, :], T.KW[2:128:16, 0:1792], [("KW", 0, 1792)], [])
-    dma("s", "o_yk1", T.yk1[:, :], T.KW[3:128:16, 0:1792], [("KW", 0, 1792)], [])
-    for h in range(2):
-        arrive(2, h)
-        ks = range(8 * h, 8 * h + 8)
-        at(n + 12.8 + 0.25 * h)
-        wrap("pA", "VW", "SP", 64, ks, h == 0, False, True)
-        at(n + 12.88 + 0.25 * h)
-        wrap("pA", "VW", "TT", 64, ks, False, h == 1, True)
-    at(n + 14)
-    preds_out(2, "pA")
+    dma("y", "o_yk0", T.yk0[:, :], T.KO[0:128:16, 0:1792], [("KO", 0, 1792)], [])
+    dma("s", "o_yk1", T.yk1[:, :], T.KO[1:128:16, 0:1792], [("KO", 0, 1792)], [])
+    for a, b in ((0, 8), (8, P["last"]), (P["last"], 16)):
+        arrive(2, 64 * a, 64 * b)
+        wrap("pD0", "VW", 0, lambda k: S("SP", 64 * k, 64 * k + 64), range(a, b), a == 0, False)
+        wrap("pD0", "VW", 144, lambda k: S("TT", 64 * k, 64 * k + 64), range(a, b), False, b == 16)
+    preds_out(2, "pD0")
     issue()

from concourse.mybir import AluOpType, AxisListType, ActivationFunctionType

A = AluOpType
F = ActivationFunctionType
DUP = 2048
TB = 1920
XAW = 6272
EW = 2592
UNIT = 1.0 / 512
HALF = 0.5 - UNIT / 2
LEVELS = (320, 704, 1088, 1472)
CYCLE, GATHER, GATHER2, SCATTER, WAKE = 0.87e-3, 1.4, 2.0, 3.8, 0.08
LOCAL, REMOTE = (1.7, 220e3, 0.15), (2.0, 35e3, 0.3)
CASES = ((1.1, 0.09, 1.0), (1.6, 0.065, 1.3))
TRIES, MEAN, SEED, AIM, HEAT = 35000, 1.0, 11, 0.5, 0.25
KIB = dict(l_prev=64, l_x=256, l_z=256, l_env=256, l_rs=256, d_ct=448, d_m1=256, d_e1=256, d_m2=136, d_e2=136, l_w=1, l_th=1)
P = dict(cut=256, c1=192, zs0=0, zs1=160, last=13)
PIN = dict(t0=7.37, p0=1.28, p=1.1, gap=6.99, lag0=1.61, lag=3.27, end=84.1, setup=35.73, leaves=2.13, codes=19.16, e=9, c=3.0,
           lead=2.84, two0=0.76, two=1.15, sh=0.85, ra0=0, ra1=0.21, rb0=-0.11, rb1=1.07, senda=1.56, sendb=1.74, s1=1.98,
           scl=6.02, sc1=5.24, sc2=9.51, pz=4.96, env=5.67, tt=5.97, hl=7.95, cu=8.64)

BUFS = {
    "bfloat16": dict(XW=2048, PW=2048, ZL=1024, RW=DUP + 1792, CT=DUP + 1792, EM=EW, EP=EW, CP=3072, CU=3072, XA0=XAW, XA1=XAW,
                     BT=1024, PG=1024, SP=1024, TT=1024, EE=1024, PB=256, PL=256, BE=128, BO=128, RN=128, DA=128,
                     S1=128, T1=128, T5=256, SA=128, SM=128, GS=128, TW=256, NEG=16, ID=128, IDM=128, IDS=128, IDQ=128, M1=128,
                     NL=128, LM=128, R3=8, R3N=16, WA=40, WP=40, WW=112, VP=144, VW=288, ON=128, C8=32, C96=96, JN=256),
    "float16": dict(J=1024, J6=128, QA=256, QB=256, W3=106, WL=128, WQ=256, CL=128, IDN=128, R3H=8, T3=128, HQ=64, HS=800, HH=260,
                    M15=128, M12=128, M63=128),
    "int32": dict(CURI=64, STI=64, PC=256, KC=256, IP=1, IQ=7, WI=1, THP=1, THL=1, H2=128, YI=128),
    "uint16": dict(IXP=192, IX=192, SL=448, ST=64, FL=64, XL=8, HL=64, HM=64, OL=64, SCL=8),
    "float32": dict(ZK=DUP + TB, KO=DUP, PZ=1024, KF=256, OWN=256, KN=256, KM=384, XV6=128, D0=96, MD=256, MB=128, SJ=16, col=64,
                    I16=128, IG=128, IC=144, SG=3, SC=3, B1=3, B3=3, B4=3, PF=1, RB=1, CURF=64, CURW=1024, YPC=1024,
                    YF1=64, YF2=64),
}
PSUM = ("pA", "pB", "pL", "pM", "pD0", "pD1", "pD2", "pD3")
SCRATCH = {n: ("sbuf", [128, w], d) for d, b in BUFS.items() for n, w in b.items()}
SCRATCH["HX"] = ("sbuf", [128, 196, 4], "float16")
for _n in ("ZA", "ZC"):
    SCRATCH[_n] = ("sbuf", [128, 32, 16], "float16")
SCRATCH["CV"] = ("sbuf", [128, 16, 16], "bfloat16")
for _n in PSUM:
    SCRATCH[_n] = ("psum", [128, 512], "float32")
LOADS = ["l_cur", "l_start", "l_prev", "l_kid", "l_x", "l_z", "l_env", "l_w", "l_th", "l_rs"]
TAGS = ("e", "c0", "c1", "c2", "i0a", "i0b", "i1a", "i1b", "i2a", "i2b")
SEMAPHORES = ["c_v", "c_s", "c_t", "c_g", "d_p", "d_k", "d_cw", "d_ct", "d_m1", "d_m2", "d_e1", "d_e2", "o_yp0", "o_yp1",
              "o_yp2", "o_yr0", "o_yr1", "o_yk0", "o_yk1"] + LOADS + [a + b for a in ("r_", "q_") for b in TAGS]
ORDER = []
EST = []


def rank_program(g, core, T, topo):
    rank = T.rank_of(core)
    if rank is None:
        return
    nxt = T.cores[(rank + 1) % len(T.cores)]
    prv = T.cores[(rank - 1) % len(T.cores)]
    queues = {"v": g.vector, "s": g.scalar, "t": g.tensor, "y": g.sync, "g": g}

    calls = []
    seen = {}

    def when(t, k, h):
        if t == 0:
            return PIN["t0"] + 2 * PIN["p0"] * k + PIN["lag0"] * h
        return PIN["t0"] + 12 * PIN["p0"] + PIN["gap"] * t + PIN["p"] * (12 * t - 12 + 2 * k) + PIN["lag"] * h

    def due(time):
        calls[-1]["pin"] = time

    def follow(*ids):
        calls[-1]["deps"] |= set(ids)
        calls[-1]["soft"] |= set(ids)
        return len(calls) - 1

    def meets(r, s):
        if r[1] >= s[2] or s[1] >= r[2]:
            return False
        return r[3] is None or s[3] is None or r[3] == s[3]

    def spec(r):
        if not isinstance(r, tuple):
            r = (r,)
        return tuple(r) + (0, 1 << 20, None)[len(r) - 1:]

    def op(q, fn, reads, writes, cost, sem=None, group=None, move=None, picks=0):
        reads, writes = [spec(r) for r in reads], [spec(r) for r in writes]
        me, deps = len(calls), set()
        for wr, regs in ((False, reads), (True, writes)):
            for r in regs:
                for s, w, i in seen.get(r[0], ()):
                    if (meets(r, s) and (wr or w)) or (r[0] in PSUM and q == "t" and calls[i]["q"] == "t"):
                        deps.add(i)
        for wr, regs in ((False, reads), (True, writes)):
            for r in regs:
                h = seen.setdefault(r[0], [])
                if wr:
                    h[:] = [x for x in h if not (r[3] is None and r[1] <= x[0][1] and x[0][2] <= r[2])]
                h.append((r, wr, me))
        calls.append(dict(q=q, fn=fn, reads=reads, writes=writes, sem=sem, group=group, deps=deps, soft=set(), cost=cost,
                          picks=picks, pin=PIN["end"], move=move, banks={r[0] for r in reads + writes if r[0] in PSUM}))

    def dma(q, sem, out, in_, reads, writes, n=1, **kw):
        op(q, lambda: queues[q].dma_start(out, in_, **kw), reads, writes, 3.0 if q == "g" else 0.05, sem, 16 * n,
           (LOCAL, KIB.get(sem, 32) << 10))

    def send(tag, dst, dlo, src, lo, hi):
        def fn():
            rid, pid = topo.addr(nxt, core)
            g.remote_dma(T[dst][:, dlo:dlo + hi - lo], T[src][:, lo:hi], T.sem["r_" + tag], T.sem["q_" + tag], pid, rid,
                         topo.mask(core, nxt))
        op("g", fn, [(src, lo, hi)], [(dst, dlo, dlo + hi - lo)], 4.0 if tag == "e" else 0.3, tag, None, (REMOTE, 256 * (hi - lo)))

    def ordered():
        n = len(calls)
        for c in calls:
            for d in list(c["deps"] - c["soft"]):
                if calls[d]["group"] and calls[d]["sem"] != c["sem"]:
                    c["deps"] |= {i for i in range(n) if calls[i]["sem"] == calls[d]["sem"]}
        for c in calls:
            if c["q"] == "t":
                c["soft"] |= {d for d in c["deps"] if calls[d]["q"] == "t"}
        users = [[] for c in calls]
        for i, c in enumerate(calls):
            for d in c["deps"]:
                users[d].append(i)
        span = [c["cost"] + WAKE + (0.06 if c["q"] == "t" else 0) for c in calls]
        for i, c in enumerate(calls):
            if c["move"]:
                way, nbytes = c["move"]
                span[i] = way[0] + nbytes / way[1] + way[2] + WAKE
        key, todo = [None] * n, list(range(n))
        while todo:
            i = todo[-1]
            more = [u for u in users[i] if key[u] is None]
            if more:
                todo.extend(more)
                continue
            todo.pop()
            key[i] = min([key[u] - (0.05 if i in calls[u]["soft"] else span[i]) for u in users[i]] + [calls[i]["pin"]])
        deps = [[(b, b in c["soft"]) for b in sorted(c["deps"])] for c in calls]
        holds = [[c["q"]] + sorted(c["banks"]) for c in calls]

        def seek(line, x):
            lo, hi = 0, len(line)
            while lo < hi:
                mid = (lo + hi) // 2
                lo, hi = (mid + 1, hi) if line[mid] < x else (lo, mid)
            return lo

        def place(key):
            left, start, end, busy = [len(d) for d in deps], [0.0] * n, [0.0] * n, {}
            ready = sorted((-key[i], -i) for i in range(n) if not left[i])
            while ready:
                i = -ready.pop()[1]
                c, q, moved = calls[i]["cost"], calls[i]["q"], True
                t = max([start[b] + 0.05 if soft else end[b] for b, soft in deps[i]] + [0.0])
                while moved:
                    moved = False
                    for r in holds[i]:
                        line = busy.setdefault(r, [])
                        for k in range(seek(line, (t - 4.5,)), len(line)):
                            s, e, other = line[k]
                            if s >= t + c + WAKE:
                                break
                            w = WAKE if other != q else 0.0
                            if s < t + c + w - 1e-9 and t < e + w - 1e-9:
                                t, moved = e + w, True
                for r in holds[i]:
                    busy[r].insert(seek(busy[r], (t,)), (t, t + c, q))
                start[i], end[i] = t, t + span[i]
                if calls[i]["move"]:
                    way, nbytes = calls[i]["move"]
                    a, d = t + way[0] / 2, nbytes / way[1] + way[2]
                    for s, e in sorted(busy.get(way, ())):
                        if s < a + d and a < e:
                            a = e
                    busy.setdefault(way, []).append((a, a + d))
                    end[i] = a + d + way[0] / 2 + WAKE
                for u in users[i]:
                    left[u] -= 1
                    if not left[u]:
                        ready.insert(seek(ready, (-key[u], -u)), (-key[u], -u))
            return start, end

        start, end = place(key)
        EST.append(max(end))
        line = sorted(range(n), key=lambda i: (start[i], i))
        names = sorted({r for h in holds for r in h} | {LOCAL, REMOTE}, key=str)
        cases = []
        for rate, wake, slow in CASES:
            cases.append((wake, []))
            for i, c in enumerate(calls):
                mv, cost = c["move"], c["cost"] + c["picks"] * CYCLE * (rate - GATHER)
                if mv:
                    mv = (names.index(mv[0]), mv[0][0] / 2, mv[1] / mv[0][1] * (slow if mv[0] == REMOTE else 1) + mv[0][2])
                cases[-1][1].append(([b for b, soft in deps[i] if not soft], [b for b, soft in deps[i] if soft], names.index(c["q"]),
                                     [names.index(b) for b in holds[i][1:]], cost, cost + wake * (2 if c["q"] == "t" else 1), mv))

        def run(line, wake, facts):
            start, end, why = [0.0] * n, [0.0] * n, [-1] * n
            free, user, by = [0.0] * len(names), [-1] * len(names), [-1] * len(names)
            for i in line:
                dep, soft, q, banks, c, sp, mv = facts[i]
                t, w = free[q], user[q]
                for b in dep:
                    if end[b] > t:
                        t, w = end[b], b
                for b in banks:
                    e = free[b] + wake if by[b] != q else free[b]
                    if e > t:
                        t, w = e, user[b]
                for b in soft:
                    if start[b] > t:
                        t, w = start[b], b
                start[i], why[i] = t, w
                free[q], user[q] = t + c, i
                for b in banks:
                    free[b], user[b], by[b] = t + c, i, q
                if mv:
                    free[mv[0]] = max(free[mv[0]], t + mv[1]) + mv[2]
                    end[i] = free[mv[0]] + mv[1] + wake
                else:
                    end[i] = t + sp
            return max(end) + MEAN * sum(end) / n, end, why

        def replay(line):
            runs = [run(line, *case) for case in cases]
            return sum(r[0] for r in runs) / len(runs), runs

        now = replay(line)
        best, x = (now[0], line), SEED
        for k in range(TRIES):
            end, why = now[1][k % len(cases)][1:]
            x = (x * 1103515245 + 12345) % 2147483648
            i, waits = end.index(max(end)) if x % 1024 < 1024 * AIM else (x >> 10) % n, []
            while i >= 0:
                if why[i] >= 0 and why[i] not in calls[i]["deps"]:
                    waits.append(i)
                i = why[i]
            if not waits:
                continue
            x = (x * 1103515245 + 12345) % 2147483648
            a = waits[(x >> 8) % len(waits)]
            b = why[a]
            lo, hi = line.index(b), line.index(a)
            mid = line[lo:hi + 1]
            if x >> 30:
                group = {a}
                for i in reversed(mid):
                    if i in group:
                        group.update(calls[i]["deps"])
                if b in group:
                    continue
                mid = [i for i in mid if i in group] + [i for i in mid if i not in group]
            else:
                group = {b}
                for i in mid:
                    if i in group:
                        group.update(users[i])
                if a in group:
                    continue
                mid = [i for i in mid if i not in group] + [i for i in mid if i in group]
            tried = line[:lo] + mid + line[hi + 1:]
            new = replay(tried)
            x = (x * 1103515245 + 12345) % 2147483648
            if new[0] <= now[0] + HEAT * (1 - k / TRIES) * (x / 2147483648) ** 3:
                now, line = new, tried
                if new[0] < best[0]:
                    best = (new[0], tried)
        EST.extend(max(r[1]) for r in replay(best[1])[1])
        return best[1]

    def issue():
        clock = {q: {} for q in queues}
        total, hist = {}, {}

        def wait(q, ev):
            sem, val, snap = ev
            c = clock[q]
            if c.get(sem, 0) >= val:
                return
            queues[q].wait_ge(T.sem[sem], val)
            for k, v in snap.items():
                if c.get(k, 0) < v:
                    c[k] = v
            c[sem] = val

        def whole(regs):
            return [spec(r[0]) if r[0] in PSUM else r for r in regs]

        def note(ev, reads, writes):
            for wr, regs in ((False, reads), (True, writes)):
                for r in regs:
                    h = hist.setdefault(r[0], [])
                    p = r[0] in PSUM
                    if wr and not p:
                        h[:] = [x for x in h if not (r[3] is None and r[1] <= x[0][1] and x[0][2] <= r[2])]
                    else:
                        kd = "p" if p else "r"
                        h[:] = [x for x in h if not (x[1] == kd and x[0] == r and x[2][0] == ev[0] and x[2][1] <= ev[1])]
                    h.append((r, "p" if p else ("w" if wr else "r"), ev))

        if not ORDER:
            ORDER.extend(ordered())
        for i in ORDER:
            c = calls[i]
            q, reads, writes, evs = c["q"], whole(c["reads"]), whole(c["writes"]), []
            for wr, regs in ((False, reads), (True, writes)):
                for r in regs:
                    for s, kind, ev in hist.get(r[0], ()):
                        if meets(r, s) and (ev[0] != "c_" + q if kind == "p" else (wr or kind == "w")) and ev[0] != c["sem"]:
                            evs.append(ev)
            evs.sort(key=lambda x: -sum(x[2].values()))
            for ev in evs:
                wait(q, ev)
            ins = c["fn"]()
            if c["sem"] in TAGS:
                a, b = "q_" + c["sem"], "r_" + c["sem"]
                total[a], total[b] = len(topo.engines(core, nxt)), len(topo.engines(prv, core))
                note((a, total[a], dict(clock[q])), reads, [])
                note((b, total[b], {}), [], writes)
                continue
            sem, inc = c["sem"] or "c_" + q, 16 if c["sem"] else 1
            ins.then_inc(T.sem[sem], inc)
            total[sem] = total.get(sem, 0) + inc
            note((sem, c["group"] or total[sem], dict(clock[q])), reads, writes)
        for sem in sorted(total):
            wait("g", (sem, total[sem], {}))

    def S(name, lo=0, hi=None, step=1):
        hi = T[name].shape[1] if hi is None else hi
        kind = "p" if name in PSUM else 4 if SCRATCH[name][2].endswith("32") else 2
        return (T[name][:, lo:hi:step] if step > 1 else T[name][:, lo:hi]), [(name, lo, hi)], (hi - lo + step - 1) // step, kind

    def G(name, lo, hi, lst, l0, l1):
        return T[name][:, lo:hi].indirect(T[lst][:, l0 // 16:l1 // 16]), [(name, lo, hi), (lst, l0 // 16, l1 // 16)], l1 - l0, "g"

    def cycles(n, more=0.03):
        return more + max(64, n) * CYCLE

    def plain(out, in_):
        return cycles(in_[2] * GATHER, 0.05) if in_[3] == "g" else cycles(out[2] * (0.5 if out[3] == in_[3] == 2 else 1))

    def num(a):
        return a if isinstance(a, tuple) else (a, [])

    def ts(out, in0, s1, op0, s2=None, op1=None):
        s1, s2 = num(s1), num(s2)

        def fn():
            if op1 is None:
                return g.vector.tensor_scalar(out[0], in0[0], s1[0], None, op0)
            return g.vector.tensor_scalar(out[0], in0[0], s1[0], s2[0], op0, op1)
        op("v", fn, in0[1] + s1[1] + s2[1], out[1], plain(out, in0), picks=in0[2] * (in0[3] == "g"))

    def tt(out, in0, in1, o):
        c = cycles(out[2] * GATHER2, 0.05) if in0[3] == "g" else cycles(out[2] * (1 if "p" in (in0[3], in1[3]) else 2))
        op("v", lambda: g.vector.tensor_tensor(out[0], in0[0], in1[0], o), in0[1] + in1[1], out[1], c)

    def cp(out, in_):
        op("v", lambda: g.vector.tensor_copy(out[0], in_[0]), in_[1], out[1], plain(out, in_))

    def scatter(name, lo, src, more=None):
        def fn():
            out = T[name][:, lo:lo + TB].indirect(T.SCL[:])
            return g.vector.tensor_tensor(out, src[0], more[0], A.add) if more else g.vector.tensor_copy(out, src[0])
        op("v", fn, src[1] + (more[1] if more else []) + ["SCL"], [(name, lo, lo + TB)], cycles(128 * SCATTER, 0.05))

    def fill(out, c):
        op("v", lambda: g.vector.memset(out[0], c), [], out[1], plain(out, out))

    def act(out, in_, func=F.Copy, scale=None, bias=None):
        kw = {k: num(v)[0] for k, v in (("scale", scale), ("bias", bias)) if v}
        op("s", lambda: g.scalar.activation(out[0], in_[0], func, **kw), in_[1] + num(scale)[1] + num(bias)[1], out[1],
           cycles(out[2] * (GATHER if in_[3] == "g" else 1), 0.08), picks=in_[2] * (in_[3] == "g"))

    def iota(out, pattern, base=0, cm=0):
        kw = {} if out[1][0][0] in BUFS["int32"] else dict(allow_small_or_imprecise_dtypes=True)
        op("g", lambda: g.iota(out[0], pattern, base, cm, **kw), [], out[1], 0.13 + 2 * out[2] * CYCLE)

    def diagonal(out, c):
        op("g", lambda: g.affine_select(T[out][:], T.M1[:], [[-1, 128]], A.not_equal, c, 0, 1), ["M1"], [out], 0.4)

    def mms(parts, start=True, stop=True):
        def fn():
            r = None
            for i, (o, l, m) in enumerate(parts):
                r = g.tensor.matmul(o[0], l[0], m[0], start and i == 0, stop and i == len(parts) - 1)
            return r
        op("t", fn, [r for o, l, m in parts for r in l[1] + m[1]], [r for o, l, m in parts for r in o[1]],
           sum(cycles(o[2], 0) for o, l, m in parts))

    def gx(dst, d0, src, s0, s1, lst, l0, lo, hi, scale=None):
        act(S(dst, d0 + lo, d0 + hi), G(src, s0, s1, lst, l0 + lo, l0 + hi), scale=scale)

    ncol = [0]

    def col(n=1):
        ncol[0] += n
        return S("col", ncol[0] - n, ncol[0])

    def colop(a, s1, op0, s2=None, op1=None):
        c = col()
        ts(c, a, s1, op0, s2, op1)
        return c

    def colact(a, scale, bias=None):
        c = col()
        act(c, a, F.Identity, scale, bias)
        return c

    def rows(name, r, lo, hi):
        return T[name][r:128:16, lo:hi], [(name, lo, hi, r)]

    def part(name, lo, hi, own=True):
        return T[name][lo:hi, :], [(name, 0, 256, lo if own else None)], 256, 4

    dma("y", "l_prev", T.PC[0:64, :], T.prev[:, :], [], ["PC"])
    last = follow()
    for i in range(4):
        dma("ys"[i % 2], "l_kid", T.KC[32 * i:32 * i + 32, :], (T.kid0, T.kid1)[i % 2][:, :], [], part("KC", 32 * i, 0)[1], 4)
        last = follow(last)
    for sem, dst, src in (("l_cur", "CURI", T.cur), ("l_start", "STI", T.start), ("l_z", "ZL", T.z)):
        dma("y", sem, T[dst][:], src[:, :], [], [dst])
        last = follow(last)
    dma("y", "l_x", T.XW[:, 0:1024], T.x[:, 0:1024], [], [("XW", 0, 1024)], 2)
    last = follow(last)
    cp(part("PB", 0, 64), part("PC", 0, 64, False))
    tt(part("PL", 0, 64), part("PC", 0, 64, False), part("PB", 0, 64, False), A.subtract)
    fill(S("EM", 0, 1024), -256.0)
    for lo in (0, 1024):
        act(S("PW", lo, lo + 1024), S("EM", 0, 1024), F.Identity, None, 256.0)
    for r, b in enumerate(("PB", "PL")):
        dma("y", "d_p", rows("PW", r, 0, 2048)[0], T[b][0:64, :], [b], rows("PW", r, 0, 2048)[1], 2)
        last = follow(last)
    dma("y", "l_x", T.XW[:, 1024:2048], T.x[:, 1024:2048], [], [("XW", 1024, 2048)], 2)
    last = follow(last)
    dma("y", "l_w", T.WI[:], T.w[:, :], [], ["WI"])
    last = follow(last)
    iota(S("THP"), [[0, 1]])
    for r in (7, 8):
        dma("y", "l_th", rows("THP", r, 0, 1)[0], T.th[:, :], [], rows("THP", r, 0, 1)[1], 2)
        last = follow(last)
    for lo in (0, DUP):
        dma("y", "l_rs", T.RW[:, lo:lo + 1024], T.rs[:, :], [], [("RW", lo, lo + 1024)], 2)
        last = follow(last)

    iota(S("IP"), [[0, 1]], 0, 1)
    iota(S("PF"), [[0, 1]], 0, 1)
    for a in range(2):
        iota((T.CV[:, a:16:2, :], [("CV", a, a + 1)], 128), [[4, 8], [0, 4], [1, 4]], 32 * a)
    iota(S("I16"), [[0, 8], [1, 16]])
    iota(S("OWN"), [[1, 256]])
    iota(S("KO", 1024, DUP), [[1, 1024]], 1024)
    for w, d in enumerate((-40000, -7 * 4096 - 1536, 512)):
        iota(S("D0", w, 96, 3), [[0, 32]], d)
    iota(S("M1"), [[0, 128]])
    diagonal("IDS", UNIT)
    diagonal("ID", 1.0)
    iota(S("IG"), [[1, 8], [0, 16]])
    iota(S("SG"), [[1, 3]], 2)
    iota(S("SC"), [[-768, 3]], -1792 - 1536)
    iota(S("WP"), [[0, 40]])
    iota(S("ON"), [[0, 128]], 1)
    iota(S("C96"), [[0, 32], [-4, 3]])
    early = [i for i, c in enumerate(calls) if c["q"] == "g"]
    for b in ("WW", "WA"):
        iota(S(b, 0, 40), [[0, 40]])
    iota(S("C8"), [[0, 32]], 8)
    iota(S("IC"), [[1, 144]], -15)
    iota(S("CURW"), [[0, 1024]])

    cuts = ((15, A.bitwise_and), (4, A.arith_shift_right), (31, A.bitwise_and), (3, A.bitwise_and), (4, A.bitwise_and),
            (1, A.bitwise_and), (8, A.bitwise_and))
    for i, (n, o) in enumerate(cuts):
        ts(S("IQ", i, i + 1), S("IP"), n, o)
    cp(col(7), S("IQ"))
    p15, p4, p31, p3, pb, p1, p8 = [S("col", i, i + 1) for i in range(7)]
    ts(S("MD", 0, 128), S("I16"), p15, A.is_equal)
    e = [S("MD", r, r + 1) for r in range(16)]

    hi64 = colop(S("PF"), 64.0, A.is_ge)
    p63 = colact(hi64, -64.0, S("PF"))
    level = colact(hi64, float(LEVELS[1] - LEVELS[0]), float(LEVELS[0]))

    def places(buf, b, lo=0, hi=16):
        return T[buf][:, b:32:2, lo:hi], [(buf, b, b + 1)], 16 * (hi - lo), 2

    def match(lo=0, hi=16):
        return T.CV[:, :, lo:hi], ["CV"], 16 * (hi - lo), 2

    ts(places("ZA", 0), match(), p63, A.is_equal, colact(hi64, 6.0, 2.0), A.mult)
    ts(places("ZA", 1), places("ZA", 0), colact(hi64, 2.0, -1.0), A.mult)
    ts(places("ZC", 0), match(), p63, A.is_equal, -768.0, A.mult)
    for m, c in enumerate((colact(hi64, -3072.0, 2304.0), colact(hi64, 3072.0, -768.0))):
        ts(places("ZC", 0, 4 * m, 4 * m + 4), match(0, 4), p63, A.is_equal, c, A.mult)
    ts(places("ZC", 1), places("ZC", 0), -1.0, A.mult)
    sign = colact(pb, -0.5, 1.0)
    zb, two = colact(sign, -1792.0, HALF), colact(sign, 2.0)
    act(S("OWN"), S("OWN"), F.Identity, None, colact(p3, 256.0))
    ts(S("QB"), S("KC"), level, A.is_ge)
    cp(part("QA", 0, 64), part("KC", 0, 64, False))
    tt(part("QA", 64, 128), part("KC", 64, 128, False), part("OWN", 64, 128), A.is_equal)
    for c in range(2):
        bank = "pD%d" % (2 + c)
        for i, (w, q) in enumerate((("ZC", "QB"), ("ZA", "QA"))):
            mms([(S(bank, 256 * j, 256 * j + 256), (T[w][:, :, 2 * c + j:16:4], [w]), S(q)) for j in range(2)], i == 0, False)
        mms([(S(bank), S("IDS"), S("ZL", 512 * c, 512 * c + 512))], False, True)
        for lo in (0, DUP):
            out = S("ZK", lo + 512 * c, lo + 512 * c + 512)
            if lo == c == 0:
                ts(out, S(bank), zb, A.add)
            else:
                act(out, S(bank), F.Identity, bias=zb)
    ts(S("B1"), S("SG"), p3, A.is_gt, 3072.0, A.mult)
    tt(S("B1"), S("B1"), S("SC"), A.add)
    act(S("B3"), S("B1"), F.Identity, sign, 8.0 + HALF)
    ends, leaves = (1024, LEVELS[2], LEVELS[3]), []
    for lo, top in ((0, DUP), (DUP, TB)):
        for i, (a, b) in enumerate(zip(ends, ends[1:] + (top,))):
            act(S("ZK", lo + a, lo + b), S("KO", a, b), F.Identity, two, S("B3", i, i + 1))
            leaves.append(len(calls) - 1)
    up = colact(p8, colact(sign, 0.25))
    act(S("B4"), S("B3"), F.Identity, None, colact(up, 1.0, -8.0))
    for i, (a, b) in enumerate(zip(ends, ends[1:] + (1536,))):
        act(S("KN", a // 2 - 512, b // 2 - 512), S("KO", a, b, 2), F.Identity, two, S("B4", i, i + 1))
    act(S("KM"), S("KO", 1024, 1792, 2), F.Identity, bias=p1)

    cp(S("SL", 0, 64), S("CURI"))
    cp(S("ST"), S("STI"))
    cp(part("KF", 0, 64), part("KC", 0, 64, False))
    for r in range(2):
        dma("y", "d_k", rows("KO", r, 0, 1024)[0], T.KF[32 * r:32 * r + 32, :], ["KF"], rows("KO", r, 0, 1024)[1], 2)

    wp = colop(p15, 2.0, A.is_lt)
    ts(S("R3"), S("I16", 0, 8), p4, A.is_equal)
    act(S("WP", 3, 35, 4), S("R3"), F.Identity, wp)
    ts(S("IDN"), S("IDS"), -512.0, A.mult)
    for out in (S("HH"), S("HS"), S("W3"), (T.HX[:], ["HX"], 784, 2)):
        ts(out, S("EM", 0, out[2]), 0.0, A.mult)
    ck1 = colact(up, 1.0 / 32)
    ck0 = colact(ck1, -1.0, colact(sign, 1.0 / 16))
    ts(S("W3", 9, 105, 12), S("R3"), -4096.0, A.mult)
    ts(S("W3", 10, 105, 12), S("R3"), ck1, A.mult)
    ts(S("W3", 11, 105, 12), S("R3"), ck0, A.mult, -1.0, A.mult)
    ts(S("GS"), S("IG"), p4, A.is_equal)
    act(S("SJ"), S("MD", 0, 16), F.Identity, -2.0, 1.0)
    fill(S("CT", 0, 1), -1.0)
    ts(S("WL"), S("GS"), 1.0 / 128, A.mult)
    ts(S("CL"), S("EM", 0, 128), 256 - 159.625, A.add)

    for b in range(11):
        ts(S("CT", 1 << b, 2 << b), S("CT", 0, 1 << b), S("SJ", b, b + 1), A.mult)
    cp(S("CURF"), S("CURI"))
    dma("y", "d_cw", T.CURW[0:128:16, :], T.CURF[:], ["CURF"], ["CURW"])
    p16 = colact(p4, 16.0)
    wf = colop(S("WI"), 1.0, A.mult)
    act(S("WA", 3, 35, 4), S("R3"), F.Identity, 97.0 / 1024)
    ts(S("WW", 3, 35, 4), S("R3"), wf, A.mult, 1.0 / 1024, A.mult)
    dma("y", "d_ct", T.CT[:, DUP:DUP + 1792], T.CT[:, 0:1792], [("CT", 0, 1792)], [("CT", DUP, DUP + 1792)])
    codes = len(calls) - 1
    dma("g", "l_env", T.EM[:, 0:1024], T.env[:, :], [("EM", 0, 1024)], [("EM", 0, 1024)], accum_op=A.add)
    follow(last, *early)
    send("e", "EP", 0, "EM", 0, 1024)
    sent = len(calls) - 1
    for b in ("EM", "EP"):
        for i, n in ((1, 1024), (2, EW - 2048)):
            dma("y", "d_%s%d" % ("m" if b == "EM" else "e", i), T[b][:, 1024 * i:1024 * i + n], T[b][:, 0:n], [(b, 0, n)],
                [(b, 1024 * i, 1024 * i + n)])
    for lo, hi in ((1024, DUP), (DUP + 1024, DUP + 1792)):
        iota(S("RW", lo, hi), [[0, hi - lo]])
    iota(S("JN"), [[0, 2], [1, 128]])
    diagonal("IDM", -1.0)
    diagonal("IDQ", 128 * UNIT)
    iota(S("NEG"), [[0, 16]], -8192)
    iota(S("NL"), [[0, 128]], 0, -1)
    iota(S("RB"), [[0, 1]], -11 * 4096, -32)
    ts(S("VP"), S("IC"), p16, A.is_equal, wp, A.mult)
    ts(S("VW", 0, 144), S("IC"), p16, A.is_equal, wf, A.mult)
    ts(S("THL"), S("THP"), 255, A.bitwise_and)
    ce = colop(p31, 11.0, A.is_lt, 64.0, A.mult)
    c27, c16 = colop(p31, 27.0, A.is_lt, 64.0, A.mult), colop(p31, 16.0, A.is_lt, 64.0, A.mult)
    thh = col()
    tt(thh, S("THP"), S("THL"), A.subtract)
    wa = colop(S("THL"), e[8], A.mult)
    co, wb = colact(c16, -1.0, c27), colop(thh, 8192.0, A.add, e[7], A.mult)
    wq = colop(wa, wb, A.add, -1.0, A.mult)
    act(S("TW", 0, 128), S("GS"), F.Identity, wq)
    act(S("TW", 128, 256), S("GS"), F.Identity, colact(e[7], -896.0))
    ts(S("WQ", 0, 128), S("GS"), 64.0, A.mult)
    ts(S("WQ", 128, 256), S("GS"), ck0, A.mult)
    act(S("WW", 40, 80), S("WW", 0, 40), scale=128.0)
    act(S("VW", 144, 288), S("VW", 0, 144), scale=128.0)
    for i in range(4):
        act(S("WW", 80 + i, 112, 4), S("WW", 43, 75, 4))
    act(S("LM"), S("MD", 0, 128), F.Identity, S("PF"))
    act(S("MB"), S("MD", 0, 128), F.Identity, -1e9, 1e9)
    turned = colact(p3, 4.0, colop(pb, p8, A.add, 0.25, A.mult))
    ts(S("MD", 128, 256), S("I16"), turned, A.is_equal)
    act(S("R3N", 8, 16), S("R3"), F.Identity, colact(turned, -1.0, p15))
    for b, c in (("M15", -15.0), ("M12", 12.0), ("M63", -63.9375)):
        ts(S(b), S("IDN"), c, A.mult)
    cp(S("R3H"), S("R3"))
    act(S("R3N", 0, 8), S("R3"), scale=-1024.0)
    for i, c in enumerate(calls):
        c["pin"] = PIN["t0"] + PIN["setup"] * i / len(calls)
    calls[sent]["pin"] = PIN["e"]
    for i in leaves:
        calls[i]["pin"] = PIN["leaves"]
    calls[codes]["pin"] = PIN["codes"]

    W = ("pA", "pB")

    def blocks(src, lo):
        return [S(src, lo + i, lo + 512, 4) for i in range(4)]

    def words(bank, c0, src, lo, wt, start=True, stop=True, w0=0):
        mms([(S(bank, c0, c0 + 32), b, S(wt, w0 + 3 - i, w0 + 35 - i)) for i, b in enumerate(blocks(src, lo))], start, stop)

    def slots(h):
        return T.HX[:, 32 * h + 3:32 * h + 35:4, :], [("HX", 32 * h + 3, 32 * h + 32)], 32, 2

    def back(bank, c0, parts):
        mms([(S(bank, c0, c0 + 32), (T.HX[:, 32 * h + 3 - j:32 * h + 35 - j, :], slots(h)[1]), S(m, j, 128, 4))
             for h, m in parts for j in range(4)])

    def spaced(h):
        return S("HH", 128 * h + 3, 128 * h + 128, 4)

    def turn(bank, c0, buf, first, step, reg):
        mms([(S(bank, c0, c0 + 32), (T[buf][:, first - step * j:first + step * (127 - j) + 1:step], reg), S("IDN", j, 128, 4))
             for j in range(4)])

    def wrap(bank, lt, w0, src, ks, start, stop):
        mms([(S(bank, 0, src(k)[2]), S(lt, w0 + 15 - k, w0 + 143 - k), src(k)) for k in ks], start, stop)

    def step(t, h, k):
        lo, hi = 512 * h, 512 * h + 512
        top, lst = (DUP + TB, "FL") if k else (1024, "ST")
        mms([(S(W[h], 0, 96), S("ON"), S("C96"))], True, False)
        if t and not k:
            tt(S("J", lo, hi), S("PZ", lo, hi), S("pD%d" % h), A.subtract)
            due(when(t, k, h))
        else:
            n, xa = P["zs1" if t else "zs0"], "XA%d" % (t % 2)
            cut = lo + P["c1" if t else "cut"]
            for a, b, later in ((lo, cut, 0.0), (cut, hi - n, PIN["two" if t else "two0"])):
                tt(S("J", a, b), G("ZK", 0, top, lst, a, b), S(xa, 1024 * k + a, 1024 * k + b), A.subtract)
                due(when(t, k, h) + later)
            if n:
                bank = "pD%d" % (2 + h)
                gx("PZ", 0, "ZK", 0, top, lst, 0, hi - n, hi)
                mms([(S(bank, 256, 256 + n), S("ID"), S(xa, 1024 * k + hi - n, 1024 * k + hi))])
                tt(S("J", hi - n, hi), S("PZ", hi - n, hi), S(bank, 256, 256 + n), A.subtract)
                due(when(t, k, h) + PIN["sh"])
        mms([(S(W[h], 0, 96), b, S("W3", 9 - 3 * i, 105 - 3 * i)) for i, b in enumerate(blocks("J", lo))], False, True)
        if t < 2 and h == 0:
            if k == 0:
                mms([(S("pL", i, i + 128), S("IDN"), S("CL")) for i in (0, 128)], True, False)
            mms([(S("pL", 128 * (k % 2), 128 * (k % 2) + 128), S("J", 0, 128), S("WL"))], False, k == 5)
        o = S("HS", 400 * h + 4, 400 * h + 388, 4)
        op("v", lambda: g.vector.tensor_tensor_scan(o[0], T.D0[:], T[W[h]][:, 0:96], 0.0, A.subtract, A.max),
           ["D0", (W[h], 0, 96)], o[1], cycles(96))
        turn(W[h], 128, "HS", 400 * h + 12, 3, o[1])
        ts(S("FL", 32 * h, 32 * h + 32), S(W[h], 128, 160), 1920.0, A.add)

    def hsum(t, h):
        lo, hi, bank = 32 * h, 32 * h + 32, "pD%d" % (2 + h)
        mms([(S(bank, 0, 32), S("ON"), S("C8"))] + [(S(bank, 0, 32), S("ON"), S("WW", 80, 112))] * (t > 0), True, False)
        for src in ("SP", "TT") if t else ("CU",):
            words(bank, 0, src, 512 * h, "WW", False, src != "SP", 40 * (src == "TT"))
        ts(S("HQ", lo, hi), S(bank, 0, 32), 0.5005, A.add)
        tt(spaced(h), S(bank, 0, 32), S("HQ", lo, hi), A.subtract)
        if t:
            turn(bank, 32, "HH", 128 * h + 3, 1, spaced(h)[1])
            ts(S("HL", lo, hi), S(bank, 32, 64), -1024.0, A.mult, 1024.0, A.add)
            due(when(t - 1, 6, h) + PIN["hl"])

    def even_lists(t, h):
        ts(slots(h), spaced(h), 4096.0, A.mult)
        ts(slots(2 + h), spaced(h), 256.0, A.mult, 1281 - 0.375, A.add)
        ts(slots(4 + h), spaced(h), 64.0, A.mult, 1089 - 0.46875, A.add)
        bank, lo = "pD%d" % h, 32 * h
        back(bank, 64 + lo, [(h, "IDN"), (2 + h, "M15"), (4 + h, "M12")])
        ts(S("HM", lo, lo + 32), S(bank, 64 + lo, 96 + lo), -1.0, A.mult, 7171.0, A.add)
        if t == 1:
            back(bank, 128 + lo, [(h, "IDN"), (4 + h, "M63")])
            ts(S("OL", lo, lo + 32), S(bank, 128 + lo, 160 + lo), -16.0, A.mult, 1114111.0, A.add)

    def outcome(t, h):
        lo, x0 = 512 * h, 64 * t + 32 * h
        for i, a in enumerate((lo, lo + 256)):
            tt(S("BT", a, a + 256), G("RW", 0, DUP + 1792, "FL", a, a + 256), S("CU", 1024 * t + a, 1024 * t + a + 256), A.is_gt)
            due(when(t, 6, h) + PIN["r" + "ab"[h] + "01"[i]])
        words(W[h], 160, "BT", lo, "WA")
        tt(slots(h), S(W[h], 160, 192), spaced(h), A.add)
        back(W[h], 192, [(h, "IDN")])
        ts(S("IX", x0, x0 + 32), S(W[h], 192, 224), -1024.0, A.mult, 1024.0, A.add)
        send("i%d" % t + "ab"[h], "IXP", x0, "IX", x0, x0 + 32)
        due(when(t, 6, h) + PIN["send" + "ab"[h]])

    def band(name, a):
        return T[name][32 * a:32 * a + 32, :], [name]

    def splits(t):
        xa, n0 = "XA%d" % (t % 2), 1024 + 256 * t
        act(S("BE"), G("CT", 0, DUP + 1792, "FL", 0, 128), F.Identity, ce)
        act(S("BO"), G("CT", 0, DUP + 1792, "FL", 0, 128), F.Identity, co)
        act(S("RN"), G("RW", 0, DUP + 1792, "FL", 0, 128))
        ts(S("J6"), G("ZK", 0, DUP + TB, "FL", 0, 128), -0.5, A.add)
        mms([(S("pM", 0, 256), S("ON"), S("TW")), (S("pM", 128, 256), S("ID"), S("NL"))], True, False)
        mms([(S("pM", 0, 256), S("J6"), S("WQ"))], False, False)
        for a in range(4):
            bank = "pD%d" % a
            mms([(S(bank, 0, 256), band("ON", a), band("JN", a))], True, False)
            mms([(S(bank, 128 * i, 128 * i + 128), band(b, a), band(b, a)) for i, b in enumerate(("BE", "BO"))], False, True)
            act(S("EE", 256 * a, 256 * a + 256), S(bank, 0, 256), F.Relu, bias=S("RB"))
            mms([(S("pM", 16 * q, 16 * q + 16), S("EE", 128 * q, 128 * q + 128), S("NEG")) for q in (2 * a, 2 * a + 1)], False, False)
        if t < 2:
            tt(S("T5"), S("pL", 0, 256), S("MD"), A.mult)
            mms([(S("pL", 384, 392), S("LM"), S("R3"))] +
                [(S("pL", 384, 392), S("T5", i, i + 128), S("R3N", b, b + 8)) for i in (0, 128) for b in (0, 8)])
            ts(S("XL"), S("pL", 384, 392), 6144.0 + 320 * 1024, A.add)
            gx("XV6", 0, xa, 0, XAW, "XL", 0, 0, 128)
        tt(S("S1"), G("EM", 0, EW, "IX", 1024 * t, 1024 * t + 128), S("CU", 1024 * t, 1024 * t + 128), A.add)
        due(when(t, 6, 0) + PIN["s1"])
        ts(S("T1"), S("S1"), 0.0, A.is_lt, 256.0, A.mult)
        mms([(S("pL", 256, 384), S("IDM"), S("RN"))], True, False)
        mms([(S("pL", 256, 384), S("ID"), S("S1"))], False, False)
        mms([(S("pL", 256, 384), S("ID"), S("T1"))], False, True)
        act(S("DA"), S("pL", 256, 384), F.Abs)
        mms([(S("pM", 0, 128), S("DA"), S("GS"))], False, True)
        mms([(S("pL", 384, 512), S("ID"), S(b)) for b in ("RN", "S1", "T1")])
        tt(S("SM"), S("pM", 0, 128), S("MB"), A.is_ge)
        tt(S("T3"), S("pM", 128, 256), S("SM"), A.mult)
        mms([(S("pM", 256, 264), S("LM"), S("R3")), (S("pM", 256, 264), S("T3"), S("R3H"))])
        ts(S("SCL"), S("pM", 256, 264), 1792.0, A.add)
        due(when(t, 6, 0) + PIN["scl"])
        for lo in (0, DUP) if t < 2 else ():
            scatter("ZK", lo, S("XV6"), S("KN", 128 * t, 128 * t + 128))
            due(when(t, 6, 0) + PIN["sc2" if lo else "sc1"])
        scatter("KO", 0, S("KM", 128 * t, 128 * t + 128))
        act(S("DA"), S("pM", 0, 128), F.Sign, bias=0.5)
        act(S("SA"), S("DA"), F.Relu)
        mms([(S("pM", 384, 512), S("SA"), S("ID"))])
        ts(S("H2"), S("pL", 384, 512), 0.5, A.mult, -0.25, A.add)
        tt(S("RW", n0, n0 + 256, 2), S("pM", 384, 512), S("RN"), A.mult)
        tt(S("RW", n0 + 1, n0 + 256, 2), S("pM", 384, 512), S("H2"), A.mult)
        if t < 2:
            act(S("RW", DUP + n0, DUP + n0 + 256), S("RW", n0, n0 + 256))
        if t:
            lo = 1024 if t == 1 else n0
            dma("y", "o_yr%d" % (t - 1), T.yr[:, lo - 1024:n0 - 768], T.RW[:, lo:n0 + 256], [("RW", lo, n0 + 256)], [])

    def arrive(t, lo, hi):
        h = lo // 512
        tt(S("SP", lo, hi), G("EP", 0, EW, "IXP", 1024 * t + lo, 1024 * t + hi), S("CP", 1024 * t + lo, 1024 * t + hi), A.add)
        due(when(t, 6, h) + PIN["env"])
        if t < 2:
            act(S("TT", lo, hi), S("SP", lo, hi), F.Sign, -1.0, -0.5)
            due(when(t, 6, h) + PIN["tt"])
            mms([(S("pD%d" % h), S("IDS"), S("SP", lo, hi))], True, False)
            mms([(S("pD%d" % h), S("IDQ"), S("TT", lo, hi))], False, True)
        else:
            ts(S("TT", lo, hi), S("SP", lo, hi), 0.0, A.is_lt, 2.0, A.mult)

    def preds_out(t, bank):
        yf = "YF%d" % t
        cp(S("YI", 0, 64), S(bank, 0, 64))
        ts(S("YI", 64, 128), S("YI", 0, 64), 1023, A.bitwise_and)
        ts(S(yf), S("YI", 64, 128), 1024.0 + 1024 * t, A.add)
        dma("y", "o_yp%d" % t, T.yp[:, 1024 * t:1024 * t + 1024], T[yf][:], [yf], [])

    for k in range(6):
        for h in range(2):
            lo, hi, bank = 512 * h, 512 * h + 512, "pD%d" % h
            gx("XA0", 1024 * k, "XW", 0, 2048, "SL", 1024 * k, lo, hi, UNIT)
            if k < 5:
                gx("PG", 0, "PW", 0, 2048, "SL", 1024 * k, lo, hi)
                due(when(0, k, h) - PIN["lead"])
                words(bank, 0, "PG", lo, "WP")
                cp(spaced(h), S(bank, 0, 32))
                turn(bank, 32, "HH", 128 * h + 3, 1, spaced(h)[1])
                ts(S("SL", 64 * k + 64 + 32 * h, 64 * k + 96 + 32 * h), S(bank, 32, 64), -1.0, A.mult)
    gx("PG", 0, "PW", 0, 2048, "SL", 5120, 0, 128)
    wrap("pM", "VP", 0, lambda k: S("PG", 4 * (k % 4) + k // 4, 128, 16), range(16), True, True)
    cp(S("SL", 384, 392), S("pM", 0, 8))
    gx("XA0", 6144, "XW", 0, 2048, "SL", 6144, 0, 128, UNIT)
    ts(S("CU", 0, 1024), S("XA0", 0, 1024), 512.0, A.mult)
    send("c0", "CP", 0, "CU", 0, 1024)
    due(when(0, 0, 1) + PIN["c"])

    for t in range(3):
        xo, xa = "XA%d" % ((t - 1) % 2), "XA%d" % (t % 2)
        for h in range(2):
            lo, hi = 512 * h, 512 * h + 512
            if t:
                act(S("PZ", lo, hi), G("ZK", 0, 1024, "ST", lo, hi), F.Identity, None, -128 * UNIT)
                due(when(t - 1, 6, 0) + 0.8 * h + PIN["pz"])
                arrive(t - 1, lo, hi)
                act(S("CU", 1024 * t + lo, 1024 * t + hi), S("pD%d" % h), F.Identity, 512.0, 128.0)
                due(when(t - 1, 6, h) + PIN["cu"])
                if t == 1 and h == 0:
                    act(S(xa, 0, 128), S("pD0", 0, 128), F.Identity, None, 128 * UNIT)
            hsum(t, h)
            if t:
                gx(xa, 1024, "CU", 1024 * t - 1024, 1024 * t, "HL", 0, lo, hi, UNIT)
        for h in range(2):
            step(t, h, 0)
        if t:
            for h in range(2):
                even_lists(t, h)
            for k in range(2, 6):
                for lo in (0, 512):
                    gx(xa, 1024 * k, xo, 1024 * k - 1024, 1024 * k, "HL" if k % 2 else "HM", 0, lo, lo + 512)
            send("c%d" % t, "CP", 1024 * t, "CU", 1024 * t, 1024 * t + 1024)
            due(when(t, 0, 1) + PIN["c"])
        if t == 1:
            gx(xa, 6144, xo, 5120, 6144, "HM", 0, 0, 128)
            for lo in (0, 512):
                gx("YPC", 0, "CURW", 0, 1024, "OL", 0, lo, lo + 512)
            dma("y", "o_yp0", T.yp[:, 0:1024], T.YPC[0:128:16, :], ["YPC"], [])
        if t == 2:
            for j in range(2):
                wrap("pM", "VW", 0, lambda k: S("CU", 2048 + 64 * k, 2112 + 64 * k), range(8 * j, 8 * j + 8), j == 0, j == 1)
            preds_out(1, "pM")
        for h in range(2):
            for k in range(1, 6):
                step(t, h, k)
        for h in range(2):
            outcome(t, h)
        splits(t)

    dma("y", "o_yk0", T.yk0[:, :], T.KO[0:128:16, 0:1792], [("KO", 0, 1792)], [])
    dma("s", "o_yk1", T.yk1[:, :], T.KO[1:128:16, 0:1792], [("KO", 0, 1792)], [])
    for a, b in ((0, 8), (8, P["last"]), (P["last"], 16)):
        arrive(2, 64 * a, 64 * b)
        wrap("pD0", "VW", 0, lambda k: S("SP", 64 * k, 64 * k + 64), range(a, b), a == 0, False)
        wrap("pD0", "VW", 144, lambda k: S("TT", 64 * k, 64 * k + 64), range(a, b), False, b == 16)
    preds_out(2, "pD0")
    issue()
